import numpy as np, ml_dtypes
CORES = [13,21,141,149]
N = 4
BF = ml_dtypes.bfloat16
def gentries(a):
    return np.ascontiguousarray(a.reshape(8, 16, -1).transpose(0, 2, 1)).reshape(8, -1)
def gtable(e):
    e = np.asarray(e); return np.ascontiguousarray(e.reshape(8, -1, 16).transpose(0, 2, 1)).reshape(128, -1).astype(np.int32)
V, G, SL, VI, RO, TH, A = 1792, 256, 640, 4, 2, 18, 176
W = V + (N - 1) * G
def corners(rng, share, wild=False):
    cen = rng.integers(30, 226, (8, 3, 16)); k = np.arange(8)[None, :, None]; u = rng.random((N, 8, V))
    cen[6, 0] = rng.integers(246, 256, 16); cen[7, 0] = rng.integers(0, 10, 16)
    cl = (u > 0.6).astype(np.int64) + (u > 0.85)
    amp = np.exp2(7 * rng.random((N, 8, 1, V))).astype(np.int64) - 1 if wild else rng.integers(0, 25, (N, 8, 1, V))
    x = cen[k, cl].transpose(0, 1, 3, 2) + np.floor((2 * amp + 1) * rng.random((N, 8, 16, V))).astype(np.int64) - amp
    odd = (rng.random((N, 8, 1, V)) < 0.08) & (rng.random((N, 8, 16, V)) < 0.3)
    x = np.clip(np.where(odd, rng.integers(0, 256, x.shape), x), 0, 255)
    flat = rng.random((N, 8, 1, V)); x = np.where(flat < 0.01, 0, np.where(flat > 0.99, 255, x))
    ql = np.where(rng.random(cl.shape) < 0.85, cl, rng.integers(0, 3, cl.shape))
    q = np.ascontiguousarray(np.clip(cen[k, ql].transpose(0, 1, 3, 2) + rng.integers(-6, 7, (N, 8, 16, V)), 0, 255))
    lost = rng.random((N, 8, V)) < share
    nb = rng.integers(0, W, (N, 8, 4, W))
    snd = rng.integers(0, 4, (N, 8, (N - 1) * G)) * W + rng.integers(0, V, (N, 8, (N - 1) * G))
    return cen, np.ascontiguousarray(x), q, lost, nb, snd
def pack(x, q, lost, nb, snd):
    x = np.where(lost[:, :, None, :], -64, x)
    return {"xv": x.reshape(N, 128, V).astype(np.float32).astype(BF), "cq": q.reshape(N, 128, V).astype(np.float32).astype(BF),
            "nb": nb.reshape(N, 8, 4 * W).astype(np.int32), "snd": np.stack([gtable(a) for a in snd])}
def setup_inputs(rng):
    cen, x, q, lost, nb, snd = corners(rng, rng.choice(np.array([0.2, 0.3, 0.4, 0.5]), (N, 8, 1)))
    return pack(x, q, lost, nb, snd)
def setup_inputs_room(rng):
    cen, x, q, lost, nb, snd = corners(rng, 0.3)
    sizes = np.array([SL, SL + 1, SL - 1, 0, 1, V, SL + 64, SL + 2]); n = rng.choice(sizes, (N, 8)); n[:, 0] = SL; n[0] = sizes
    lost = np.argsort(rng.random((N, 8, V)), axis=-1) < n[..., None]
    return pack(x, q, lost, nb, snd)
def setup_inputs_chain(rng):
    cen, x, q, lost, nb, snd = corners(rng, 0.15); H = 32
    nb[:, 5] = np.where(rng.random((N, 4, W)) < 0.25, np.arange(W), nb[:, 5])
    nb[:, 6] = np.where(rng.random((N, 4, W)) < 0.125, rng.choice(np.array([0, V - 1, V, W - 1]), (N, 4, W)), nb[:, 6])
    for a in range(N):
        for g in range(8):
            o = rng.permutation(V); se = o[:128]; ci = o[128:128 + H * VI]; ta = o[128 + H * VI:192 + H * VI]; c = cen[g, 0][:, None]
            lost[a, g, se] = True; lost[a, g, ci] = True; lost[a, g, ta] = False
            x[a, g][:, ta] = np.clip(c + rng.integers(-4, 5, (16, 64)), 0, 255); q[a, g][:, se] = np.clip(c + rng.integers(-6, 7, (16, 128)), 0, 255)
            for k in range(4):
                ck = rng.permutation(ci).reshape(H, VI)
                nb[a, g, k][ck[:, :-1]] = ck[:, 1:]; nb[a, g, k][ck[:, -1]] = rng.choice(ta, H)
                i = rng.integers(1, VI + 1, 128); i[:32] = 1; i[32 + k:64:4] = 0
                nb[a, g, k][se] = np.where(i < VI, ck[rng.integers(0, H, 128), np.minimum(i, VI - 1)], rng.choice(ta, 128))
    return pack(x, q, lost, nb, snd)
def setup_inputs_ties(rng):
    cen, x, q, lost, nb, snd = corners(rng, 0.2); place = np.argsort(rng.random((N, 8, V)), axis=-1)
    for a in range(N):
        for g in range(8):
            lost[a, g, place[a, g, :48]] = True; lost[a, g, place[a, g, 48:240]] = False
    L = np.sum(lost, axis=(1, 2)); R = A - 8 * TH - 7
    base = np.array([TH] + [R // 8 + (1 if i < R % 8 else 0) for i in range(8)] + [TH + 1] * 7)
    for a in range(N):
        for g in range(8):
            for s in range(48):
                kind = s % 6; v = place[a, g, s]; mo = place[a, g, 48 + 4 * s:52 + 4 * s]
                if kind < 4:
                    c = rng.integers(30, 226, 16); e = np.array(base)
                    e[15] += (int(L[a]) & 7) + (1 if kind == 1 else 0)
                    e[0] += 1 if kind == 2 else 0
                    e = e[rng.permutation(16)]
                    m = np.stack([c + e, c - e, c, c + (1 if kind == 3 else 0)])[rng.permutation(4)]
                else:
                    m = np.zeros((4, 16), np.int64); c = np.zeros(16, np.int64); i = rng.permutation(16); kk = np.sort(rng.permutation(4)[:2])
                    m[kk[0], i[:7]] = rng.integers(160, 200, 7); m[kk[1], i[7:14]] = rng.integers(210, 256, 7)
                    if kind == 5: m = 255 - m; c = 255 - c
                x[a, g][:, mo] = m.T; q[a, g][:, v] = c; nb[a, g][:, v] = mo
    return pack(x, q, lost, nb, snd)
def point(rng, links, slots, bad):
    n = bad.size; S = (N - 1) * G
    pk = np.argsort(rng.random((4, n)), axis=1); back = np.argsort(pk, axis=1); links[:, bad] = bad[pk]
    t = rng.permutation(np.concatenate([np.arange(n), rng.integers(0, n, S - n)])); kk = rng.integers(0, 4, S)
    slots[:] = kk * W + bad[back[kk, t]]
def setup_inputs_flood(rng):
    cen, x, q, lost, nb, snd = corners(rng, 0.15); S = (N - 1) * G; B = 3 * S // 4; E = min(S, V - 2 * SL - 32); H = SL - SL % 256; M = min(SL, S)
    for a in range(N):
        for g in range(8):
            n = (SL + E if a == 0 else SL, 1, B if a == 0 else 0, 0, 8, 8, 8, B)[g]; m = G if g == 6 else SL; c = cen[g, 0][:, None]
            o = rng.permutation(V)
            if g == 0 and a == 0:
                s = int(rng.integers(0, V - SL + 1)); run = (o >= s) & (o < s + SL); rest = o[~run]
                o = np.concatenate([rest[:SL + 32], o[run], rest[SL + 32:]])
            se = o[:m]; good = o[SL:SL + 32]; bad = o[SL + 32:SL + 32 + n]
            lost[a, g] = False; lost[a, g, o[:SL]] = True
            x[a, g][:, good] = np.clip(c + rng.integers(-4, 5, (16, 32)), 0, 255); q[a, g][:, se] = np.clip(c + rng.integers(-6, 7, (16, m)), 0, 255)
            far = np.argsort(rng.random((16, n)), axis=0) < 6
            x[a, g][:, bad] = np.where(far, (c + 128) & 255, np.clip(c + rng.integers(-4, 5, (16, n)), 0, 255))
            nb[a, g][:, se] = rng.choice(good, (4, m)); k = rng.integers(0, 4, m)
            if g == 0:
                nb[a, g, k, se] = rng.permutation(bad[:SL])
                if a == 0: point(rng, nb[a, g], snd[a, g], bad[SL:])
                else: nb[a, g, k[:G], se[:G]] = V + (a - 1) * G + rng.permutation(G)
            elif g == 1: nb[a, g, k, se] = bad[0]
            elif g == 2 and a == 0: point(rng, nb[a, g], snd[a, g], bad)
            elif g == 2: nb[a, g, k[:G], se[:G]] = V + (a - 1) * G + rng.permutation(G)
            elif g == 4 or g == 5:
                sh = o[SL + 40:SL + 72]; kk = rng.integers(0, 4, 32); nb[a, g, kk, sh] = bad[0]
                snd[a, g] = (kk * W + sh)[rng.integers(0, 32, S)]
                if g == 4: nb[a, g, k[:G], se[:G]] = V + rng.permutation(G)
                else: nb[a, g, k[:H], se[:H]] = V + int(rng.integers(0, S))
            elif g == 6:
                sh = o[SL + 40:SL + 72]; kk = rng.integers(0, 4, 32); nb[a, g, kk, sh] = rng.choice(bad, 32)
                snd[a, g].reshape(N - 1, G)[:, :48] = (kk * W + sh)[rng.integers(0, 32, (N - 1, 48))]
                nb[a, g, k, se] = V + rng.integers(0, N - 1, G) * G + rng.integers(0, 4 if a & 1 else 48, G)
            elif g == 7:
                point(rng, nb[a, g], snd[a, g], bad)
                nb[a, g, k[:M], se[:M]] = V + rng.permutation(S)[:M]
    return pack(x, q, lost, nb, snd)
def setup_inputs_spread(rng):
    share = rng.choice(np.array([0.02, 0.1, 0.25, 0.4, 0.6, 0.9]), (N, 8, 1)); share[:, 3] = 0.3; share[int(rng.integers(0, N))] = 0
    cen, x, q, lost, nb, snd = corners(rng, share, True)
    return pack(x, q, lost, nb, snd)
def check_inputs(d):
    bad = []
    x = np.asarray(d["xv"]).astype(np.float32).reshape(N, 8, 16, V); q = np.asarray(d["cq"]).astype(np.float32)
    fine = (x >= 0) & (x <= 255) & (x == np.floor(x)); gone = x == -64
    if not np.all(np.all(fine, axis=2) | np.all(gone, axis=2)): bad.append("columns of xv")
    if not np.all((q >= 0) & (q <= 255) & (q == np.floor(q))): bad.append("range of cq")
    if np.min(d["nb"]) < 0 or np.max(d["nb"]) > W - 1: bad.append("range of nb")
    if np.min(d["snd"]) < 0 or np.max(d["snd"]) > 4 * W - 1 or np.max(np.asarray(d["snd"]) % W) > V - 1: bad.append("entries of snd")
    return bad
def reference(xv, cq, nb, snd):
    x = np.full((N, 8, 16, W), -64, np.int32); x[..., :V] = xv.astype(np.float32).astype(np.int32).reshape(N, 8, 16, V)
    q = cq.astype(np.float32).astype(np.int32).reshape(N, 8, 16, V)
    ln = nb.astype(np.int64).reshape(N, 8, 4, W); sl = np.stack([gentries(a) for a in snd]).astype(np.int64)
    for rnd in range(RO):
        shown = np.take_along_axis(ln.reshape(N, 8, 4 * W), sl, 2)
        col = np.take_along_axis(x, shown[:, :, None, :], 3).reshape(N, 8, 16, N - 1, G)
        x[..., V:] = np.stack([np.concatenate([col[(a - d) % N][:, :, d - 1] for d in range(1, N)], axis=2) for a in range(N)])
        lost = x[:, :, 0, :V] < 0; many = np.add.reduce(lost.astype(np.int64), axis=2)
        lim = A + (np.add.reduce(many, axis=1) & 7)
        nx = np.array(x); nl = np.array(ln); fall = np.zeros((N, 8, W), bool)
        for a in range(N):
            v = np.argsort(~lost[a], axis=1, kind="stable")[:, :SL]; there = np.arange(SL)[None, :] < many[a][:, None]
            qa = np.take_along_axis(q[a], v[:, None, :], 2)[:, :, None, :]
            j = np.take_along_axis(ln[a], np.broadcast_to(v[:, None, :], (8, 4, SL)), 2)
            for t in range(VI):
                m = np.take_along_axis(x[a], j.reshape(8, 1, 4 * SL), 2).reshape(8, 16, 4, SL)
                ok = np.add.reduce((np.abs(m - qa) <= TH).astype(np.int32), axis=1) >= 9
                if t < VI - 1: j = np.where(ok, j, np.take_along_axis(ln[a], j, 2))
            found = np.all(ok, axis=1) & there
            y = (np.add.reduce(m, axis=2) - np.max(m, axis=2) - np.min(m, axis=2)) >> 1
            D = np.add.reduce(np.abs(m - y[:, :, None, :]), axis=1)
            good = np.max(D, axis=1) <= lim[a]
            worst = np.take_along_axis(j, np.argmax(D, axis=1)[:, None, :], 1)[:, 0]
            for g in range(8):
                b = np.flatnonzero(found[g] & good[g]); c = v[g][b]
                nx[a, g][:, c] = y[g][:, b]; nl[a, g][:, c] = j[g][:, b]
                fall[a, g, worst[g][found[g] & ~good[g]]] = True
        for a in range(N):
            down = np.array(fall[a, :, :V])
            for d in range(1, N):
                flag = fall[(a + d) % N, :, V + (d - 1) * G:V + d * G]; s = shown[a, :, (d - 1) * G:d * G]
                for g in range(8):
                    h = s[g][flag[g]]; down[g, h[h < V]] = True
            nx[a, :, :, :V] = np.where(down[:, None, :], -64, nx[a, :, :, :V])
        x = nx; ln = nl
    return {"yx": np.ascontiguousarray(x[..., :V]).reshape(N, 128, V).astype(np.float32).astype(BF), "yn": np.ascontiguousarray(ln[..., :V]).reshape(N, 8, 4 * V).astype(np.float32)}

@@ -1,0 +1,595 @@
+from concourse.bass import DstId, RemoteDMATransfer
+from concourse.mybir import AluOpType as Op, ActivationFunctionType as Fn, AxisListType
+
+N, V, G, W, SL = 4, 1792, 256, 2560, 640
+BF, F32, I32, U16 = "bfloat16", "float32", "int32", "uint16"
+SB = {
+    "X7": (W + SL, F32), "LW": (W + SL, BF), "IDW": (W, BF), "HW": (W + 16, BF), "XB": (V, BF), "QB": (V, BF), "SG": (V, BF),
+    "NB": (640, I32), "NT": (640, I32), "DG": (1280, BF), "IG": (1280, BF), "IH": (640, F32), "SHF": (768, F32),
+    "SN": (48, I32), "SK": (96, I32), "S1": (96, F32), "S2": (48, F32), "CL": (96, U16), "KL": (96, U16), "XL": (48, U16),
+    "MK": (1536, BF), "SH": (768, BF), "XS": (768, BF), "ST": (1536, BF), "FL": (512, BF), "NL": (768, BF), "RB": (1280, BF),
+    "PI": (8, I32), "CI": (8, I32), "CF": (16, F32), "JF": (144, BF), "J16": (128, BF), "REL": (144, BF), "JM": (112, F32),
+    "DM": (112, F32), "DB": (112, F32), "RM": (4, F32), "Z": (9 * 144, BF), "ZF": (144, F32), "ONB": (128, BF), "CA": (128, BF),
+    "CN": (128, BF), "UP": (128, BF), "UH": (2048, BF), "ID": (768, BF), "ALL": (128, BF), "HF": (320, BF), "MW": (16, BF),
+    "SEL": (16, BF), "YS": (32, BF), "C16": (48, F32), "SF": (SL, F32), "SW": (80, F32), "KC": (160, F32), "DK": (48, F32),
+    "JA": (66, BF), "KX": (1280, BF), "KN": (1280, BF),
+    "F": (112, BF), "FN": (112, BF), "INC": (112, F32), "PW": (120, F32), "W2": (112, F32), "TI": (16, I32), "TB": (8, F32),
+    "BS": (7 * 48, BF), "AB": (14 * 128, BF), "LO": (40, U16), "L16": (40, F32), "VF": (40, F32), "VL": (40, U16),
+    "TH": (40, F32), "DV": (40, F32), "LM": (4, F32), "LI": (4, I32),
+    "Q7": (SL, F32), "QS": (SL, BF), "MG": (2 * SL, BF), "R": (2 * W, BF), "LK": (2 * W, BF), "JL": (640, U16), "JB": (640, F32),
+    "SCR": (640, F32), "BST": (160, F32), "BI": (160, I32), "MI": (160, I32), "ML": (160, U16), "MF": (160, F32), "FD": (280, F32),
+    "FT": (40, F32), "M": (W, BF), "MX": (W, BF), "MN": (W, BF), "YB": (SL, BF), "Y7": (SL, F32), "MV": (SL, BF), "KK": (160, F32),
+    "K2": (200, F32), "EQ": (160, F32), "E2": (120, F32), "FA": (160, F32), "WL": (40, U16), "SCL": (40, U16), "GW": (SL, BF),
+    "SC": (80, F32), "BB": (40 * 112, BF), "AA": (40 * 66, BF), "YN": (V, F32), "YX": (V, BF),
+}
+SCRATCH = {n: ("sbuf", [128, c], d) for n, (c, d) in SB.items()}
+SCRATCH["OS"] = ("sbuf", [128, 8, 64], F32)
+SCRATCH["PS"] = ("psum", [128, 3072], F32)
+SCRATCH["PH"] = ("psum", [128, 8, 128], F32)
+KINDS = [(0, "x"), (0, "s"), (0, "f"), (1, "s"), (1, "x"), (1, "f")]
+SEMAPHORES = ["v", "a", "p", "q", "left"] + ["in%d%s" % k for k in KINDS] + ["d%d" % i for i in range(40)]
+M7, M23, M27, M31, B18 = 49152.0, 12582912.0, 201326592.0, 3221225472.0, 262144.0
+CYCLE, PE, GATHER, SCATTER, WAKE, TRIP = 1.04, 0.55, 1.56, 3.8, 60.0, 6000.0
+ORDER, TRIES = [], 400
+AHEAD, WAYS = (3, 4), ("bbbbbaaa", "bbbbaaaa")
+
+
+def route(T, topo, src, dst):
+    if topo.may_write(src, dst):
+        return None
+    far = [c for c in T.cores if c != src and not topo.may_write(src, c)]
+    can = [c for c in topo.cores_of(src) if T.rank_of(c) is None and topo.may_write(c, dst)]
+    can.sort(key=lambda c: topo.die(c) != topo.die(src))
+    return can[far.index(dst) % len(can)]
+
+
+def legs(kind, rank):
+    return [(d, (rank - d) % N if kind == "f" else (rank + d) % N) for d in range(1, N)]
+
+
+def landing(rnd, kind, d):
+    if kind == "s":
+        return "HW", V + (d - 1) * G, G
+    if kind == "x":
+        return "ST", 768 * rnd + (d - 1) * G, G
+    return "NL", 384 * rnd + (d - 1) * 128, 128
+
+
+def slot(rnd, kind):
+    return 640 * rnd + {"s": 0, "x": 256, "f": 512}[kind]
+
+
+def bits(engines):
+    return sum(1 << e for e in engines)
+
+
+def hops(T, topo, core, kind):
+    todo = [(d, r, route(T, topo, core, T.cores[r])) for d, r in legs(kind, T.rank_of(core))]
+    out, used = [], []
+    for d, r, via in todo:
+        if via is None:
+            e = topo.engines(core, T.cores[r]); used += e
+            out.append((d, r, T.cores[r], e))
+    rest = [x for x in todo if x[2] is not None]
+    for i, (d, r, via) in enumerate(rest):
+        free = [e for e in topo.engines(core, via) if e not in used]
+        n = len(free) // len(rest)
+        out.append((d, r, via, free[i * n:(i + 1) * n]))
+    return out
+
+
+def relay_program(g, core, T, topo):
+    jobs = [(s, T.cores[r]) for s in T.cores for r in range(N) if T.cores[r] != s and route(T, topo, s, T.cores[r]) == core]
+    total = 0
+    for src, dst in jobs:
+        rid, pid = topo.addr(dst, core); e = topo.engines(core, dst)
+        for rnd, kind in KINDS:
+            d, n = [(h[0], len(h[3])) for h in hops(T, topo, src, kind) if h[2] == core][0]
+            name, a, w = landing(rnd, kind, d); o = slot(rnd, kind); sem = T.sem["in%d%s" % (rnd, kind)]
+            g.wait_ge(sem, n)
+            g.remote_dma_fused([RemoteDMATransfer(dst_ids=[DstId(rid=rid, pnc=pid)], dma_engine_mask=bits(e), remote_sem=sem,
+                                                  src=T.RB[:, o:o + w], dst=T[name][:, a:a + w])], local_sem=T.sem.left)
+            total += len(e)
+    if total:
+        g.wait_ge(T.sem.left, total)
+
+
+def rank_program(g, core, T, topo):
+    rank = T.rank_of(core)
+    if rank is None:
+        relay_program(g, core, T, topo)
+        return
+    ops, hist, free_sems = [], {}, ["d%d" % i for i in range(40)]
+    queue = {"v": g.vector, "a": g.scalar, "p": g.tensor, "q": g, "s": g.sync}
+
+    def A(name, a=0, b=None, st=None, p=slice(0, 128), lane=None):
+        b = SB[name][0] if b is None else b
+        return (T[name][p, a:b] if st is None else T[name][p, a:b:st], [(name, a, b, lane)], len(range(a, b, st or 1)),
+                2 if SB[name][1] in (BF, U16) else 4, "")
+
+    def PS(bank, a, b, st=None, p=slice(0, 128)):
+        o = 512 * bank
+        ap = T.PS[p, o + a:o + b] if st is None else T.PS[p, o + a:o + b:st]
+        return (ap, [("PS", k, k + 1, None) for k in range((o + a) // 512, (o + b - 1) // 512 + 1)], len(range(a, b, st or 1)), 4, "ps")
+
+    def PH(j, a, b, p=slice(0, 128), j2=None):
+        if j2 is None:
+            return (T.PH[p, j, a:b], [("PS", 6 + j // 4, 7 + j // 4, None)], b - a, 4, "ps")
+        return (T.PH[p, j:j2, a:b], [("PS", k, k + 1, None) for k in range(6 + j // 4, 7 + (j2 - 1) // 4)], (b - a) * (j2 - j), 4, "ps")
+
+    def OS(j, j2, a, b):
+        return (T.OS[0:112, j:j2, a:b], [("OS", j // 4, (j2 - 1) // 4 + 1, None)], (j2 - j) * (b - a), 4, "")
+
+    def IND(win, off):
+        return (win[0].indirect(off[0]), win[1] + off[1], 16 * off[2], win[3], "ind")
+
+    def add(e, fn, rd, wr, cost, sem=None, cnt=0, lag=0.0):
+        me = len(ops); deps, after = set(), set()
+        for regs, w in ((rd, False), (wr, True)):
+            for (n, a, b, lane) in regs:
+                for (a2, b2, lane2, o, w2) in hist.get(n, []):
+                    if a2 >= b or a >= b2 or (lane is not None and lane2 is not None and lane != lane2):
+                        continue
+                    same = ops[o]["e"] == e and ops[o]["sem"] is None
+                    if same and e == "p":
+                        if w or w2:
+                            after.add(o)
+                    elif w or w2 or (n == "PS" and not same):
+                        deps.add(o)
+        ops.append({"e": e, "fn": fn, "deps": deps, "after": after, "sem": sem, "cnt": cnt, "cost": cost, "lag": lag, "need": False})
+        for (n, a, b, lane) in wr:
+            if lane is None:
+                hist[n] = [h for h in hist.get(n, []) if not (a <= h[0] and h[1] <= b)]
+        for regs, w in ((rd, False), (wr, True)):
+            for (n, a, b, lane) in regs:
+                hist.setdefault(n, []).append((a, b, lane, me, w))
+
+    def val(x):
+        return x[0] if isinstance(x, tuple) else x
+
+    def reg(*xs):
+        return [r for x in xs if isinstance(x, tuple) for r in x[1]]
+
+    def span_of(o, i, rate=None, *more):
+        if i[4] == "ind":
+            return 50 + o[2] * GATHER * CYCLE
+        if rate is None:
+            rate = 0.5 if all(x[3] == 2 for x in (o, i) + more) else 1.0
+        return max(64, o[2] * rate) * CYCLE
+
+    def ts(o, i, s1, op0, s2=None, op1=None):
+        if op1 is None:
+            add("v", lambda q: q.tensor_scalar(o[0], i[0], val(s1), None, op0), reg(i, s1), o[1], span_of(o, i))
+        else:
+            add("v", lambda q: q.tensor_scalar(o[0], i[0], val(s1), val(s2), op0, op1), reg(i, s1, s2), o[1], span_of(o, i))
+
+    def tt(o, x, y, op):
+        add("v", lambda q: q.tensor_tensor(o[0], x[0], y[0], op), reg(x, y), o[1], span_of(o, x, 1.0 if "ps" in (x[4], y[4]) else 2.0))
+
+    def cp(o, i):
+        add("v", lambda q: q.tensor_copy(o[0], i[0]), i[1], o[1], span_of(o, i))
+
+    def scatter(win, off, i):
+        add("v", lambda q: q.tensor_copy(win[0].indirect(off[0]), i[0]), reg(off, i), win[1], 50 + i[2] * SCATTER * CYCLE)
+
+    def ms(o, c):
+        add("v", lambda q: q.memset(o[0], c), [], o[1], span_of(o, o))
+
+    def scan(o, x, y, op0, op1):
+        add("v", lambda q: q.tensor_tensor_scan(o[0], x[0], y[0], 0.0, op0, op1), reg(x, y), o[1], span_of(o, x, None, y))
+
+    def act(o, i, f=Fn.Identity, bias=0.0, scale=1.0):
+        add("a", lambda q: q.activation(o[0], i[0], f, bias=val(bias), scale=val(scale)), reg(i, bias, scale), o[1], span_of(o, i, 1.0))
+
+    def mm(o, l, r, start, stop, more=()):
+        add("p", lambda q: q.matmul(o[0], l[0], r[0], start, stop), reg(l, r, *more), o[1], max(64, r[2]) * PE * (4 if l[3] == 4 else 1))
+
+    def iota(o, pat, base=0, cm=0):
+        if SB[o[1][0][0]][1] == I32:
+            add("q", lambda q: q.iota(o[0], pat, base, cm), [], o[1], 130 + 2 * o[2] * CYCLE)
+        else:
+            add("q", lambda q: q.iota(o[0], pat, base, cm, allow_small_or_imprecise_dtypes=True), [], o[1], 130 + 2 * o[2] * CYCLE)
+
+    def dma(o, i, nbytes, e="s"):
+        add(e, lambda q: q.dma_start(o[0], i[0]), i[1], o[1], 60.0, free_sems.pop(0), 16, 1800 + nbytes / 200)
+
+    def send(rnd, kind, src, w, after=()):
+        trs, n = [], 0
+        off = w if kind == "f" else 0
+        for d, r, to, e in hops(T, topo, core, kind):
+            rid, pid = topo.addr(to, core)
+            if to == T.cores[r]:
+                name, a, _ = landing(rnd, kind, d)
+            else:
+                name, a = "RB", slot(rnd, kind)
+            trs.append(RemoteDMATransfer(dst_ids=[DstId(rid=rid, pnc=pid)], dma_engine_mask=bits(e), remote_sem=T.sem["in%d%s" % (rnd, kind)],
+                                         src=T[src][:, off + (d - 1) * w:off + d * w], dst=T[name][:, a:a + w]))
+            n += len(e)
+        sem = free_sems.pop(0)
+        add("q", lambda q: q.remote_dma_fused(trs, local_sem=T.sem[sem]), reg(A(src, off, off + 3 * w), *after) + [("sent", 0, 1, None)],
+            [("sent", 0, 1, None)], 300.0, sem, n, 2500.0)
+        ops[-1]["remote"] = True
+        turn = [o for o in ops[-1]["deps"] if "remote" in ops[o] and ops[o]["src"] != src]
+        ops[-1]["src"] = src; ops[-1]["deps"].difference_update(turn); ops[-1]["after"].update(turn)
+        name, a, _ = landing(rnd, kind, 1)
+        cnt = 0
+        for s in T.cores:
+            if s != core:
+                cnt += len(topo.engines(route(T, topo, s, core) or s, core))
+        add(None, None, [], A(name, a, a + 3 * w)[1], TRIP, "in%d%s" % (rnd, kind), cnt)
+        ops[-1]["after"].add(len(ops) - 2)
+
+    def Z(m, i):
+        if m is None:
+            return A("ZF", 15 - i, 143 - i)
+        return A("Z", 144 * m + 15 - i, 144 * m + 143 - i)
+    ZA, ZB, Z4, Z0, ZL, ZK = 0, 1, 2, 3, 4, 5
+
+    def wrap(out, m, name, a, b, start=True, stop=True):
+        for i in range(16):
+            mm(out, Z(m, i), A(name, a + i, b, 16), start and i == 0, stop and i == 15, [A(name, a, b)])
+
+    def col(name, j):
+        return A(name, j, j + 1)
+
+    def hbm(ap):
+        return (ap, [])
+
+    def zc(m):
+        return A("Z", 144 * m, 144 * m + 144)
+
+    def idm(j):
+        return A("ID", 128 * j, 128 * j + 128)
+    XW, LWW = A("X7", 0, W), A("LW", 0, W)
+
+    dma(A("SN"), hbm(T.snd[:]), 24576); dma(A("XB"), hbm(T.xv[:]), 458752, "a"); dma(A("NB"), hbm(T.nb[:]), 327680)
+    iota(A("PI", 0, 1), [[0, 1]], 0, 1); iota(A("JM"), [[0, 7], [1, 16]]); iota(A("JF"), [[1, 144]]); iota(A("J16"), [[16, 8], [0, 16]])
+    iota(A("C16", 0, 41), [[32, 41]], -1); iota(A("X7", V, W), [[0, W - V]], -448); iota(A("SF"), [[1, SL]])
+    iota(A("DK"), [[4, 3], [0, 16]]); iota(A("SW", 0, 40), [[16, 40]])
+    ms(A("ALL"), 1.0); ms(A("PW", 112, 120), 4096.0); ms(A("HF"), 0.5); ms(A("HW", W, W + 16), 4096.0)
+    p = A("PI", 0, 1)
+    ts(col("CI", 0), p, 240, Op.bitwise_and); ts(col("CI", 1), p, 15, Op.bitwise_and); ts(col("CI", 2), p, 3, Op.bitwise_and)
+    ts(col("CI", 3), p, 2, Op.logical_shift_right); ts(col("CI", 4), p, 2, Op.logical_shift_right, 3, Op.bitwise_and)
+    ts(col("CI", 5), p, 127, Op.bitwise_and)
+    cp(A("CF", 0, 6), A("CI", 0, 6))
+    g16, row, r4, p4, kr, pp = [col("CF", j) for j in range(6)]
+    l2 = col("CF", 6)
+    ts(A("DM"), A("JM"), row, Op.is_equal); ts(A("REL"), A("JF"), g16, Op.subtract); ts(A("ONB"), A("J16"), g16, Op.is_equal)
+    ts(l2, r4, 2.0, Op.is_lt); ts(A("DB"), A("DM"), 4096.0, Op.mult)
+    ts(zc(Z0), A("REL"), 15.0, Op.is_equal, col("DM", 0), Op.mult); ts(A("ZF"), A("REL"), 15.0, Op.is_equal)
+    ts(A("CA"), A("REL", 0, 128), 1.0, Op.add); ts(A("CN"), A("REL", 0, 128), -16.0, Op.add)
+    tt(A("CA"), A("CA"), A("ONB"), Op.mult); tt(A("CN"), A("CN"), A("ONB"), Op.mult)
+    ts(A("RM"), A("JF", 0, 4), kr, Op.is_equal, l2, Op.mult)
+    ts(A("UP"), A("CN"), 16.0, Op.add, row, Op.is_lt); ts(zc(ZA), A("REL"), 15.0, Op.is_equal)
+    for k in range(4):
+        ts(zc(ZK + k), A("REL"), 15.0, Op.is_equal, col("RM", k), Op.mult)
+    ts(zc(ZB), A("REL"), 15.0, Op.is_equal, 32768.0, Op.mult); ts(zc(Z4), A("REL"), 15.0, Op.is_equal, 4.0, Op.mult)
+    ts(zc(ZL), A("REL"), 15.0, Op.is_equal, l2, Op.mult)
+    ts(A("SW", 0, 40), A("SW", 0, 40), row, Op.add); ts(A("SW", 40, 80), A("SW", 0, 40), float(W), Op.add)
+    for j, s in enumerate((1.0, 0.5, -0.5, 7.0, -7.0, -1.0)):
+        ts(idm(j), A("JF", 0, 128), pp, Op.is_equal, s, Op.mult)
+    ts(col("CF", 7), r4, 0.0, Op.is_equal, 0.0625, Op.mult); ts(col("CF", 8), r4, 1.0, Op.is_equal, -1.0, Op.mult)
+    ts(col("CF", 10), r4, 640.0, Op.mult)
+    ts(A("JA"), A("JF", 0, 66), -0.5, Op.add); ts(A("YS"), A("JF", 0, 32), p4, Op.is_equal, l2, Op.mult)
+    ts(col("CF", 9), col("DM", 2), 16.0, Op.mult, col("CF", 8), Op.add)
+    ts(A("SEL", 0, 8), A("J16", 0, 128, 16), g16, Op.is_equal, col("CF", 7), Op.mult)
+    ts(A("SEL", 8, 16), A("J16", 0, 128, 16), g16, Op.is_equal, col("CF", 9), Op.mult)
+    for h in range(16):
+        act(A("UH", 128 * h, 128 * h + 128), A("ONB"), scale=col("DM", h))
+    iota(A("KC"), [[-1, 4], [0, 40]], 3); iota(A("FL"), [[0, 512]]); iota(A("HW", 0, V), [[0, V]])
+    iota(A("KX"), [[0, 320], [256, 4]]); iota(A("KN"), [[0, 320], [-256, 4]], 256)
+    ts(A("SK", 0, 48), A("SN"), 1.0 / 640, Op.mult, 0.5 / 640 - 0.5, Op.add)
+    cp(A("KL", 0, 48), A("SK", 0, 48)); ts(A("S1", 0, 48), A("SK", 0, 48), -640.0, Op.mult)
+    tt(A("S1", 0, 48), A("S1", 0, 48), A("SN"), Op.add); cp(A("CL", 0, 48), A("S1", 0, 48))
+    act(A("MK", 0, 768), IND(A("DB", 0, 16), A("KL", 0, 48)))
+    tt(A("SHF"), IND(A("NB"), A("CL", 0, 48)), A("MK", 0, 768), Op.min)
+    act(A("X7", 0, V), A("XB"), scale=7.0)
+    wrap(PS(4, 0, 112), Z0, "XB", 0, V)
+    ts(A("IH"), A("NB"), -7.5, Op.add, M27, Op.add); act(A("DG", 0, 640), A("IH"), bias=-M27)
+    ts(A("NT"), A("NB"), 15, Op.bitwise_and); cp(A("DG", 640, 1280), A("NT"))
+    for j in range(4):
+        dma(A("LW", 0, W, p=slice(j, 128, 4), lane=j), A("DG", 640 * (j % 2), 640 * (j % 2) + 640), 163840)
+    dma(A("QB"), hbm(T.cq[:]), 458752)
+    ops[-1]["after"].add(len(ops) - 2)
+    iota(A("IG", 640, 1280), [[0, 40], [1, 16]]); iota(A("IH"), [[16, 40], [0, 16]])
+    act(A("IG", 0, 640), A("IH"), bias=col("CF", 10))
+    for j in range(4):
+        dma(A("IDW", 0, W, p=slice(j, 128, 4), lane=j), A("IG", 640 * (j % 2), 640 * (j % 2) + 640), 163840)
+    for j in range(2):
+        dma(A("HW", 0, V, p=slice(j, 128, 16), lane=j), A("IDW", 0, V, p=slice(j, 128, 16)), 28672)
+    ts(A("MW", 0, 4), A("RM"), 4096.0, Op.mult, col("DM", 2), Op.subtract)
+    ts(A("MW", 4, 8), A("MW", 0, 4), col("DM", 2), Op.subtract); ts(A("MW", 8, 12), A("MW", 4, 8), col("DM", 2), Op.subtract)
+    ts(A("SK", 48, 96), A("SK", 0, 48), 2, Op.logical_shift_right)
+    ts(A("S1", 48, 96), A("SK", 48, 96), -float(W), Op.mult); tt(A("S2"), A("SK", 48, 96), A("DK"), Op.add)
+    tt(A("S1", 48, 96), A("S1", 48, 96), A("SN"), Op.add); cp(A("KL", 48, 96), A("S2")); cp(A("CL", 48, 96), A("S1", 48, 96))
+    act(A("MK", 768, 1536), IND(A("MW", 0, 12), A("KL", 48, 96)))
+
+    def shown_digits():
+        tt(A("SH"), IND(LWW, A("CL", 48, 96)), A("MK", 768, 1536), Op.min)
+
+    def show(rnd):
+        act(A("XS"), IND(XW, A("XL")), scale=1.0 / 7)
+        send(rnd, "x", "XS", G)
+
+    def unwrap(lost, kept):
+        ts(A("FN"), A("F"), lost - kept, Op.mult, kept, Op.add)
+        for b in range(4):
+            for h in range(16):
+                mm(PS(b, h, 16 * min(32, 112 - 32 * b), 16), A("UH", 128 * h, 128 * h + 128), A("FN", 32 * b, min(112, 32 * b + 32)), True, True)
+
+    def lose(out, src, b):
+        n = min(512, V - 512 * b)
+        tt(A(out, 512 * b, 512 * b + n), A(src, 512 * b, 512 * b + n), PS(b, 0, n), Op.min)
+
+    def jl(t, k):
+        return A("JL", 160 * t + 40 * k, 160 * t + 40 * k + 40)
+
+    def follow(u, both):
+        t, hf = divmod(u, 2); o = W * (t % 2) + 1280 * hf
+        if both:
+            act(A("LK", o, o + SL), IND(LWW, jl(t, 2 * hf)), scale=col("RM", 2 * hf))
+        else:
+            ts(A("LK", o, o + SL), IND(LWW, jl(t, 2 * hf)), col("RM", 2 * hf), Op.mult)
+        act(A("LK", o + SL, o + 1280), IND(LWW, jl(t, 2 * hf + 1)), scale=col("RM", 2 * hf + 1))
+        wrap(PS(hf, 0, 80), ZA, "LK", o, o + 1280)
+
+    def fetch(u, side):
+        t, hf = divmod(u, 2); o = SL * side
+        act(A("MG", o, o + SL), IND(XW, jl(t, 2 * hf + 1)), scale=1.0 / 7)
+        for a, b in ([(128 * j, 128 * j + 128) for j in range(5)] if side else [(0, 512), (512, SL)]):
+            out = PH(a // 128, 0, 128) if side else PS(4, a, b)
+            mm(out, idm(4), A("QS", a, b), True, False); mm(out, idm(3), A("MG", o + a, o + b), False, True)
+        return PH(0, 0, 128, j2=5) if side else PS(4, 0, SL)
+
+    def score(u):
+        t, hf = divmod(u, 2); c = 80 * hf; new = A("SCR", 80 * u, 80 * u + 80)
+        tt(new if t else A("BST", c, c + 80), PS(2 + hf, 0, 80), A("JB", 80 * u, 80 * u + 80), Op.min)
+        if t:
+            tt(A("BI" if t == 3 else "BST", c, c + 80), A("BST", c, c + 80), new, Op.max)
+        if t == 3:
+            ts(A("MI", c, c + 80), A("BI", c, c + 80), 4095, Op.bitwise_and)
+            cp(A("ML", c, c + 80), A("MI", c, c + 80))
+            for k in (2 * hf, 2 * hf + 1):
+                ts(A("M", k, 640, 4, lane=k), IND(XW, A("ML", 40 * k, 40 * k + 10)), 1.0 / 7, Op.mult)
+                act(A("M", 640 + k, 1280, 4, lane=k), IND(XW, A("ML", 40 * k + 10, 40 * k + 20)), scale=1.0 / 7)
+            for k in (2 * hf, 2 * hf + 1):
+                act(A("M", 1280 + k, W, 4, lane=k), IND(XW, A("ML", 40 * k + 20, 40 * k + 40)), scale=1.0 / 7)
+
+    top, low = slice(0, 112), slice(0, 32)
+    for rnd in range(2):
+        ts(A("F"), PS(4, 0, 112), -1.0 if rnd == 0 else 0.0, Op.is_lt if rnd == 0 else Op.is_ge)
+        mm(PS(5, 0, 112), A("ONB"), A("F"), True, True); mm(PS(5, 112, 224), A("UP"), A("F"), True, True)
+        mm(PS(5, 224, 336), A("ALL"), A("F"), True, True)
+        if rnd:
+            unwrap(-448.0, 2048.0)
+            send(rnd, "s", "SH", G, [A("NL", 0, 384)])
+            for b in range(4):
+                lose("X7", "X7", b)
+        else:
+            wrap(PH(7, 0, 48), None, "SHF", 0, 768)
+            cp(A("XL"), PH(7, 0, 48))
+        show(rnd)
+        if rnd == 0:
+            shown_digits(); send(rnd, "s", "SH", G)
+        scan(A("INC"), A("ALL", 0, 112), PS(5, 0, 112), Op.mult, Op.add)
+        scan(A("W2"), A("DB"), A("INC"), Op.add, Op.min)
+        tt(A("PW", 0, 112), A("INC"), PS(5, 112, 224), Op.subtract)
+        cp(A("TI", 0, 7), A("W2", 15, 112, 16))
+        ts(A("TI", 8, 15), A("TI", 0, 7), 15, Op.bitwise_and)
+        add("v", lambda q: q.tensor_reduce(T.LM[:, 0:1], T.PS[:, 5 * 512 + 224:5 * 512 + 336], AxisListType.X, Op.add), PS(5, 0, 1)[1], col("LM", 0)[1], 120.0)
+        cp(A("TB", 0, 7), A("TI", 8, 15))
+        for b in range(7):
+            act(A("BS", 48 * b, 48 * b + 41), A("C16", 0, 41), Fn.Sign, col("W2", 16 * b + 15), -0.5)
+            ts(A("AB", 256 * b, 256 * b + 128), A("CA"), col("TB", b), Op.is_gt)
+            ts(A("AB", 256 * b + 128, 256 * b + 256), A("CN"), 16.0, Op.add, col("TB", b), Op.is_lt)
+        for b in range(7):
+            mm(PH(0, 0, 40), A("AB", 256 * b, 256 * b + 128), A("BS", 48 * b + 1, 48 * b + 41), b == 0, False, [A("AB", 256 * b, 256 * b + 256)])
+            mm(PH(0, 0, 40), A("AB", 256 * b + 128, 256 * b + 256), A("BS", 48 * b, 48 * b + 40), False, b == 6)
+        cp(col("LI", 0), col("LM", 0))
+        ts(A("LO"), PH(0, 0, 40), -0.5, Op.mult, 56.0, Op.add)
+        act(A("L16"), PH(0, 0, 40), bias=896.0, scale=-8.0)
+        tt(A("GW"), IND(A("PW"), A("LO")), A("SF"), Op.is_le)
+        wrap(PH(4, 0, 40), ZA, "GW", 0, SL)
+        ts(col("LI", 1), col("LI", 0), 7, Op.bitwise_and)
+        ts(A("TH"), A("SW", 0, 40), col("INC", 111), Op.is_lt)
+        ts(col("LM", 1), col("LI", 1), 4.0, Op.mult, 4.0 * 176 + 4, Op.add)
+        tt(A("VF"), PH(4, 0, 40), A("L16"), Op.add)
+        ts(A("VL"), A("VF"), float(V - 1), Op.min)
+        tt(A("DV"), A("VF"), A("SW", 40, 80), Op.subtract)
+        cp(A("GW", 0, 320), IND(LWW, A("VL", 0, 20))); act(A("GW", 320, SL), IND(LWW, A("VL", 20, 40)))
+        act(A("QS"), IND(A("QB"), A("VL")))
+        act(A("Q7"), A("QS"), bias=-M7, scale=7.0)
+        for k in range(4):
+            wrap(PS(k // 2, 40 * (k % 2), 40 * (k % 2) + 40), ZK + k, "GW", 0, SL)
+        act(A("X7", V, W), A("ST", 768 * rnd, 768 * rnd + 768), scale=7.0)
+        for u in range(8):
+            cp(A("JL", 80 * u, 80 * u + 80), PS(u % 2, 0, 80))
+            act(A("JB", 80 * u, 80 * u + 80), PS(u % 2, 0, 80), bias=B18 + 4096.0 * (4 - u // 2))
+            if u < 6:
+                follow(u, u >= AHEAD[rnd])
+        for u in range(8):
+            o = W * (u // 2 % 2) + 1280 * (u % 2); way = WAYS[rnd][u]
+            tt(A("R", o, o + SL), IND(XW, jl(u // 2, 2 * (u % 2))), A("Q7"), Op.subtract)
+            if way == "v":
+                tt(A("R", o + SL, o + 1280), IND(XW, jl(u // 2, 2 * (u % 2) + 1)), A("Q7"), Op.subtract)
+            else:
+                out = fetch(u, sum(x != "v" for x in WAYS[rnd][:u]) % 2)
+            if way == "a":
+                act(A("R", o + SL, o + 1280), out, bias=M7)
+            if way == "b":
+                ts(A("R", o, o + SL), A("R", o, o + SL), M7, Op.is_equal)
+                ts(A("R", o + SL, o + 1280), out, M31, Op.add, M31, Op.is_equal)
+            else:
+                ts(A("R", o, o + 1280), A("R", o, o + 1280), M7, Op.is_equal)
+            wrap(PS(2 + u % 2, 0, 80), ZB, "R", o, o + 1280)
+            score(u)
+        ts(A("FD", 0, 160), A("BI"), B18 + 4095.0, Op.is_gt)
+        ts(A("MF"), A("MI"), -float(W), Op.add)
+        tt(A("FD", 160, 240), A("FD", 0, 80), A("FD", 80, 160), Op.min)
+        tt(A("FD", 240, 280), A("FD", 160, 200), A("FD", 200, 240), Op.min)
+        tt(A("FT"), A("FD", 240, 280), A("TH"), Op.mult)
+        for k in range(4):
+            tt(A("MF", 40 * k, 40 * k + 40), A("MF", 40 * k, 40 * k + 40), A("FT"), Op.mult)
+            act(A("LK", SL * k, SL * k + SL), IND(A("IDW"), A("ML", 40 * k, 40 * k + 40)), scale=col("RM", k))
+        for ch in range(2):
+            o = 1280 * ch; y = A("YB", 320 * ch, 320 * ch + 320)
+            scan(A("MX", o, o + 1280), A("KX"), A("M", o, o + 1280), Op.min, Op.max)
+            scan(A("MN", o, o + 1280), A("KN"), A("M", o, o + 1280), Op.max, Op.min)
+            mm(PS(ch, 0, 320), idm(2), A("HF"), True, False)
+            for k in range(4):
+                mm(PS(ch, 0, 320), idm(1), A("M", o + k, o + 1280, 4), False, False)
+            mm(PS(ch, 0, 320), idm(2), A("MX", o + 3, o + 1280, 4), False, False)
+            mm(PS(ch, 0, 320), idm(2), A("MN", o + 3, o + 1280, 4), False, True)
+            ts(y, PS(ch, 0, 320), M23, Op.add, M23, Op.subtract)
+            for k in range(4):
+                c = SL * k + 320 * ch
+                mm(PS(2 + k % 2, 0, 320), idm(0), A("M", o + k, o + 1280, 4), True, False); mm(PS(2 + k % 2, 0, 320), idm(5), y, False, True)
+                act(A("R", c, c + 320), PS(2 + k % 2, 0, 320), Fn.Abs)
+                if ch and k % 2:
+                    wrap(PS(4 + k // 2, 0, 80), Z4, "R", SL * (k - 1), SL * (k + 1))
+        act(A("Y7"), A("YB"), scale=7.0)
+        tt(A("KK", 0, 80), PS(4, 0, 80), A("KC", 0, 80), Op.add)
+        tt(A("K2", 0, 40), A("KK", 0, 40), A("KK", 40, 80), Op.max)
+        ts(A("K2", 120, 160), A("K2", 0, 40), col("LM", 1), Op.max)
+        tt(A("KK", 80, 160), PS(5, 0, 80), A("KC", 80, 160), Op.add)
+        tt(A("K2", 40, 80), A("KK", 80, 120), A("KK", 120, 160), Op.max)
+        tt(A("K2", 80, 120), A("K2", 120, 160), A("K2", 40, 80), Op.max)
+        tt(A("K2", 160, 200), A("K2", 0, 40), A("K2", 40, 80), Op.max)
+        for k in range(4):
+            tt(A("EQ", 40 * k, 40 * k + 40), A("KK", 40 * k, 40 * k + 40), A("K2", 80, 120), Op.is_equal)
+        tt(A("EQ"), A("EQ"), A("MF"), Op.mult)
+        tt(A("E2", 0, 80), A("EQ", 0, 80), A("EQ", 80, 160), Op.add)
+        tt(A("E2", 80, 120), A("E2", 0, 40), A("E2", 40, 80), Op.add)
+        ts(A("WL"), A("E2", 80, 120), float(W), Op.add)
+        ts(A("FA", 0, 40), A("K2", 160, 200), col("LM", 1), Op.is_lt)
+        tt(A("FA", 40, 80), A("FA", 0, 40), A("FT"), Op.mult)
+        tt(A("FA", 80, 120), A("FA", 40, 80), A("DV"), Op.mult)
+        tt(A("FA", 120, 160), A("FA", 80, 120), A("SW", 40, 80), Op.add)
+        cp(A("SCL"), A("FA", 120, 160))
+        cp(A("GW", 0, 384), IND(A("HW"), A("WL", 0, 24))); act(A("GW", 384, SL), IND(A("HW"), A("WL", 24, 40)))
+        for c in range(5):
+            mm(PS(4, 16 * c, 16 * c + 16), A("GW", 128 * c, 128 * c + 128), A("SEL"), True, True)
+        cp(A("SC"), PS(4, 0, 80))
+        for gr in range(8):
+            for c in range(5):
+                j = 5 * gr + c
+                ts(A("BB", 112 * j, 112 * j + 112), A("JF", 0, 112), col("SC", 16 * c + gr), Op.is_equal)
+                act(A("AA", 66 * j, 66 * j + 65), A("JA", 0, 65), Fn.Sign, col("SC", 16 * c + 8 + gr))
+            for c in range(5):
+                j = 5 * gr + c
+                mm(PH(gr, 0, 65, top), A("BB", 112 * j, 112 * j + 112), A("AA", 66 * j, 66 * j + 65), c == 0, c == 4,
+                   [A("BB", 560 * gr, 560 * gr + 560), A("AA", 330 * gr, 330 * gr + 330)])
+        cp(OS(0, 4, 0, 64), PH(0, 0, 64, top, 4)); act(OS(4, 8, 0, 64), PH(4, 0, 64, top, 8))
+        for d in (1, 2, 3, 0):
+            tt(A("FL", 128 * d, 128 * d + 128, p=top), PH(0, 16 * d + 1, 16 * d + 17, top, 8), OS(0, 8, 16 * d, 16 * d + 16), Op.not_equal)
+        send(rnd, "f", "FL", 128)
+        for ch in range(2):
+            for k in range(4):
+                mm(PS(ch, 0, 320), idm(0), A("LK", SL * k + 320 * ch, SL * k + 320 * ch + 320), k == 0, k == 3)
+            act(A("MV", 320 * ch, 320 * ch + 320), PS(ch, 0, 320))
+        scatter(A("X7"), A("SCL"), A("Y7"))
+        scatter(A("LW"), A("SCL"), A("MV"))
+        ident = A("ID", 0, 112, p=top)
+        if rnd == 0:
+            act(A("SG"), A("X7", 0, V), Fn.Sign, -1.0, -1.0)
+            wrap(PS(4, 0, 112), Z0, "SG", 0, V, stop=False)
+            shown_digits()
+            wrap(PH(7, 0, 48), ZL, "SH", 0, 768)
+            cp(A("XL"), PH(7, 0, 48))
+        else:
+            act(A("XB"), A("X7", 0, V), scale=1.0 / 7)
+            for b in range(4):
+                n = min(512, V - 512 * b)
+                for j in range(n // 128):
+                    mm(PS(5, 128 * j, 128 * j + 128, p=low) if b % 2 else PH(j, 0, 128, low), A("YS"),
+                       A("LW", 512 * b + 128 * j, 512 * b + 128 * j + 128), True, True)
+                act(A("YN", 512 * b, 512 * b + n, p=low), PS(5, 0, n, p=low) if b % 2 else PH(0, 0, 128, low, n // 128))
+            dma(hbm(T.yn[:]), A("YN", p=low), 229376, "a")
+        mm(PS(4, 0, 112), A("FL", 0, 128, p=top), ident, rnd == 1, False)
+        for d in range(3):
+            o = 384 * rnd + 128 * d
+            mm(PS(4, 0, 112), A("NL", o, o + 128, p=top), ident, False, d == 2)
+    ts(A("F"), PS(4, 0, 112), 1.0, Op.is_ge)
+    unwrap(-64.0, 256.0)
+    for b in range(4):
+        n = min(512, V - 512 * b)
+        lose("YX", "XB", b)
+        dma(hbm(T.yx[:, 512 * b:512 * b + n]), A("YX", 512 * b, 512 * b + n), 256 * n)
+
+    cost = [o["cost"] for o in ops]
+    before = [[(d, ops[d]["lag"] + WAKE) for d in o["deps"]] + [(d, 0.0) for d in o["after"] - o["deps"]] for o in ops]
+    behind = [[] for _ in ops]
+    for i, b in enumerate(before):
+        for d, gap in b:
+            behind[d].append((i, gap))
+    every = range(len(ops))
+
+    def fit(turn, first, lead):
+        end, busy = [0.0] * len(ops), {e: [] for e in queue}
+        for i in turn:
+            at = max([lead[i]] + [end[d] + gap for d, gap in first[i]])
+            if ops[i]["e"] is not None:
+                line = busy[ops[i]["e"]]; k = len(line)
+                while k and line[k - 1][1] > at:
+                    k -= 1
+                while k < len(line) and at + cost[i] > line[k][0]:
+                    at = max(at, line[k][1]); k += 1
+                line.insert(k, (at, at + cost[i]))
+            end[i] = at + cost[i]
+        return end
+
+    def place(weight):
+        ahead = [0.0] * len(ops)
+        for i in reversed(every):
+            ahead[i] = weight[i] + max([0.0] + [ahead[j] + gap for j, gap in behind[i]])
+        end = fit(sorted(every, key=lambda i: (-ahead[i], i)), before, [0.0] * len(ops))
+        for _ in range(2):
+            back = fit(sorted(every, key=lambda i: (-end[i], -i)), behind, [o["lag"] for o in ops])
+            end = fit(sorted(every, key=lambda i: (-back[i], i)), before, [0.0] * len(ops))
+        return max(end[i] + ops[i]["lag"] for i in every), end
+
+    if not ORDER:
+        w, seed = cost, 1
+        span, end = place(w)
+        for _ in range(TRIES):
+            w2 = []
+            for c in w:
+                seed = (seed * 1103515245 + 12345) % 2147483648
+                w2.append(c * (0.75 + seed / 2147483648 * 0.5))
+            span2, end2 = place(w2)
+            if span2 < span:
+                span, end, w = span2, end2, w2
+        ORDER.extend(sorted(every, key=lambda i: (end[i] - cost[i], i)))
+
+    known = {e: {} for e in queue}
+    for n, i in enumerate(ORDER):
+        o = ops[i]; o["waits"] = []
+        o["key"], o["val"] = (o["e"], n + 1) if o["sem"] is None else (o["sem"], 1)
+        kn = known[o["e"]] if o["e"] is not None else {}
+        for d in sorted((ops[d] for d in o["deps"] if o["e"] is not None), key=lambda d: -d["place"]):
+            if kn.get(d["key"], 0) < d["val"]:
+                d["need"] = True; o["waits"].append(d)
+                for k, v in d["clock"].items():
+                    kn[k] = max(kn.get(k, 0), v)
+        o["place"] = n; o["clock"] = dict(kn); o["clock"][o["key"]] = o["val"]
+    count = {e: 0 for e in queue}
+    for i in ORDER:
+        o = ops[i]
+        if o["sem"] is None and o["need"]:
+            count[o["e"]] += 1; o["cnt"] = count[o["e"]]
+    for i in ORDER:
+        o = ops[i]
+        if o["e"] is None:
+            continue
+        q = queue[o["e"]]
+        for d in o["waits"]:
+            q.wait_ge(T.sem[d["key"]], d["cnt"])
+        ins = o["fn"](q)
+        if o["sem"] is None:
+            if o["need"]:
+                ins.then_inc(T.sem[o["e"]], 1)
+        elif "remote" not in o:
+            ins.then_inc(T.sem[o["sem"]], 16)
+    for o in ops:
+        if o["sem"] is not None and not o["need"]:
+            g.wait_ge(T.sem[o["sem"]], o["cnt"])

@@ -9,12 +9,12 @@ SB = {
     "SN": (48, I32), "SK": (96, I32), "S1": (96, F32), "S2": (48, F32), "CL": (96, U16), "KL": (96, U16), "XL": (48, U16),
     "MK": (1536, BF), "SH": (768, BF), "XS": (768, BF), "ST": (1536, BF), "FL": (512, BF), "NL": (768, BF), "RB": (1280, BF),
     "PI": (8, I32), "CI": (8, I32), "CF": (16, F32), "JF": (144, BF), "J16": (128, BF), "REL": (144, BF), "JM": (112, F32),
-    "DM": (112, F32), "DB": (112, F32), "RM": (4, F32), "Z": (9 * 144, BF), "ZF": (144, F32), "ONB": (128, BF), "CA": (128, BF),
-    "CN": (128, BF), "UP": (128, BF), "UH": (2048, BF), "ID": (768, BF), "ALL": (128, BF), "HF": (320, BF), "MW": (16, BF),
-    "SEL": (16, BF), "YS": (32, BF), "C16": (48, F32), "SF": (SL, F32), "SW": (80, F32), "KC": (160, F32), "DK": (48, F32),
-    "JA": (66, BF), "KX": (1280, BF), "KN": (1280, BF),
+    "DM": (112, F32), "DB": (112, F32), "RM": (4, F32), "Z": (9 * 144, BF), "ZF": (144, F32), "IDF": (128, F32), "ONB": (128, BF),
+    "CA": (128, BF), "CN": (128, BF), "UP": (128, BF), "UH": (2048, BF), "ID": (768, BF), "ALL": (128, BF), "HF": (320, BF),
+    "MW": (16, BF), "SEL": (16, BF), "YS": (32, BF), "C16": (48, F32), "SF": (SL, F32), "SW": (80, F32), "KC": (160, F32),
+    "DK": (48, F32), "JA": (66, BF), "KX": (1280, BF), "KN": (1280, BF),
     "F": (112, BF), "FN": (112, BF), "INC": (112, F32), "PW": (120, F32), "W2": (112, F32), "TI": (16, I32), "TB": (8, F32),
-    "BS": (7 * 48, BF), "AB": (14 * 128, BF), "LO": (40, U16), "L16": (40, F32), "VF": (40, F32), "VL": (40, U16),
+    "BS": (14 * 48, BF), "AB": (7 * 128, BF), "LO": (40, U16), "L16": (40, F32), "VF": (40, F32), "VL": (40, U16),
     "TH": (40, F32), "DV": (40, F32), "LM": (4, F32), "LI": (4, I32),
     "Q7": (SL, F32), "QS": (SL, BF), "MG": (2 * SL, BF), "R": (2 * W, BF), "LK": (2 * W, BF), "JL": (640, U16), "JB": (640, F32),
     "SCR": (640, F32), "BST": (160, F32), "BI": (160, I32), "MI": (160, I32), "ML": (160, U16), "MF": (160, F32), "FD": (280, F32),
@@ -29,9 +29,11 @@ SCRATCH["PH"] = ("psum", [128, 8, 128], F32)
 KINDS = [(0, "x"), (0, "s"), (0, "f"), (1, "s"), (1, "x"), (1, "f")]
 SEMAPHORES = ["v", "a", "p", "q", "left"] + ["in%d%s" % k for k in KINDS] + ["d%d" % i for i in range(40)]
 M7, M23, M27, M31, B18 = 49152.0, 12582912.0, 201326592.0, 3221225472.0, 262144.0
-CYCLE, PE, GATHER, SCATTER, WAKE, TRIP = 1.04, 0.55, 1.56, 3.8, 60.0, 6000.0
-ORDER, TRIES = [], 400
-AHEAD, WAYS = (3, 4), ("bbbbbaaa", "bbbbaaaa")
+UN7, BACK = 9363.0 / 65536, -448 * 9363.0 / 65536
+CYCLE, PE, GATHER, SCATTER, WAKE, TRIP, FIXED = 0.95, 0.48, 1.56, 3.8, 130.0, 6000.0, 55.0
+CASES = [(0.9, 0.88, 1.0), (0.9, 0.62, 1.0), (1.25, 1.65, 1.1), (1.05, 1.1, 0.8), (1.05, 1.0, 1.4)]
+ORDER, STARTS, TRIES = [], 3, 200
+AHEAD, WAYS = (4, 5), ("bbbbbbaa", "bbbbbaaa")
 
 
 def route(T, topo, src, dst):
@@ -65,17 +67,12 @@ def bits(engines):
 
 def hops(T, topo, core, kind):
     todo = [(d, r, route(T, topo, core, T.cores[r])) for d, r in legs(kind, T.rank_of(core))]
-    out, used = [], []
-    for d, r, via in todo:
-        if via is None:
-            e = topo.engines(core, T.cores[r]); used += e
-            out.append((d, r, T.cores[r], e))
-    rest = [x for x in todo if x[2] is not None]
-    for i, (d, r, via) in enumerate(rest):
-        free = [e for e in topo.engines(core, via) if e not in used]
-        n = len(free) // len(rest)
-        out.append((d, r, via, free[i * n:(i + 1) * n]))
-    return out
+    far = [x for x in todo if x[2] is not None]
+    first = []
+    for i, (d, r, via) in enumerate(far):
+        e = topo.engines(core, via); n = len(e) // len(far)
+        first.append((d, r, via, e[i * n:(i + 1) * n]))
+    return first, [(d, r, T.cores[r], topo.engines(core, T.cores[r])) for d, r, via in todo if via is None]
 
 
 def relay_program(g, core, T, topo):
@@ -84,7 +81,7 @@ def relay_program(g, core, T, topo):
     for src, dst in jobs:
         rid, pid = topo.addr(dst, core); e = topo.engines(core, dst)
         for rnd, kind in KINDS:
-            d, n = [(h[0], len(h[3])) for h in hops(T, topo, src, kind) if h[2] == core][0]
+            d, n = [(h[0], len(h[3])) for h in hops(T, topo, src, kind)[0] if h[2] == core][0]
             name, a, w = landing(rnd, kind, d); o = slot(rnd, kind); sem = T.sem["in%d%s" % (rnd, kind)]
             g.wait_ge(sem, n)
             g.remote_dma_fused([RemoteDMATransfer(dst_ids=[DstId(rid=rid, pnc=pid)], dma_engine_mask=bits(e), remote_sem=sem,
@@ -152,10 +149,10 @@ def rank_program(g, core, T, topo):
 
     def span_of(o, i, rate=None, *more):
         if i[4] == "ind":
-            return 50 + o[2] * GATHER * CYCLE
+            return round(50 + o[2] * GATHER * CYCLE) + 0.5
         if rate is None:
             rate = 0.5 if all(x[3] == 2 for x in (o, i) + more) else 1.0
-        return max(64, o[2] * rate) * CYCLE
+        return FIXED + o[2] * rate * CYCLE
 
     def ts(o, i, s1, op0, s2=None, op1=None):
         if op1 is None:
@@ -170,7 +167,7 @@ def rank_program(g, core, T, topo):
         add("v", lambda q: q.tensor_copy(o[0], i[0]), i[1], o[1], span_of(o, i))
 
     def scatter(win, off, i):
-        add("v", lambda q: q.tensor_copy(win[0].indirect(off[0]), i[0]), reg(off, i), win[1], 50 + i[2] * SCATTER * CYCLE)
+        add("v", lambda q: q.tensor_copy(win[0].indirect(off[0]), i[0]), reg(off, i), win[1], round(50 + i[2] * SCATTER * CYCLE) + 0.5)
 
     def ms(o, c):
         add("v", lambda q: q.memset(o[0], c), [], o[1], span_of(o, o))
@@ -194,30 +191,33 @@ def rank_program(g, core, T, topo):
         add(e, lambda q: q.dma_start(o[0], i[0]), i[1], o[1], 60.0, free_sems.pop(0), 16, 1800 + nbytes / 200)
 
     def send(rnd, kind, src, w, after=()):
-        trs, n = [], 0
         off = w if kind == "f" else 0
-        for d, r, to, e in hops(T, topo, core, kind):
-            rid, pid = topo.addr(to, core)
-            if to == T.cores[r]:
-                name, a, _ = landing(rnd, kind, d)
-            else:
-                name, a = "RB", slot(rnd, kind)
-            trs.append(RemoteDMATransfer(dst_ids=[DstId(rid=rid, pnc=pid)], dma_engine_mask=bits(e), remote_sem=T.sem["in%d%s" % (rnd, kind)],
-                                         src=T[src][:, off + (d - 1) * w:off + d * w], dst=T[name][:, a:a + w]))
-            n += len(e)
-        sem = free_sems.pop(0)
-        add("q", lambda q: q.remote_dma_fused(trs, local_sem=T.sem[sem]), reg(A(src, off, off + 3 * w), *after) + [("sent", 0, 1, None)],
-            [("sent", 0, 1, None)], 300.0, sem, n, 2500.0)
-        ops[-1]["remote"] = True
-        turn = [o for o in ops[-1]["deps"] if "remote" in ops[o] and ops[o]["src"] != src]
-        ops[-1]["src"] = src; ops[-1]["deps"].difference_update(turn); ops[-1]["after"].update(turn)
+        calls = []
+        for pieces in hops(T, topo, core, kind):
+            trs, n, rd = [], 0, []
+            for d, r, to, e in pieces:
+                rid, pid = topo.addr(to, core)
+                name, a = landing(rnd, kind, d)[:2] if to == T.cores[r] else ("RB", slot(rnd, kind))
+                piece = A(src, off + (d - 1) * w, off + d * w)
+                trs.append(RemoteDMATransfer(dst_ids=[DstId(rid=rid, pnc=pid)], dma_engine_mask=bits(e),
+                                             remote_sem=T.sem["in%d%s" % (rnd, kind)], src=piece[0], dst=T[name][:, a:a + w]))
+                n += len(e); rd += piece[1]
+            sem = free_sems.pop(0)
+            add("q", lambda q, trs=trs, sem=sem: q.remote_dma_fused(trs, local_sem=T.sem[sem]), rd + reg(*after) + [("sent", 0, 1, None)],
+                [("sent", 0, 1, None)], 300.0, sem, n, 2500.0)
+            ops[-1]["remote"] = True; calls.append(len(ops) - 1)
+            turn = [o for o in ops[-1]["deps"] if "remote" in ops[o]]
+            ops[-1]["deps"].difference_update(turn); ops[-1]["after"].update(turn)
         name, a, _ = landing(rnd, kind, 1)
         cnt = 0
         for s in T.cores:
             if s != core:
                 cnt += len(topo.engines(route(T, topo, s, core) or s, core))
         add(None, None, [], A(name, a, a + 3 * w)[1], TRIP, "in%d%s" % (rnd, kind), cnt)
-        ops[-1]["after"].add(len(ops) - 2)
+        ops[-1]["after"].update(calls)
+
+    def blocks(kind):
+        return [h[0] for pieces in hops(T, topo, core, kind) for h in pieces]
 
     def Z(m, i):
         if m is None:
@@ -244,7 +244,7 @@ def rank_program(g, core, T, topo):
 
     dma(A("SN"), hbm(T.snd[:]), 24576); dma(A("XB"), hbm(T.xv[:]), 458752, "a"); dma(A("NB"), hbm(T.nb[:]), 327680)
     iota(A("PI", 0, 1), [[0, 1]], 0, 1); iota(A("JM"), [[0, 7], [1, 16]]); iota(A("JF"), [[1, 144]]); iota(A("J16"), [[16, 8], [0, 16]])
-    iota(A("C16", 0, 41), [[32, 41]], -1); iota(A("X7", V, W), [[0, W - V]], -448); iota(A("SF"), [[1, SL]])
+    iota(A("C16", 0, 41), [[32, 41]], -1); iota(A("X7", V, W), [[0, W - V]]); iota(A("SF"), [[1, SL]])
     iota(A("DK"), [[4, 3], [0, 16]]); iota(A("SW", 0, 40), [[16, 40]])
     ms(A("ALL"), 1.0); ms(A("PW", 112, 120), 4096.0); ms(A("HF"), 0.5); ms(A("HW", W, W + 16), 4096.0)
     p = A("PI", 0, 1)
@@ -275,7 +275,7 @@ def rank_program(g, core, T, topo):
     ts(A("SEL", 0, 8), A("J16", 0, 128, 16), g16, Op.is_equal, col("CF", 7), Op.mult)
     ts(A("SEL", 8, 16), A("J16", 0, 128, 16), g16, Op.is_equal, col("CF", 9), Op.mult)
     for h in range(16):
-        act(A("UH", 128 * h, 128 * h + 128), A("ONB"), scale=col("DM", h))
+        act(A("UH", 128 * h, 128 * h + 128), A("ONB"), scale=col("DB", h))
     iota(A("KC"), [[-1, 4], [0, 40]], 3); iota(A("FL"), [[0, 512]]); iota(A("HW", 0, V), [[0, V]])
     iota(A("KX"), [[0, 320], [256, 4]]); iota(A("KN"), [[0, 320], [-256, 4]], 256)
     ts(A("SK", 0, 48), A("SN"), 1.0 / 640, Op.mult, 0.5 / 640 - 0.5, Op.add)
@@ -283,7 +283,8 @@ def rank_program(g, core, T, topo):
     tt(A("S1", 0, 48), A("S1", 0, 48), A("SN"), Op.add); cp(A("CL", 0, 48), A("S1", 0, 48))
     act(A("MK", 0, 768), IND(A("DB", 0, 16), A("KL", 0, 48)))
     tt(A("SHF"), IND(A("NB"), A("CL", 0, 48)), A("MK", 0, 768), Op.min)
-    act(A("X7", 0, V), A("XB"), scale=7.0)
+    act(A("X7", 0, V), A("XB"), bias=448.0, scale=7.0)
+    ts(A("IDF"), A("JF", 0, 128), pp, Op.is_equal)
     wrap(PS(4, 0, 112), Z0, "XB", 0, V)
     ts(A("IH"), A("NB"), -7.5, Op.add, M27, Op.add); act(A("DG", 0, 640), A("IH"), bias=-M27)
     ts(A("NT"), A("NB"), 15, Op.bitwise_and); cp(A("DG", 640, 1280), A("NT"))
@@ -308,18 +309,15 @@ def rank_program(g, core, T, topo):
         tt(A("SH"), IND(LWW, A("CL", 48, 96)), A("MK", 768, 1536), Op.min)
 
     def show(rnd):
-        act(A("XS"), IND(XW, A("XL")), scale=1.0 / 7)
+        for d in blocks("x"):
+            act(A("XS", G * d - G, G * d), IND(XW, A("XL", 16 * d - 16, 16 * d)), bias=BACK, scale=UN7)
         send(rnd, "x", "XS", G)
 
-    def unwrap(lost, kept):
-        ts(A("FN"), A("F"), lost - kept, Op.mult, kept, Op.add)
+    def unwrap(onto):
         for b in range(4):
             for h in range(16):
-                mm(PS(b, h, 16 * min(32, 112 - 32 * b), 16), A("UH", 128 * h, 128 * h + 128), A("FN", 32 * b, min(112, 32 * b + 32)), True, True)
-
-    def lose(out, src, b):
-        n = min(512, V - 512 * b)
-        tt(A(out, 512 * b, 512 * b + n), A(src, 512 * b, 512 * b + n), PS(b, 0, n), Op.min)
+                mm(PS(b, h, 16 * min(32, 112 - 32 * b), 16), A("UH", 128 * h, 128 * h + 128), A("FN", 32 * b, min(112, 32 * b + 32)),
+                   not onto, h == 15 or not onto)
 
     def jl(t, k):
         return A("JL", 160 * t + 40 * k, 160 * t + 40 * k + 40)
@@ -335,25 +333,30 @@ def rank_program(g, core, T, topo):
 
     def fetch(u, side):
         t, hf = divmod(u, 2); o = SL * side
-        act(A("MG", o, o + SL), IND(XW, jl(t, 2 * hf + 1)), scale=1.0 / 7)
+        act(A("MG", o, o + SL), IND(XW, jl(t, 2 * hf + 1)), bias=BACK, scale=UN7)
         for a, b in ([(128 * j, 128 * j + 128) for j in range(5)] if side else [(0, 512), (512, SL)]):
             out = PH(a // 128, 0, 128) if side else PS(4, a, b)
             mm(out, idm(4), A("QS", a, b), True, False); mm(out, idm(3), A("MG", o + a, o + b), False, True)
         return PH(0, 0, 128, j2=5) if side else PS(4, 0, SL)
 
     def score(u):
-        t, hf = divmod(u, 2); c = 80 * hf; new = A("SCR", 80 * u, 80 * u + 80)
-        tt(new if t else A("BST", c, c + 80), PS(2 + hf, 0, 80), A("JB", 80 * u, 80 * u + 80), Op.min)
-        if t:
-            tt(A("BI" if t == 3 else "BST", c, c + 80), A("BST", c, c + 80), new, Op.max)
+        t, hf = divmod(u, 2); c = 80 * hf
+        if t < 3 and hf:
+            new = A("SCR", 160 * t, 160 * t + 160)
+            tt(new if t else A("BST"), PS(2 + t % 2, 0, 160), A("JB", 160 * t, 160 * t + 160), Op.min)
+            if t:
+                tt(A("BST"), A("BST"), new, Op.max)
         if t == 3:
+            new = A("SCR", 80 * u, 80 * u + 80)
+            tt(new, PS(3 - hf, 0, 80), A("JB", 80 * u, 80 * u + 80), Op.min)
+            tt(A("BI", c, c + 80), A("BST", c, c + 80), new, Op.max)
             ts(A("MI", c, c + 80), A("BI", c, c + 80), 4095, Op.bitwise_and)
             cp(A("ML", c, c + 80), A("MI", c, c + 80))
             for k in (2 * hf, 2 * hf + 1):
-                ts(A("M", k, 640, 4, lane=k), IND(XW, A("ML", 40 * k, 40 * k + 10)), 1.0 / 7, Op.mult)
-                act(A("M", 640 + k, 1280, 4, lane=k), IND(XW, A("ML", 40 * k + 10, 40 * k + 20)), scale=1.0 / 7)
+                ts(A("M", k, 640, 4, lane=k), IND(XW, A("ML", 40 * k, 40 * k + 10)), UN7, Op.mult, BACK, Op.add)
+                act(A("M", 640 + k, 1280, 4, lane=k), IND(XW, A("ML", 40 * k + 10, 40 * k + 20)), bias=BACK, scale=UN7)
             for k in (2 * hf, 2 * hf + 1):
-                act(A("M", 1280 + k, W, 4, lane=k), IND(XW, A("ML", 40 * k + 20, 40 * k + 40)), scale=1.0 / 7)
+                act(A("M", 1280 + k, W, 4, lane=k), IND(XW, A("ML", 40 * k + 20, 40 * k + 40)), bias=BACK, scale=UN7)
 
     top, low = slice(0, 112), slice(0, 32)
     for rnd in range(2):
@@ -361,10 +364,11 @@ def rank_program(g, core, T, topo):
         mm(PS(5, 0, 112), A("ONB"), A("F"), True, True); mm(PS(5, 112, 224), A("UP"), A("F"), True, True)
         mm(PS(5, 224, 336), A("ALL"), A("F"), True, True)
         if rnd:
-            unwrap(-448.0, 2048.0)
+            ts(A("FN"), PS(4, 0, 112), 0.0, Op.is_ge, -1.0, Op.mult); unwrap(True)
             send(rnd, "s", "SH", G, [A("NL", 0, 384)])
             for b in range(4):
-                lose("X7", "X7", b)
+                n = min(512, V - 512 * b)
+                act(A("X7", 512 * b, 512 * b + n), PS(b, 0, n), Fn.Relu)
         else:
             wrap(PH(7, 0, 48), None, "SHF", 0, 768)
             cp(A("XL"), PH(7, 0, 48))
@@ -380,11 +384,12 @@ def rank_program(g, core, T, topo):
         cp(A("TB", 0, 7), A("TI", 8, 15))
         for b in range(7):
             act(A("BS", 48 * b, 48 * b + 41), A("C16", 0, 41), Fn.Sign, col("W2", 16 * b + 15), -0.5)
-            ts(A("AB", 256 * b, 256 * b + 128), A("CA"), col("TB", b), Op.is_gt)
-            ts(A("AB", 256 * b + 128, 256 * b + 256), A("CN"), 16.0, Op.add, col("TB", b), Op.is_lt)
+            act(A("BS", 336 + 48 * b, 336 + 48 * b + 40), A("BS", 48 * b, 48 * b + 40), scale=-1.0)
+            ts(A("AB", 128 * b, 128 * b + 128), A("CA"), col("TB", b), Op.is_gt)
         for b in range(7):
-            mm(PH(0, 0, 40), A("AB", 256 * b, 256 * b + 128), A("BS", 48 * b + 1, 48 * b + 41), b == 0, False, [A("AB", 256 * b, 256 * b + 256)])
-            mm(PH(0, 0, 40), A("AB", 256 * b + 128, 256 * b + 256), A("BS", 48 * b, 48 * b + 40), False, b == 6)
+            mm(PH(0, 0, 40), A("ONB"), A("BS", 48 * b, 48 * b + 40), b == 0, False)
+            mm(PH(0, 0, 40), A("AB", 128 * b, 128 * b + 128), A("BS", 48 * b + 1, 48 * b + 41), False, False)
+            mm(PH(0, 0, 40), A("AB", 128 * b, 128 * b + 128), A("BS", 336 + 48 * b, 336 + 48 * b + 40), False, b == 6)
         cp(col("LI", 0), col("LM", 0))
         ts(A("LO"), PH(0, 0, 40), -0.5, Op.mult, 56.0, Op.add)
         act(A("L16"), PH(0, 0, 40), bias=896.0, scale=-8.0)
@@ -393,15 +398,16 @@ def rank_program(g, core, T, topo):
         ts(col("LI", 1), col("LI", 0), 7, Op.bitwise_and)
         ts(A("TH"), A("SW", 0, 40), col("INC", 111), Op.is_lt)
         ts(col("LM", 1), col("LI", 1), 4.0, Op.mult, 4.0 * 176 + 4, Op.add)
+        ts(col("LM", 2), col("LI", 1), 4.0, Op.mult, 4.0 * 176 + 4 + 65536, Op.add)
         tt(A("VF"), PH(4, 0, 40), A("L16"), Op.add)
         ts(A("VL"), A("VF"), float(V - 1), Op.min)
         tt(A("DV"), A("VF"), A("SW", 40, 80), Op.subtract)
         cp(A("GW", 0, 320), IND(LWW, A("VL", 0, 20))); act(A("GW", 320, SL), IND(LWW, A("VL", 20, 40)))
         act(A("QS"), IND(A("QB"), A("VL")))
-        act(A("Q7"), A("QS"), bias=-M7, scale=7.0)
+        act(A("Q7"), A("QS"), bias=448.0 - M7, scale=7.0)
         for k in range(4):
             wrap(PS(k // 2, 40 * (k % 2), 40 * (k % 2) + 40), ZK + k, "GW", 0, SL)
-        act(A("X7", V, W), A("ST", 768 * rnd, 768 * rnd + 768), scale=7.0)
+        act(A("X7", V, W), A("ST", 768 * rnd, 768 * rnd + 768), bias=448.0, scale=7.0)
         for u in range(8):
             cp(A("JL", 80 * u, 80 * u + 80), PS(u % 2, 0, 80))
             act(A("JB", 80 * u, 80 * u + 80), PS(u % 2, 0, 80), bias=B18 + 4096.0 * (4 - u // 2))
@@ -421,15 +427,15 @@ def rank_program(g, core, T, topo):
                 ts(A("R", o + SL, o + 1280), out, M31, Op.add, M31, Op.is_equal)
             else:
                 ts(A("R", o, o + 1280), A("R", o, o + 1280), M7, Op.is_equal)
-            wrap(PS(2 + u % 2, 0, 80), ZB, "R", o, o + 1280)
+            wrap(PS(2 + u // 2 % 2, 80 * (u % 2), 80 * (u % 2) + 80) if u < 6 else PS(9 - u, 0, 80), ZB, "R", o, o + 1280)
             score(u)
         ts(A("FD", 0, 160), A("BI"), B18 + 4095.0, Op.is_gt)
         ts(A("MF"), A("MI"), -float(W), Op.add)
         tt(A("FD", 160, 240), A("FD", 0, 80), A("FD", 80, 160), Op.min)
         tt(A("FD", 240, 280), A("FD", 160, 200), A("FD", 200, 240), Op.min)
         tt(A("FT"), A("FD", 240, 280), A("TH"), Op.mult)
+        ts(A("FA", 0, 40), A("FT"), col("LM", 1), Op.mult); ts(A("FT"), A("FT"), -65536.0, Op.mult, col("LM", 2), Op.add)
         for k in range(4):
-            tt(A("MF", 40 * k, 40 * k + 40), A("MF", 40 * k, 40 * k + 40), A("FT"), Op.mult)
             act(A("LK", SL * k, SL * k + SL), IND(A("IDW"), A("ML", 40 * k, 40 * k + 40)), scale=col("RM", k))
         for ch in range(2):
             o = 1280 * ch; y = A("YB", 320 * ch, 320 * ch + 320)
@@ -447,10 +453,10 @@ def rank_program(g, core, T, topo):
                 act(A("R", c, c + 320), PS(2 + k % 2, 0, 320), Fn.Abs)
                 if ch and k % 2:
                     wrap(PS(4 + k // 2, 0, 80), Z4, "R", SL * (k - 1), SL * (k + 1))
-        act(A("Y7"), A("YB"), scale=7.0)
+        act(A("Y7"), A("YB"), bias=448.0, scale=7.0)
         tt(A("KK", 0, 80), PS(4, 0, 80), A("KC", 0, 80), Op.add)
         tt(A("K2", 0, 40), A("KK", 0, 40), A("KK", 40, 80), Op.max)
-        ts(A("K2", 120, 160), A("K2", 0, 40), col("LM", 1), Op.max)
+        tt(A("K2", 120, 160), A("K2", 0, 40), A("FT"), Op.max)
         tt(A("KK", 80, 160), PS(5, 0, 80), A("KC", 80, 160), Op.add)
         tt(A("K2", 40, 80), A("KK", 80, 120), A("KK", 120, 160), Op.max)
         tt(A("K2", 80, 120), A("K2", 120, 160), A("K2", 40, 80), Op.max)
@@ -461,8 +467,7 @@ def rank_program(g, core, T, topo):
         tt(A("E2", 0, 80), A("EQ", 0, 80), A("EQ", 80, 160), Op.add)
         tt(A("E2", 80, 120), A("E2", 0, 40), A("E2", 40, 80), Op.add)
         ts(A("WL"), A("E2", 80, 120), float(W), Op.add)
-        ts(A("FA", 0, 40), A("K2", 160, 200), col("LM", 1), Op.is_lt)
-        tt(A("FA", 40, 80), A("FA", 0, 40), A("FT"), Op.mult)
+        tt(A("FA", 40, 80), A("K2", 160, 200), A("FA", 0, 40), Op.is_lt)
         tt(A("FA", 80, 120), A("FA", 40, 80), A("DV"), Op.mult)
         tt(A("FA", 120, 160), A("FA", 80, 120), A("SW", 40, 80), Op.add)
         cp(A("SCL"), A("FA", 120, 160))
@@ -480,7 +485,7 @@ def rank_program(g, core, T, topo):
                 mm(PH(gr, 0, 65, top), A("BB", 112 * j, 112 * j + 112), A("AA", 66 * j, 66 * j + 65), c == 0, c == 4,
                    [A("BB", 560 * gr, 560 * gr + 560), A("AA", 330 * gr, 330 * gr + 330)])
         cp(OS(0, 4, 0, 64), PH(0, 0, 64, top, 4)); act(OS(4, 8, 0, 64), PH(4, 0, 64, top, 8))
-        for d in (1, 2, 3, 0):
+        for d in blocks("f") + [0]:
             tt(A("FL", 128 * d, 128 * d + 128, p=top), PH(0, 16 * d + 1, 16 * d + 17, top, 8), OS(0, 8, 16 * d, 16 * d + 16), Op.not_equal)
         send(rnd, "f", "FL", 128)
         for ch in range(2):
@@ -491,13 +496,16 @@ def rank_program(g, core, T, topo):
         scatter(A("LW"), A("SCL"), A("MV"))
         ident = A("ID", 0, 112, p=top)
         if rnd == 0:
-            act(A("SG"), A("X7", 0, V), Fn.Sign, -1.0, -1.0)
+            act(A("SG"), A("X7", 0, V), Fn.Sign, 1.0, -1.0)
+            for b in range(4):
+                n = min(512, V - 512 * b)
+                mm(PS(b, 0, n), A("IDF"), A("X7", 512 * b, 512 * b + n), True, False)
             wrap(PS(4, 0, 112), Z0, "SG", 0, V, stop=False)
             shown_digits()
             wrap(PH(7, 0, 48), ZL, "SH", 0, 768)
             cp(A("XL"), PH(7, 0, 48))
         else:
-            act(A("XB"), A("X7", 0, V), scale=1.0 / 7)
+            act(A("XB"), A("X7", 0, V), bias=BACK, scale=UN7)
             for b in range(4):
                 n = min(512, V - 512 * b)
                 for j in range(n // 128):
@@ -509,11 +517,10 @@ def rank_program(g, core, T, topo):
         for d in range(3):
             o = 384 * rnd + 128 * d
             mm(PS(4, 0, 112), A("NL", o, o + 128, p=top), ident, False, d == 2)
-    ts(A("F"), PS(4, 0, 112), 1.0, Op.is_ge)
-    unwrap(-64.0, 256.0)
+    ts(A("FN"), PS(4, 0, 112), 1.0, Op.is_lt, 1.0 / 64, Op.subtract); unwrap(False)
     for b in range(4):
         n = min(512, V - 512 * b)
-        lose("YX", "XB", b)
+        tt(A("YX", 512 * b, 512 * b + n), A("XB", 512 * b, 512 * b + n), PS(b, 0, n), Op.min)
         dma(hbm(T.yx[:, 512 * b:512 * b + n]), A("YX", 512 * b, 512 * b + n), 256 * n)
 
     cost = [o["cost"] for o in ops]
@@ -523,6 +530,8 @@ def rank_program(g, core, T, topo):
         for d, gap in b:
             behind[d].append((i, gap))
     every = range(len(ops))
+    cases = [[o["cost"] * (trip if o["e"] is None else 1.0 if o["sem"] else ga if o["cost"] % 1 == 0.5 else co) for o in ops]
+             for co, ga, trip in CASES]
 
     def fit(turn, first, lead):
         end, busy = [0.0] * len(ops), {e: [] for e in queue}
@@ -546,19 +555,32 @@ def rank_program(g, core, T, topo):
         for _ in range(2):
             back = fit(sorted(every, key=lambda i: (-end[i], -i)), behind, [o["lag"] for o in ops])
             end = fit(sorted(every, key=lambda i: (-back[i], i)), before, [0.0] * len(ops))
-        return max(end[i] + ops[i]["lag"] for i in every), end
+        turn = sorted(every, key=lambda i: (end[i] - cost[i], i)); total = 0.0
+        for c in cases:
+            done, free = [0.0] * len(ops), {e: 0.0 for e in queue}
+            for i in turn:
+                e = ops[i]["e"]
+                done[i] = max([free.get(e, 0.0)] + [done[d] + gap for d, gap in before[i]]) + c[i]
+                if e is not None:
+                    free[e] = done[i]
+            total += max(done[i] + ops[i]["lag"] for i in every)
+        return total, end
 
     if not ORDER:
-        w, seed = cost, 1
-        span, end = place(w)
-        for _ in range(TRIES):
-            w2 = []
-            for c in w:
-                seed = (seed * 1103515245 + 12345) % 2147483648
-                w2.append(c * (0.75 + seed / 2147483648 * 0.5))
-            span2, end2 = place(w2)
-            if span2 < span:
-                span, end, w = span2, end2, w2
+        seed, found = 1, []
+        for _ in range(STARTS):
+            w = cost
+            span, end = place(w)
+            for n in range(TRIES):
+                w2, wide = [], 0.5 if n % 2 else 0.25
+                for c in w:
+                    seed = (seed * 1103515245 + 12345) % 2147483648
+                    w2.append(c * (1 + (seed / 2147483648 - 0.5) * wide))
+                span2, end2 = place(w2)
+                if span2 < span:
+                    span, end, w = span2, end2, w2
+            found.append((span, end))
+        end = min(found)[1]
         ORDER.extend(sorted(every, key=lambda i: (end[i] - cost[i], i)))
 
     known = {e: {} for e in queue}

@@ -1,39 +1,44 @@
+import math
 from concourse.bass import DstId, RemoteDMATransfer
 from concourse.mybir import AluOpType as Op, ActivationFunctionType as Fn, AxisListType
 
 N, V, G, W, SL = 4, 1792, 256, 2560, 640
 BF, F32, I32, U16 = "bfloat16", "float32", "int32", "uint16"
 SB = {
-    "X7": (W + SL, F32), "LW": (W + SL, BF), "IDW": (W, BF), "HW": (W + 16, BF), "XB": (V, BF), "QB": (V, BF), "SG": (V, BF),
+    "X7": (W + SL, F32), "LW": (W + SL, BF), "XB": (W + SL, BF), "IDW": (W, BF), "HW": (W + 16, BF), "QB": (V + 16, BF), "X0": (V, BF),
     "NB": (640, I32), "NT": (640, I32), "DG": (1280, BF), "IG": (1280, BF), "IH": (640, F32), "SHF": (768, F32),
     "SN": (48, I32), "SK": (96, I32), "S1": (96, F32), "S2": (48, F32), "CL": (96, U16), "KL": (96, U16), "XL": (48, U16),
     "MK": (1536, BF), "SH": (768, BF), "XS": (768, BF), "ST": (1536, BF), "FL": (512, BF), "NL": (768, BF), "RB": (1280, BF),
-    "PI": (8, I32), "CI": (8, I32), "CF": (16, F32), "JF": (144, BF), "J16": (128, BF), "REL": (144, BF), "JM": (112, F32),
-    "DM": (112, F32), "DB": (112, F32), "RM": (4, F32), "Z": (9 * 144, BF), "ZF": (144, F32), "IDF": (128, F32), "ONB": (128, BF),
-    "CA": (128, BF), "CN": (128, BF), "UP": (128, BF), "UH": (2048, BF), "ID": (768, BF), "ALL": (128, BF), "HF": (320, BF),
-    "MW": (16, BF), "SEL": (16, BF), "YS": (32, BF), "C16": (48, F32), "SF": (SL, F32), "SW": (80, F32), "KC": (160, F32),
-    "DK": (48, F32), "JA": (66, BF), "KX": (1280, BF), "KN": (1280, BF),
-    "F": (112, BF), "FN": (112, BF), "INC": (112, F32), "PW": (120, F32), "W2": (112, F32), "TI": (16, I32), "TB": (8, F32),
-    "BS": (14 * 48, BF), "AB": (7 * 128, BF), "LO": (40, U16), "L16": (40, F32), "VF": (40, F32), "VL": (40, U16),
-    "TH": (40, F32), "DV": (40, F32), "LM": (4, F32), "LI": (4, I32),
-    "Q7": (SL, F32), "QS": (SL, BF), "MG": (2 * SL, BF), "R": (2 * W, BF), "LK": (2 * W, BF), "JL": (640, U16), "JB": (640, F32),
-    "SCR": (640, F32), "BST": (160, F32), "BI": (160, I32), "MI": (160, I32), "ML": (160, U16), "MF": (160, F32), "FD": (280, F32),
-    "FT": (40, F32), "M": (W, BF), "MX": (W, BF), "MN": (W, BF), "YB": (SL, BF), "Y7": (SL, F32), "MV": (SL, BF), "KK": (160, F32),
-    "K2": (200, F32), "EQ": (160, F32), "E2": (120, F32), "FA": (160, F32), "WL": (40, U16), "SCL": (40, U16), "GW": (SL, BF),
-    "SC": (80, F32), "BB": (40 * 112, BF), "AA": (40 * 66, BF), "YN": (V, F32), "YX": (V, BF),
+    "CI": (8, I32), "CF": (16, F32), "JF": (160, BF), "J16": (128, BF), "REL": (144, BF), "JM": (112, F32),
+    "DM": (112, F32), "DB": (112, F32), "RM": (4, F32), "Z": (9 * 144, BF), "ZF": (144, F32), "ZS": (144, BF), "C112": (112, BF),
+    "ONB": (128, BF), "CA": (128, BF), "UP": (128, BF), "ID": (896, BF), "KEEP": (112, U16),
+    "ALL": (144, BF), "HF": (384, BF), "MW": (16, BF), "SEL": (8, BF), "YS": (132, BF), "C16": (48, F32), "SF": (SL, F32),
+    "SW": (40, F32), "DK": (48, F32), "JA": (260, BF), "SX": (520, BF), "KX": (1536, BF), "KN": (1536, BF),
+    "F": (112, BF), "INC": (112, F32), "PW": (120, F32), "W2": (112, F32), "TB": (8, F32),
+    "BS": (14 * 41, BF), "AB": (7 * 128, BF), "LO": (40, U16), "L16": (40, BF), "VL": (40, U16),
+    "VF": (40, F32), "NF": (40, BF), "KC": (96, BF), "LM": (4, F32), "LI": (4, I32), "GW": (SL, BF), "GL": (SL, BF), "GH": (SL, BF),
+    "Q7": (SL, F32), "QS": (SL, BF), "MG": (2 * SL, BF), "R": (2 * W, BF), "LK": (2 * W, BF), "JL": (640, U16), "JB": (800, F32),
+    "SS": (800, I32), "MI": (160, I32), "ML": (160, U16), "MF": (160, F32), "FD": (120, F32),
+    "M": (W, BF), "MX": (W, BF), "MN": (W, BF), "YB": (SL, BF), "MV": (SL, BF), "KD": (96, F32),
+    "KS": (160, F32), "EQ": (160, F32), "E2": (160, F32), "K4": (96, F32), "FA": (120, F32), "WL": (40, U16), "SCL": (40, U16),
+    "BB": (40 * 112, BF), "AA": (40 * 65, BF), "YN": (448, F32), "YX": (V, BF),
 }
 SCRATCH = {n: ("sbuf", [128, c], d) for n, (c, d) in SB.items()}
 SCRATCH["OS"] = ("sbuf", [128, 8, 64], F32)
+SCRATCH["RD"] = ("sbuf", [128, 40, 64], BF)
 SCRATCH["PS"] = ("psum", [128, 3072], F32)
 SCRATCH["PH"] = ("psum", [128, 8, 128], F32)
 KINDS = [(0, "x"), (0, "s"), (0, "f"), (1, "s"), (1, "x"), (1, "f")]
 SEMAPHORES = ["v", "a", "p", "q", "left"] + ["in%d%s" % k for k in KINDS] + ["d%d" % i for i in range(40)]
 M7, M23, M27, M31, B18 = 49152.0, 12582912.0, 201326592.0, 3221225472.0, 262144.0
 UN7, BACK = 9363.0 / 65536, -448 * 9363.0 / 65536
-CYCLE, PE, GATHER, SCATTER, WAKE, TRIP, FIXED = 0.95, 0.48, 1.56, 3.8, 130.0, 6000.0, 55.0
-CASES = [(0.9, 0.88, 1.0), (0.9, 0.62, 1.0), (1.25, 1.65, 1.1), (1.05, 1.1, 0.8), (1.05, 1.0, 1.4)]
-ORDER, STARTS, TRIES = [], 3, 200
-AHEAD, WAYS = (4, 5), ("bbbbbbaa", "bbbbbaaa")
+CASES = [(0.855, 1.52, 3.7, 6000.0, 50.0), (1.1, 2.0, 5.0, 5500.0, -65.0), (0.95, 1.15, 2.5, 7500.0, 55.0)]
+WAKE, ORDER, HEAT, STEPS = 130.0, [], 200.0, 120000
+PARTS = ((0, 24), (24, 40))
+FOLLOW = (("vava" "aaaa" "aaaa", "vava" "aaaa" "aaaa"), ("vava" "aaaa" "aaaa", "vava" "aaaa" "aaaa"))
+TEST = (("vvvv" "vvvv" "vvva" "vvva", "vvaa" "vvaa" "vvaa" "vvaa"), ("vvvv" "vvvv" "vvva" "vvva", "vvaa" "vvaa" "vvaa" "vvaa"))
+KEEP, LAST, SHOW, GHOST = "vava", "vava", ("ava", "ava"), (384, 384)
+MONU, HOME = (0, 8), (0, 8)
 
 
 def route(T, topo, src, dst):
@@ -91,6 +96,135 @@ def relay_program(g, core, T, topo):
         g.wait_ge(T.sem.left, total)
 
 
+def arrange(eng, other, before, lag, cases, spare):
+    n = len(eng); every = range(n); above = [0] * n; first = []; then = [[] for _ in every]
+    for i in every:
+        first.append([(d, gap) for d, gap in before[i] if not any(above[x] >> d & 1 and (y > 0 or gap == 0) for x, y in before[i])])
+        for d, gap in before[i]:
+            if gap > 0 or lag[d] == 0:
+                above[i] |= above[d] | 1 << d
+        for d, gap in first[i]:
+            then[d].append((i, gap))
+
+    def fit(turn, links, lead, cost):
+        end, busy = [0.0] * n, {e: [] for e in eng}
+        for i in turn:
+            at = max([lead[i]] + [end[d] + gap for d, gap in links[i]])
+            if eng[i]:
+                line = busy[eng[i]]; k = len(line)
+                while k and line[k - 1][1] > at:
+                    k -= 1
+                while k < len(line) and at + cost[i] > line[k][0]:
+                    at = max(at, line[k][1]); k += 1
+                line.insert(k, (at, at + cost[i]))
+            end[i] = at + cost[i]
+        return end
+
+    def sweep(turn, cost, links, lead, out, a, b, step):
+        free = {None: 0.0}
+        for k in range(a, b + step, step):
+            i = turn[k]; e = eng[i]; at = free.get(e)
+            if at is None:
+                j = a - step
+                while 0 <= j < n and eng[turn[j]] != e:
+                    j -= step
+                at = out[turn[j]] if 0 <= j < n else 0.0
+            if lead[i] > at:
+                at = lead[i]
+            for d, gap in links[i]:
+                x = out[d] + gap
+                if x > at:
+                    at = x
+            out[i] = at = at + cost[i]
+            if e:
+                free[e] = at
+
+    def flip(i):
+        eng[i], other[i] = other[i], eng[i]
+        for c, c2 in zip(cases, spare):
+            c[i], c2[i] = c2[i], c[i]
+    none = [0.0] * n; back = [0.0] * n
+    for i in reversed(every):
+        back[i] = cases[0][i] + max([lag[i]] + [back[j] + gap for j, gap in then[i]])
+    for _ in range(3):
+        end = fit(sorted(every, key=lambda i: (-back[i], i)), first, none, cases[0])
+        back = fit(sorted(every, key=lambda i: (-end[i], -i)), then, lag, cases[0])
+    turn = sorted(every, key=lambda i: (end[i] - cases[0][i], i))
+    done, left = [none[:] for c in cases], [none[:] for c in cases]
+    best, pos, seed, lo = (1e30,), [0] * n, 1, n
+    for step in range(STEPS + 1):
+        if step % 400 == 0 or step == STEPS:
+            for c, d, l in zip(cases, done, left):
+                sweep(turn, c, first, none, d, 0, n - 1, 1); sweep(turn, c, then, lag, l, n - 1, 0, -1)
+            span = [max(l) for l in left]; now = sum(span); pairs = None
+            best = min(best, (now, turn[:], eng[:]))
+            lo = lo + 100 if lo + 240 < n else 0; hi = min(n, lo + 240) - 1
+            for k, i in enumerate(turn):
+                pos[i] = k
+            over = [max([0.0] + [d[i] + lag[i] for i in turn[:lo]] + [l[i] for i in turn[hi + 1:]] +
+                        [d[i] + gap + l[j] for i in turn[:lo] for j, gap in then[i] if pos[j] > hi]) for d, l in zip(done, left)]
+        if pairs is None:
+            pairs = []
+            for d, l, s in zip(done, left, span):
+                last = {}
+                for i in turn[lo:hi + 1]:
+                    e = eng[i]
+                    if e in last and d[last[e]] + l[i] > s - 1.0:
+                        pairs.append((last[e], i))
+                    if e:
+                        last[e] = i
+        if not pairs:
+            continue
+        seed = (seed * 1103515245 + 12345) % 2147483648; v, u = pairs[(seed >> 6) % len(pairs)]
+        seed = (seed * 1103515245 + 12345) % 2147483648; far, kind = seed >> 8 & 3, (seed >> 12) % 5
+        swap = -1
+        if kind == 4:
+            swap = u if far & 1 else v
+            if not other[swap]:
+                continue
+            new = turn; a = b = pos[swap]; flip(swap)
+        else:
+            way, who, p, links = (-1, u, pos[v], first) if kind & 1 else (1, v, pos[u], then)
+            k = p + way
+            while far and lo <= k <= hi:
+                if eng[turn[k]] == eng[u]:
+                    p = k; far -= 1
+                k += way
+            move, todo = {who}, [who]
+            while todo and len(move) < 9:
+                for d, gap in links[todo.pop()]:
+                    if (pos[d] - p) * way <= 0 and d not in move:
+                        move.add(d); todo.append(d)
+            if todo or turn[p] in move:
+                continue
+            a, b = min(p, pos[who]), max(p, pos[who])
+            new = turn[:a] + sorted(turn[a:b + 1], key=lambda i: (i in move) * way) + turn[b + 1:]
+        seed = (seed * 1103515245 + 12345) % 2147483648
+        bar = now - HEAT * (1 - step / STEPS) * math.log((seed + 1) / 2147483649)
+        seg = new[a:b + 1]; low = 0.0; old = []
+        for c, d, l in zip(cases, done, left):
+            old.append([(i, d[i], l[i]) for i in seg])
+            sweep(new, c, first, none, d, a, b, 1); sweep(new, c, then, lag, l, b, a, -1)
+            low += max(d[i] + l[i] - c[i] for i in seg)
+        if low <= bar:
+            d2, l2, seg = [d[:] for d in done], [l[:] for l in left], new[lo:hi + 1]
+            for c, d, l in zip(cases, d2, l2):
+                sweep(new, c, first, none, d, b + 1, hi, 1); sweep(new, c, then, lag, l, a - 1, lo, -1)
+            s2 = [max(x, max(d[i] + l[i] - c[i] for i in seg)) for c, d, l, x in zip(cases, d2, l2, over)]; low = sum(s2)
+        if low <= bar:
+            now, done, left, span, pairs = low, d2, l2, s2, None
+            turn = new[:lo] + [i for x, k, i in sorted((done[0][i] - cases[0][i], k, i) for k, i in enumerate(seg))] + new[hi + 1:]
+            for k in range(lo, hi + 1):
+                pos[turn[k]] = k
+        else:
+            for was, d, l in zip(old, done, left):
+                for i, x, y in was:
+                    d[i], l[i] = x, y
+            if swap >= 0:
+                flip(swap)
+    return best[1:]
+
+
 def rank_program(g, core, T, topo):
     rank = T.rank_of(core)
     if rank is None:
@@ -117,10 +251,13 @@ def rank_program(g, core, T, topo):
     def OS(j, j2, a, b):
         return (T.OS[0:112, j:j2, a:b], [("OS", j // 4, (j2 - 1) // 4 + 1, None)], (j2 - j) * (b - a), 4, "")
 
+    def RD(c, c2, a, b):
+        return (T.RD[:, c:c2, a:b], [("RD", c, c2, None)], (c2 - c) * (b - a), 2, "")
+
     def IND(win, off):
         return (win[0].indirect(off[0]), win[1] + off[1], 16 * off[2], win[3], "ind")
 
-    def add(e, fn, rd, wr, cost, sem=None, cnt=0, lag=0.0):
+    def add(e, fn, rd, wr, cost, sem=None, cnt=0, lag=0.0, both=None):
         me = len(ops); deps, after = set(), set()
         for regs, w in ((rd, False), (wr, True)):
             for (n, a, b, lane) in regs:
@@ -131,9 +268,9 @@ def rank_program(g, core, T, topo):
                     if same and e == "p":
                         if w or w2:
                             after.add(o)
-                    elif w or w2 or (n == "PS" and not same):
+                    elif w or w2 or (n == "PS" and (not same or both or ops[o]["both"])):
                         deps.add(o)
-        ops.append({"e": e, "fn": fn, "deps": deps, "after": after, "sem": sem, "cnt": cnt, "cost": cost, "lag": lag, "need": False})
+        ops.append({"e": e, "fn": fn, "deps": deps, "after": after, "sem": sem, "cnt": cnt, "cost": cost, "lag": lag, "both": both, "need": False})
         for (n, a, b, lane) in wr:
             if lane is None:
                 hist[n] = [h for h in hist.get(n, []) if not (a <= h[0] and h[1] <= b)]
@@ -149,10 +286,10 @@ def rank_program(g, core, T, topo):
 
     def span_of(o, i, rate=None, *more):
         if i[4] == "ind":
-            return round(50 + o[2] * GATHER * CYCLE) + 0.5
+            return ("gather", o[2])
         if rate is None:
             rate = 0.5 if all(x[3] == 2 for x in (o, i) + more) else 1.0
-        return FIXED + o[2] * rate * CYCLE
+        return ("call", o[2] * rate)
 
     def ts(o, i, s1, op0, s2=None, op1=None):
         if op1 is None:
@@ -167,28 +304,45 @@ def rank_program(g, core, T, topo):
         add("v", lambda q: q.tensor_copy(o[0], i[0]), i[1], o[1], span_of(o, i))
 
     def scatter(win, off, i):
-        add("v", lambda q: q.tensor_copy(win[0].indirect(off[0]), i[0]), reg(off, i), win[1], round(50 + i[2] * SCATTER * CYCLE) + 0.5)
+        add("v", lambda q: q.tensor_copy(win[0].indirect(off[0]), i[0]), reg(off, i), win[1], ("scatter", i[2]))
 
     def ms(o, c):
         add("v", lambda q: q.memset(o[0], c), [], o[1], span_of(o, o))
 
-    def scan(o, x, y, op0, op1):
-        add("v", lambda q: q.tensor_tensor_scan(o[0], x[0], y[0], 0.0, op0, op1), reg(x, y), o[1], span_of(o, x, None, y))
+    def scan(o, x, y, op0, op1, first=0.0):
+        add("v", lambda q: q.tensor_tensor_scan(o[0], x[0], y[0], first, op0, op1), reg(x, y), o[1], span_of(o, x, None, y))
 
     def act(o, i, f=Fn.Identity, bias=0.0, scale=1.0):
+        if f == Fn.Identity:
+            return lin("a", o, i, scale, bias)
         add("a", lambda q: q.activation(o[0], i[0], f, bias=val(bias), scale=val(scale)), reg(i, bias, scale), o[1], span_of(o, i, 1.0))
 
-    def mm(o, l, r, start, stop, more=()):
-        add("p", lambda q: q.matmul(o[0], l[0], r[0], start, stop), reg(l, r, *more), o[1], max(64, r[2]) * PE * (4 if l[3] == 4 else 1))
+    def lin(e, o, i, scale=1.0, bias=0.0):
+        both = {"a": (lambda q: q.activation(o[0], i[0], Fn.Identity, bias=val(bias), scale=val(scale)), span_of(o, i, 1.0)),
+                "v": (lambda q: q.tensor_scalar(o[0], i[0], val(scale), val(bias), Op.mult, Op.add), span_of(o, i))}
+        add(e, both[e][0], reg(i, bias, scale), o[1], both[e][1], both=both)
+
+    def mms(some):
+        add("p", lambda q: [q.matmul(o[0], l[0], r[0], a, b) for o, l, r, a, b in some][-1], reg(*[x for m in some for x in m[1:3]]),
+            reg(*[m[0] for m in some]), ("plain", sum(max(64, r[2]) * (2.0 if l[3] == 4 else 0.5) for o, l, r, a, b in some)))
+
+    def mm(*one):
+        mms([one])
 
     def iota(o, pat, base=0, cm=0):
         if SB[o[1][0][0]][1] == I32:
-            add("q", lambda q: q.iota(o[0], pat, base, cm), [], o[1], 130 + 2 * o[2] * CYCLE)
+            add("q", lambda q: q.iota(o[0], pat, base, cm), [], o[1], ("plain", 150 + 2 * o[2]))
         else:
-            add("q", lambda q: q.iota(o[0], pat, base, cm, allow_small_or_imprecise_dtypes=True), [], o[1], 130 + 2 * o[2] * CYCLE)
+            add("q", lambda q: q.iota(o[0], pat, base, cm, allow_small_or_imprecise_dtypes=True), [], o[1], ("plain", 150 + 2 * o[2]))
+
+    def pick(o, i, pat, base, cm):
+        add("q", lambda q: q.affine_select(o[0], i[0], pat, Op.is_equal, 0.0, base, cm), i[1], o[1], ("plain", 200 + 2 * o[2]))
 
     def dma(o, i, nbytes, e="s"):
-        add(e, lambda q: q.dma_start(o[0], i[0]), i[1], o[1], 60.0, free_sems.pop(0), 16, 1800 + nbytes / 200)
+        add(e, lambda q: q.dma_start(o[0], i[0]), i[1], o[1], ("ns", 60.0), free_sems.pop(0), 16, 1800 + nbytes / 200)
+
+    def behind():
+        ops[-1]["after"].add(len(ops) - 2)
 
     def send(rnd, kind, src, w, after=()):
         off = w if kind == "f" else 0
@@ -204,7 +358,7 @@ def rank_program(g, core, T, topo):
                 n += len(e); rd += piece[1]
             sem = free_sems.pop(0)
             add("q", lambda q, trs=trs, sem=sem: q.remote_dma_fused(trs, local_sem=T.sem[sem]), rd + reg(*after) + [("sent", 0, 1, None)],
-                [("sent", 0, 1, None)], 300.0, sem, n, 2500.0)
+                [("sent", 0, 1, None)], ("ns", 300.0), sem, n, 2500.0)
             ops[-1]["remote"] = True; calls.append(len(ops) - 1)
             turn = [o for o in ops[-1]["deps"] if "remote" in ops[o]]
             ops[-1]["deps"].difference_update(turn); ops[-1]["after"].update(turn)
@@ -213,7 +367,7 @@ def rank_program(g, core, T, topo):
         for s in T.cores:
             if s != core:
                 cnt += len(topo.engines(route(T, topo, s, core) or s, core))
-        add(None, None, [], A(name, a, a + 3 * w)[1], TRIP, "in%d%s" % (rnd, kind), cnt)
+        add(None, None, [], A(name, a, a + 3 * w)[1], ("trip", 0), "in%d%s" % (rnd, kind), cnt)
         ops[-1]["after"].update(calls)
 
     def blocks(kind):
@@ -226,8 +380,7 @@ def rank_program(g, core, T, topo):
     ZA, ZB, Z4, Z0, ZL, ZK = 0, 1, 2, 3, 4, 5
 
     def wrap(out, m, name, a, b, start=True, stop=True):
-        for i in range(16):
-            mm(out, Z(m, i), A(name, a + i, b, 16), start and i == 0, stop and i == 15, [A(name, a, b)])
+        mms([(out, Z(m, i), A(name, a + i, b, 16), start and i == 0, stop and i == 15) for i in range(16)])
 
     def col(name, j):
         return A(name, j, j + 1)
@@ -240,58 +393,66 @@ def rank_program(g, core, T, topo):
 
     def idm(j):
         return A("ID", 128 * j, 128 * j + 128)
-    XW, LWW = A("X7", 0, W), A("LW", 0, W)
 
-    dma(A("SN"), hbm(T.snd[:]), 24576); dma(A("XB"), hbm(T.xv[:]), 458752, "a"); dma(A("NB"), hbm(T.nb[:]), 327680)
-    iota(A("PI", 0, 1), [[0, 1]], 0, 1); iota(A("JM"), [[0, 7], [1, 16]]); iota(A("JF"), [[1, 144]]); iota(A("J16"), [[16, 8], [0, 16]])
-    iota(A("C16", 0, 41), [[32, 41]], -1); iota(A("X7", V, W), [[0, W - V]]); iota(A("SF"), [[1, SL]])
-    iota(A("DK"), [[4, 3], [0, 16]]); iota(A("SW", 0, 40), [[16, 40]])
-    ms(A("ALL"), 1.0); ms(A("PW", 112, 120), 4096.0); ms(A("HF"), 0.5); ms(A("HW", W, W + 16), 4096.0)
-    p = A("PI", 0, 1)
+    def J(a, b):
+        return A("JF", 16 + a, 16 + b)
+    XW, LWW = A("X7", 0, W), A("LW", 0, W)
+    top, eight = slice(0, 112), slice(0, 8)
+
+    dma(A("X0", p=eight), hbm(T.xv[0:128:16, :]), 28672); dma(A("SN"), hbm(T.snd[:]), 24576)
+    dma(A("NB"), hbm(T.nb[:]), 327680, "a"); dma(A("XB", 0, V), hbm(T.xv[:]), 786432, "a"); behind()
+    dma(A("QB", 0, V), hbm(T.cq[:]), 1245184, "a"); behind()
+    iota(col("CI", 5), [[0, 1]], 0, 1); iota(A("JM"), [[0, 7], [1, 16]]); iota(A("JF"), [[1, 160]], -16); iota(A("J16"), [[16, 8], [0, 16]])
+    iota(A("C16", 0, 41), [[32, 41]], -16); iota(A("SF"), [[1, SL]], -7)
+    iota(A("DK"), [[4, 3], [0, 16]]); iota(A("SW"), [[16, 40]], W)
+    ms(A("ALL"), 1.0); ms(A("PW", 112, 120), 4096.0); ms(A("HW", W, W + 16), 4096.0); ms(A("QB", V, V + 16), 1024.0)
+    ms(A("JB", 0, 800, 5, lane=0), 0.0); ms(A("KD"), 1048576.0)
+    pick(A("ZS", p=eight), A("ALL", p=eight), [[1, 144]], -15, -16)
+    p = col("CI", 5)
     ts(col("CI", 0), p, 240, Op.bitwise_and); ts(col("CI", 1), p, 15, Op.bitwise_and); ts(col("CI", 2), p, 3, Op.bitwise_and)
-    ts(col("CI", 3), p, 2, Op.logical_shift_right); ts(col("CI", 4), p, 2, Op.logical_shift_right, 3, Op.bitwise_and)
-    ts(col("CI", 5), p, 127, Op.bitwise_and)
+    ts(col("CI", 3), p, 252, Op.bitwise_and); ts(col("CI", 4), p, 2, Op.logical_shift_right, 3, Op.bitwise_and)
     cp(A("CF", 0, 6), A("CI", 0, 6))
-    g16, row, r4, p4, kr, pp = [col("CF", j) for j in range(6)]
+    g16, row, r4, pq, kr, pp = [col("CF", j) for j in range(6)]
     l2 = col("CF", 6)
-    ts(A("DM"), A("JM"), row, Op.is_equal); ts(A("REL"), A("JF"), g16, Op.subtract); ts(A("ONB"), A("J16"), g16, Op.is_equal)
-    ts(l2, r4, 2.0, Op.is_lt); ts(A("DB"), A("DM"), 4096.0, Op.mult)
-    ts(zc(Z0), A("REL"), 15.0, Op.is_equal, col("DM", 0), Op.mult); ts(A("ZF"), A("REL"), 15.0, Op.is_equal)
-    ts(A("CA"), A("REL", 0, 128), 1.0, Op.add); ts(A("CN"), A("REL", 0, 128), -16.0, Op.add)
-    tt(A("CA"), A("CA"), A("ONB"), Op.mult); tt(A("CN"), A("CN"), A("ONB"), Op.mult)
-    ts(A("RM"), A("JF", 0, 4), kr, Op.is_equal, l2, Op.mult)
-    ts(A("UP"), A("CN"), 16.0, Op.add, row, Op.is_lt); ts(zc(ZA), A("REL"), 15.0, Op.is_equal)
-    for k in range(4):
-        ts(zc(ZK + k), A("REL"), 15.0, Op.is_equal, col("RM", k), Op.mult)
-    ts(zc(ZB), A("REL"), 15.0, Op.is_equal, 32768.0, Op.mult); ts(zc(Z4), A("REL"), 15.0, Op.is_equal, 4.0, Op.mult)
-    ts(zc(ZL), A("REL"), 15.0, Op.is_equal, l2, Op.mult)
-    ts(A("SW", 0, 40), A("SW", 0, 40), row, Op.add); ts(A("SW", 40, 80), A("SW", 0, 40), float(W), Op.add)
-    for j, s in enumerate((1.0, 0.5, -0.5, 7.0, -7.0, -1.0)):
-        ts(idm(j), A("JF", 0, 128), pp, Op.is_equal, s, Op.mult)
+    ts(A("DM"), A("JM"), row, Op.is_equal); ts(A("REL"), J(0, 144), g16, Op.subtract); ts(A("ONB"), A("J16"), g16, Op.is_equal)
+    ts(l2, r4, 2.0, Op.is_lt); act(A("DB"), A("DM"), scale=4096.0)
+    act(A("CA"), A("REL", 0, 128), bias=1.0); tt(A("CA"), A("CA"), A("ONB"), Op.mult); act(A("CA"), A("CA"), bias=-8.0)
+    ts(A("RM"), J(0, 4), kr, Op.is_equal, l2, Op.mult); act(col("CF", 12), row, bias=-7.0)
+    ts(A("UP"), A("CA"), col("CF", 12), Op.is_ge, -1.0, Op.mult); ts(zc(ZA), A("REL"), 15.0, Op.is_equal)
+    ts(idm(0), J(0, 128), pp, Op.is_equal); ts(col("CF", 11), col("DM", 0), 1.0 / 64, Op.mult)
+    act(A("ZF"), zc(ZA))
+    for m, s in [(ZK + k, col("RM", k)) for k in range(4)] + [(ZB, 32768.0), (Z4, 4.0), (ZL, l2), (Z0, col("CF", 11))]:
+        act(zc(m), zc(ZA), scale=s)
+    for j, s in enumerate((0.5, -0.5, 7.0, -7.0, -1.0, 2048.0)):
+        act(idm(j + 1), idm(0), scale=s)
+    ts(A("SW"), A("SW"), row, Op.add)
     ts(col("CF", 7), r4, 0.0, Op.is_equal, 0.0625, Op.mult); ts(col("CF", 8), r4, 1.0, Op.is_equal, -1.0, Op.mult)
     ts(col("CF", 10), r4, 640.0, Op.mult)
-    ts(A("JA"), A("JF", 0, 66), -0.5, Op.add); ts(A("YS"), A("JF", 0, 32), p4, Op.is_equal, l2, Op.mult)
+    iota(A("JA"), [[0, 4], [1, 65]]); ts(A("YS", 0, 131), J(-3, 128), pq, Op.is_equal, l2, Op.mult)
     ts(col("CF", 9), col("DM", 2), 16.0, Op.mult, col("CF", 8), Op.add)
-    ts(A("SEL", 0, 8), A("J16", 0, 128, 16), g16, Op.is_equal, col("CF", 7), Op.mult)
-    ts(A("SEL", 8, 16), A("J16", 0, 128, 16), g16, Op.is_equal, col("CF", 9), Op.mult)
-    for h in range(16):
-        act(A("UH", 128 * h, 128 * h + 128), A("ONB"), scale=col("DB", h))
-    iota(A("KC"), [[-1, 4], [0, 40]], 3); iota(A("FL"), [[0, 512]]); iota(A("HW", 0, V), [[0, V]])
-    iota(A("KX"), [[0, 320], [256, 4]]); iota(A("KN"), [[0, 320], [-256, 4]], 256)
+    ts(A("SEL"), A("J16", 0, 128, 16), g16, Op.is_equal, col("CF", 7), Op.mult)
+    iota(A("SX"), [[16, 8], [0, 65]]); ts(A("SX"), A("SX"), g16, Op.is_equal, col("CF", 9), Op.mult)
+    iota(A("C112"), [[16, 112]]); iota(A("KC"), [[0, 24], [-1, 4]], 3)
+    iota(A("K4"), [[0, 24], [1, 4]]); ts(A("K4"), A("K4"), 1.0, Op.min); iota(A("FL"), [[0, 512]])
+    for a in range(0, V, 448):
+        iota(A("HW", a, a + 448), [[0, 448]])
+    for a in range(0, 1536, 512):
+        iota(A("KX", a, a + 512), [[0, 128], [256, 4]]); iota(A("KN", a, a + 512), [[0, 128], [-256, 4]], 256)
     ts(A("SK", 0, 48), A("SN"), 1.0 / 640, Op.mult, 0.5 / 640 - 0.5, Op.add)
     cp(A("KL", 0, 48), A("SK", 0, 48)); ts(A("S1", 0, 48), A("SK", 0, 48), -640.0, Op.mult)
     tt(A("S1", 0, 48), A("S1", 0, 48), A("SN"), Op.add); cp(A("CL", 0, 48), A("S1", 0, 48))
     act(A("MK", 0, 768), IND(A("DB", 0, 16), A("KL", 0, 48)))
     tt(A("SHF"), IND(A("NB"), A("CL", 0, 48)), A("MK", 0, 768), Op.min)
-    act(A("X7", 0, V), A("XB"), bias=448.0, scale=7.0)
-    ts(A("IDF"), A("JF", 0, 128), pp, Op.is_equal)
-    wrap(PS(4, 0, 112), Z0, "XB", 0, V)
+    act(A("X7", 0, V), A("XB", 0, V), bias=448.0, scale=7.0)
+    mms([(PS(4, 0, 112), A("ZS", 15 - i, 143 - i, p=eight), A("X0", i, V, 16, p=eight), i == 0, i == 15) for i in range(16)])
     ts(A("IH"), A("NB"), -7.5, Op.add, M27, Op.add); act(A("DG", 0, 640), A("IH"), bias=-M27)
     ts(A("NT"), A("NB"), 15, Op.bitwise_and); cp(A("DG", 640, 1280), A("NT"))
-    for j in range(4):
+    ms(A("LW", 0, 768), 0.0); act(A("XB", V, W), A("LW", 0, 768), bias=-64.0)
+    for a in range(768, W, 448):
+        iota(A("LW", a, a + 448), [[0, 448]])
+    act(A("HF"), A("XB", V, V + 384), scale=0.0, bias=0.5)
+    for j in range(2):
         dma(A("LW", 0, W, p=slice(j, 128, 4), lane=j), A("DG", 640 * (j % 2), 640 * (j % 2) + 640), 163840)
-    dma(A("QB"), hbm(T.cq[:]), 458752)
-    ops[-1]["after"].add(len(ops) - 2)
     iota(A("IG", 640, 1280), [[0, 40], [1, 16]]); iota(A("IH"), [[16, 40], [0, 16]])
     act(A("IG", 0, 640), A("IH"), bias=col("CF", 10))
     for j in range(4):
@@ -309,282 +470,227 @@ def rank_program(g, core, T, topo):
         tt(A("SH"), IND(LWW, A("CL", 48, 96)), A("MK", 768, 1536), Op.min)
 
     def show(rnd):
-        for d in blocks("x"):
-            act(A("XS", G * d - G, G * d), IND(XW, A("XL", 16 * d - 16, 16 * d)), bias=BACK, scale=UN7)
+        for d, e in zip(blocks("x"), SHOW[rnd]):
+            o, l = A("XS", G * d - G, G * d), A("XL", 16 * d - 16, 16 * d)
+            if rnd:
+                lin(e, o, IND(XW, l), UN7, BACK)
+            else:
+                lin(e, o, IND(A("XB", 0, W), l))
         send(rnd, "x", "XS", G)
 
-    def unwrap(onto):
-        for b in range(4):
-            for h in range(16):
-                mm(PS(b, h, 16 * min(32, 112 - 32 * b), 16), A("UH", 128 * h, 128 * h + 128), A("FN", 32 * b, min(112, 32 * b + 32)),
-                   not onto, h == 15 or not onto)
+    def keep(out, who, scale, bias):
+        ts(A("KEEP"), PS(0, 0, 112), row, Op.add, float(V), Op.min)
+        n = V // len(who)
+        for b, e in enumerate(who):
+            lin(e, A(out, n * b, n * b + n), IND(A("XB", 0, W), A("KEEP", n // 16 * b, n // 16 * (b + 1))), scale, bias)
+            if out == "YX":
+                dma(hbm(T.yx[:, n * b:n * b + n]), A("YX", n * b, n * b + n), 256 * n)
 
-    def jl(t, k):
-        return A("JL", 160 * t + 40 * k, 160 * t + 40 * k + 40)
+    def runs(word, keep):
+        out = []
+        for k, c in enumerate(word):
+            if c in keep:
+                if out and out[-1][1] == k:
+                    out[-1][1] = k + 1
+                else:
+                    out.append([k, k + 1])
+        return out
 
-    def follow(u, both):
-        t, hf = divmod(u, 2); o = W * (t % 2) + 1280 * hf
-        if both:
-            act(A("LK", o, o + SL), IND(LWW, jl(t, 2 * hf)), scale=col("RM", 2 * hf))
+    def part(rnd, s):
+        c0, c1 = PARTS[s]; cn = c1 - c0; j0, j1, n = 16 * c0, 16 * c1, 16 * cn
+
+        def jl(t, k, k2=None):
+            return A("JL", 160 * t + 4 * c0 + cn * k, 160 * t + 4 * c0 + cn * (k2 or k + 1))
+
+        def four(name, k=0, k2=4, a=0, b=None):
+            return A(name, 4 * c0 + cn * k + a, 4 * c0 + cn * k2 if b is None else 4 * c0 + cn * k + b)
+        mm(PS(4 + s, 0, cn), idm(0), A("L16", c0, c1), True, False)
+        tt(A("GW", j0, j1), IND(A("PW"), A("LO", c0, c1)), A("SF", j0, j1), Op.is_lt)
+        wrap(PS(4 + s, 0, cn), ZA, "GW", j0, j1, start=False)
+        cp(A("VL", c0, c1), PS(4 + s, 0, cn))
+        act(A("VF", c0, c1), PS(4 + s, 0, cn))
+        h = (cn // 2 + 1) // 2 * 2
+        lin("v", A("GL", j0, j0 + 16 * h), IND(LWW, A("VL", c0, c0 + h))); act(A("GL", j0 + 16 * h, j1), IND(LWW, A("VL", c0 + h, c1)))
+        if TEST[rnd][s] == "v" * 16:
+            act(A("Q7", j0, j1), IND(A("QB"), A("VL", c0, c1)), bias=448.0 - M7, scale=7.0)
         else:
-            ts(A("LK", o, o + SL), IND(LWW, jl(t, 2 * hf)), col("RM", 2 * hf), Op.mult)
-        act(A("LK", o + SL, o + 1280), IND(LWW, jl(t, 2 * hf + 1)), scale=col("RM", 2 * hf + 1))
-        wrap(PS(hf, 0, 80), ZA, "LK", o, o + 1280)
+            act(A("QS", j0, j1), IND(A("QB"), A("VL", c0, c1)))
+            act(A("Q7", j0, j1), A("QS", j0, j1), bias=448.0 - M7, scale=7.0)
+        for k in range(4):
+            wrap(PS(s + k // 2 * 2, cn * k, cn * k + cn), ZK + k, "GL", j0, j1)
+        for t in range(4):
+            o = W * (t % 2) + 4 * j0
+            for bank, k, k2 in ((s, 0, 4),) if t else ((s, 0, 2), (s + 2, 2, 4)):
+                cp(jl(t, k, k2), PS(bank, cn * k, cn * k2))
+                act(A("JB", 20 * c0 + 5 * cn * k + 4 - t, 20 * c0 + 5 * cn * k2, 5, lane=4 - t), PS(bank, cn * k, cn * k2), bias=B18 + 4096.0 * (4 - t))
+            if rnd == t == 0:
+                mm(PS(2 + s, 0, 20 * cn, 5), A("ONB"), A("ALL", 0, 4 * cn), True, True)
+            if t < 3:
+                for k in range(4):
+                    lin(FOLLOW[rnd][s][4 * t + k], A("LK", o + n * k, o + n * k + n), IND(LWW, jl(t, k)), col("RM", k))
+                wrap(PS(s, 0, 4 * cn), ZA, "LK", o, o + 4 * n)
+        for t in range(4):
+            o = W * (t % 2) + 4 * j0; way = TEST[rnd][s][4 * t:4 * t + 4]
+            for k in range(4):
+                r = A("R", o + n * k, o + n * k + n)
+                if way[k] == "v":
+                    tt(r, IND(XW, jl(t, k)), A("Q7", j0, j1), Op.subtract)
+                    continue
+                mg = A("MG", SL * (k % 2) + j0, SL * (k % 2) + j1)
+                act(mg, IND(XW, jl(t, k)), bias=BACK, scale=UN7)
+                mms([(PS(4 + s, 0, n), idm(4), A("QS", j0, j1), True, False), (PS(4 + s, 0, n), idm(3), mg, False, True)])
+                if way[k] == "a":
+                    act(r, PS(4 + s, 0, n), bias=M7)
+                else:
+                    ts(r, PS(4 + s, 0, n), M31, Op.add, M31, Op.is_equal)
+            for k, k2 in runs(way, "va"):
+                ts(A("R", o + n * k, o + n * k2), A("R", o + n * k, o + n * k2), M7, Op.is_equal)
+            wrap(PS(2 + s, 4 - t, 20 * cn, 5), ZB, "R", o, o + 4 * n)
+        scan(A("SS", 20 * c0, 20 * c1), PS(2 + s, 0, 20 * cn), A("JB", 20 * c0, 20 * c1), Op.max, Op.min)
+        ts(four("MI"), A("SS", 20 * c0 + 4, 20 * c1, 5), 4095, Op.bitwise_and)
+        cp(four("ML"), four("MI"))
+        o = 4 * j0; x = MONU[s]
+        for k in range(4):
+            if x:
+                lin("v", A("M", o + k, o + 64 * x, 4, lane=k), IND(XW, four("ML", k, b=x)), UN7, BACK)
+            if x < cn:
+                lin("a", A("M", o + 64 * x + k, o + 4 * n, 4, lane=k), IND(XW, four("ML", k, k + 1, x)), UN7, BACK)
+        f = 3 * c0
+        tt(A("FD", f, f + 2 * cn), A("SS", 20 * c0 + 4, 20 * c0 + 10 * cn, 5), A("SS", 20 * c0 + 10 * cn + 4, 20 * c1, 5), Op.min)
+        tt(A("FD", f + 2 * cn, f + 3 * cn), A("FD", f, f + cn), A("FD", f + cn, f + 2 * cn), Op.min)
+        ts(A("NF", c0, c1), A("FD", f + 2 * cn, f + 3 * cn), B18 + 4095.0, Op.is_le, -65536.0, Op.mult)
+        for k in range(4):
+            ts(A("MF", 4 * c0 + k, 4 * c1, 4, lane=k), four("MI", k, k + 1), -float(W), Op.add)
+            act(A("LK", o + n * k, o + n * k + n), IND(A("IDW"), four("ML", k, k + 1)), scale=col("RM", k))
+        y = A("YB", j0, j1)
+        scan(A("MX", o, o + 4 * n), A("KX", 0, 4 * n), A("M", o, o + 4 * n), Op.min, Op.max)
+        scan(A("MN", o, o + 4 * n), A("KN", 0, 4 * n), A("M", o, o + 4 * n), Op.max, Op.min)
+        mm(PS(s, 0, n), idm(2), A("HF", 0, n), True, False)
+        mms([(PS(s, 0, n), idm(1), A("M", o + k, o + 4 * n, 4), False, False) for k in range(4)])
+        mm(PS(s, 0, n), idm(2), A("MX", o + 3, o + 4 * n, 4), False, False)
+        mm(PS(s, 0, n), idm(2), A("MN", o + 3, o + 4 * n, 4), False, True)
+        ts(y, PS(s, 0, n), M23, Op.add, M23, Op.subtract)
+        for c in range(c0, c1, 8):
+            bank = 2 + 2 * (c // 8 % 2) + s
+            mm(PS(bank, 0, 512), idm(0), A("M", 64 * c, 64 * c + 512), True, False)
+            mms([(PS(bank, k, 512, 4), idm(5), A("YB", 16 * c, 16 * c + 128), False, k == 3) for k in range(4)])
+            act(RD(c, c + 8, 0, 64), PS(bank, 0, 512), Fn.Abs)
+        mms([(PS(s, 0, 4 * cn), idm(0), A("KC", 0, 4 * cn), True, False)] +
+            [(PS(s, k, 4 * cn, 4), idm(0), A("NF", c0, c1), False, False) for k in range(4)])
+        mms([(PS(s, 0, 4 * cn), Z(Z4, i), RD(c0, c1, 4 * i, 4 * i + 4), False, i == 15) for i in range(16)])
+        scan(four("KS"), A("KD", 0, 4 * cn), PS(s, 0, 4 * cn), Op.min, Op.max, 1048576.0)
+        for k in range(4):
+            tt(A("EQ", 4 * c0 + k, 4 * c1, 4, lane=k), PS(s, k, 4 * cn, 4), A("KS", 4 * c0 + 3, 4 * c1, 4), Op.is_equal)
+        tt(four("EQ"), four("EQ"), four("MF"), Op.mult)
+        scan(four("E2"), A("K4", 0, 4 * cn), four("EQ"), Op.mult, Op.add)
+        ts(A("WL", c0, c1), A("E2", 4 * c0 + 3, 4 * c1, 4), float(W), Op.add)
+        x = HOME[s]
+        if x:
+            lin("v", A("GH", j0, j0 + 16 * x), IND(A("HW"), A("WL", c0, c0 + x)))
+        if x < cn:
+            act(A("GH", j0 + 16 * x, j1), IND(A("HW"), A("WL", c0 + x, c1)))
+        some = range(c0 // 8, c1 // 8)
+        mms([(PS(s, 8 * c, 8 * c + 8), A("GH", 128 * c, 128 * c + 128), A("SEL"), True, True) for c in some])
+        for hf in range(2):
+            for c in some:
+                d = PS(2 + 2 * ((c + hf * len(some)) % 2) + s, 0, 260)
+                mm(d, A("ALL", 0, 128, p=slice(0, 1)), A("JA", p=slice(0, 1)), True, False)
+                mm(d, A("GH", 128 * c, 128 * c + 128), A("SX", 260 * hf, 260 * hf + 260), False, True)
+                act(A("AA", 520 * c + 260 * hf, 520 * c + 260 * hf + 260), d, Fn.Sign, -0.5)
+        for gr in range(8):
+            u = 8 * some[0] + len(some) * gr
+            for j, c in enumerate(some, u):
+                ts(A("BB", 112 * j, 112 * j + 112), J(0, 112), PS(s, 8 * c + gr, 8 * c + gr + 1), Op.is_equal)
+            mms([(PH(gr, 0, 65, top), A("BB", 112 * j, 112 * j + 112), A("AA", 520 * c + 65 * gr, 520 * c + 65 * gr + 65),
+                  c == 0 and gr % 4 == 0, c == 4 and gr % 4 == 3) for j, c in enumerate(some, u)])
+        mms([(PS(4 + s, 0, n), idm(0), A("LK", o + n * k, o + n * k + n), k == 0, k == 3) for k in range(4)])
+        act(A("MV", j0, j1), PS(4 + s, 0, n))
 
-    def fetch(u, side):
-        t, hf = divmod(u, 2); o = SL * side
-        act(A("MG", o, o + SL), IND(XW, jl(t, 2 * hf + 1)), bias=BACK, scale=UN7)
-        for a, b in ([(128 * j, 128 * j + 128) for j in range(5)] if side else [(0, 512), (512, SL)]):
-            out = PH(a // 128, 0, 128) if side else PS(4, a, b)
-            mm(out, idm(4), A("QS", a, b), True, False); mm(out, idm(3), A("MG", o + a, o + b), False, True)
-        return PH(0, 0, 128, j2=5) if side else PS(4, 0, SL)
-
-    def score(u):
-        t, hf = divmod(u, 2); c = 80 * hf
-        if t < 3 and hf:
-            new = A("SCR", 160 * t, 160 * t + 160)
-            tt(new if t else A("BST"), PS(2 + t % 2, 0, 160), A("JB", 160 * t, 160 * t + 160), Op.min)
-            if t:
-                tt(A("BST"), A("BST"), new, Op.max)
-        if t == 3:
-            new = A("SCR", 80 * u, 80 * u + 80)
-            tt(new, PS(3 - hf, 0, 80), A("JB", 80 * u, 80 * u + 80), Op.min)
-            tt(A("BI", c, c + 80), A("BST", c, c + 80), new, Op.max)
-            ts(A("MI", c, c + 80), A("BI", c, c + 80), 4095, Op.bitwise_and)
-            cp(A("ML", c, c + 80), A("MI", c, c + 80))
-            for k in (2 * hf, 2 * hf + 1):
-                ts(A("M", k, 640, 4, lane=k), IND(XW, A("ML", 40 * k, 40 * k + 10)), UN7, Op.mult, BACK, Op.add)
-                act(A("M", 640 + k, 1280, 4, lane=k), IND(XW, A("ML", 40 * k + 10, 40 * k + 20)), bias=BACK, scale=UN7)
-            for k in (2 * hf, 2 * hf + 1):
-                act(A("M", 1280 + k, W, 4, lane=k), IND(XW, A("ML", 40 * k + 20, 40 * k + 40)), bias=BACK, scale=UN7)
-
-    top, low = slice(0, 112), slice(0, 32)
     for rnd in range(2):
-        ts(A("F"), PS(4, 0, 112), -1.0 if rnd == 0 else 0.0, Op.is_lt if rnd == 0 else Op.is_ge)
-        mm(PS(5, 0, 112), A("ONB"), A("F"), True, True); mm(PS(5, 112, 224), A("UP"), A("F"), True, True)
-        mm(PS(5, 224, 336), A("ALL"), A("F"), True, True)
+        ts(A("F"), PS(4, 0, 112), 0.0, Op.is_lt)
+        mm(PS(5, 0, 112), A("ONB"), A("F"), True, True); mm(PS(5, 112, 224), A("UP"), A("F"), True, False)
+        mm(PS(5, 112, 224), A("ONB"), A("F"), False, True); mm(PS(5, 224, 336), A("ALL", 0, 128), A("F"), True, True)
         if rnd:
-            ts(A("FN"), PS(4, 0, 112), 0.0, Op.is_ge, -1.0, Op.mult); unwrap(True)
+            keep("X7", KEEP, 7.0, 448.0)
             send(rnd, "s", "SH", G, [A("NL", 0, 384)])
-            for b in range(4):
-                n = min(512, V - 512 * b)
-                act(A("X7", 512 * b, 512 * b + n), PS(b, 0, n), Fn.Relu)
         else:
             wrap(PH(7, 0, 48), None, "SHF", 0, 768)
             cp(A("XL"), PH(7, 0, 48))
         show(rnd)
         if rnd == 0:
             shown_digits(); send(rnd, "s", "SH", G)
-        scan(A("INC"), A("ALL", 0, 112), PS(5, 0, 112), Op.mult, Op.add)
+        else:
+            act(A("XB", 0, V), A("X7", 0, V), bias=BACK, scale=UN7)
+        scan(A("INC"), A("ALL", 0, 112), PS(5, 0, 112), Op.mult, Op.add, -7.5)
         scan(A("W2"), A("DB"), A("INC"), Op.add, Op.min)
+        ts(A("TB", 0, 7), A("W2", 15, 112, 16), M27, Op.add, M27, Op.subtract)
         tt(A("PW", 0, 112), A("INC"), PS(5, 112, 224), Op.subtract)
-        cp(A("TI", 0, 7), A("W2", 15, 112, 16))
-        ts(A("TI", 8, 15), A("TI", 0, 7), 15, Op.bitwise_and)
-        add("v", lambda q: q.tensor_reduce(T.LM[:, 0:1], T.PS[:, 5 * 512 + 224:5 * 512 + 336], AxisListType.X, Op.add), PS(5, 0, 1)[1], col("LM", 0)[1], 120.0)
-        cp(A("TB", 0, 7), A("TI", 8, 15))
+        add("v", lambda q: q.tensor_reduce(T.LM[:, 0:1], T.PS[:, 5 * 512 + 224:5 * 512 + 336], AxisListType.X, Op.add), PS(5, 0, 1)[1],
+            col("LM", 0)[1], ("call", 112))
         for b in range(7):
-            act(A("BS", 48 * b, 48 * b + 41), A("C16", 0, 41), Fn.Sign, col("W2", 16 * b + 15), -0.5)
-            act(A("BS", 336 + 48 * b, 336 + 48 * b + 40), A("BS", 48 * b, 48 * b + 40), scale=-1.0)
-            ts(A("AB", 128 * b, 128 * b + 128), A("CA"), col("TB", b), Op.is_gt)
+            act(A("BS", 41 * b, 41 * b + 41), A("C16", 0, 41), Fn.Sign, col("W2", 16 * b + 15), -0.5)
+            ts(A("AB", 128 * b, 128 * b + 128), A("CA"), col("TB", b), Op.add, col("W2", 16 * b + 15), Op.is_gt)
+        for a, b in ((0, 4), (4, 7)):
+            act(A("BS", 287 + 41 * a, 287 + 41 * b), A("BS", 41 * a, 41 * b), scale=-1.0)
         for b in range(7):
-            mm(PH(0, 0, 40), A("ONB"), A("BS", 48 * b, 48 * b + 40), b == 0, False)
-            mm(PH(0, 0, 40), A("AB", 128 * b, 128 * b + 128), A("BS", 48 * b + 1, 48 * b + 41), False, False)
-            mm(PH(0, 0, 40), A("AB", 128 * b, 128 * b + 128), A("BS", 336 + 48 * b, 336 + 48 * b + 40), False, b == 6)
-        cp(col("LI", 0), col("LM", 0))
+            mms([(PH(0, 0, 40), A("ONB"), A("BS", 41 * b, 41 * b + 40), b == 0, False),
+                 (PH(0, 0, 40), A("AB", 128 * b, 128 * b + 128), A("BS", 41 * b + 1, 41 * b + 41), False, False)])
+        for a, b in ((0, 4), (4, 7)):
+            mms([(PH(0, 0, 40), A("AB", 128 * u, 128 * u + 128), A("BS", 287 + 41 * u, 287 + 41 * u + 40), False, u == 6) for u in range(a, b)])
         ts(A("LO"), PH(0, 0, 40), -0.5, Op.mult, 56.0, Op.add)
         act(A("L16"), PH(0, 0, 40), bias=896.0, scale=-8.0)
-        tt(A("GW"), IND(A("PW"), A("LO")), A("SF"), Op.is_le)
-        wrap(PH(4, 0, 40), ZA, "GW", 0, SL)
+        cp(col("LI", 0), col("LM", 0))
         ts(col("LI", 1), col("LI", 0), 7, Op.bitwise_and)
-        ts(A("TH"), A("SW", 0, 40), col("INC", 111), Op.is_lt)
-        ts(col("LM", 1), col("LI", 1), 4.0, Op.mult, 4.0 * 176 + 4, Op.add)
-        ts(col("LM", 2), col("LI", 1), 4.0, Op.mult, 4.0 * 176 + 4 + 65536, Op.add)
-        tt(A("VF"), PH(4, 0, 40), A("L16"), Op.add)
-        ts(A("VL"), A("VF"), float(V - 1), Op.min)
-        tt(A("DV"), A("VF"), A("SW", 40, 80), Op.subtract)
-        cp(A("GW", 0, 320), IND(LWW, A("VL", 0, 20))); act(A("GW", 320, SL), IND(LWW, A("VL", 20, 40)))
-        act(A("QS"), IND(A("QB"), A("VL")))
-        act(A("Q7"), A("QS"), bias=448.0 - M7, scale=7.0)
-        for k in range(4):
-            wrap(PS(k // 2, 40 * (k % 2), 40 * (k % 2) + 40), ZK + k, "GW", 0, SL)
-        act(A("X7", V, W), A("ST", 768 * rnd, 768 * rnd + 768), bias=448.0, scale=7.0)
-        for u in range(8):
-            cp(A("JL", 80 * u, 80 * u + 80), PS(u % 2, 0, 80))
-            act(A("JB", 80 * u, 80 * u + 80), PS(u % 2, 0, 80), bias=B18 + 4096.0 * (4 - u // 2))
-            if u < 6:
-                follow(u, u >= AHEAD[rnd])
-        for u in range(8):
-            o = W * (u // 2 % 2) + 1280 * (u % 2); way = WAYS[rnd][u]
-            tt(A("R", o, o + SL), IND(XW, jl(u // 2, 2 * (u % 2))), A("Q7"), Op.subtract)
-            if way == "v":
-                tt(A("R", o + SL, o + 1280), IND(XW, jl(u // 2, 2 * (u % 2) + 1)), A("Q7"), Op.subtract)
-            else:
-                out = fetch(u, sum(x != "v" for x in WAYS[rnd][:u]) % 2)
-            if way == "a":
-                act(A("R", o + SL, o + 1280), out, bias=M7)
-            if way == "b":
-                ts(A("R", o, o + SL), A("R", o, o + SL), M7, Op.is_equal)
-                ts(A("R", o + SL, o + 1280), out, M31, Op.add, M31, Op.is_equal)
-            else:
-                ts(A("R", o, o + 1280), A("R", o, o + 1280), M7, Op.is_equal)
-            wrap(PS(2 + u // 2 % 2, 80 * (u % 2), 80 * (u % 2) + 80) if u < 6 else PS(9 - u, 0, 80), ZB, "R", o, o + 1280)
-            score(u)
-        ts(A("FD", 0, 160), A("BI"), B18 + 4095.0, Op.is_gt)
-        ts(A("MF"), A("MI"), -float(W), Op.add)
-        tt(A("FD", 160, 240), A("FD", 0, 80), A("FD", 80, 160), Op.min)
-        tt(A("FD", 240, 280), A("FD", 160, 200), A("FD", 200, 240), Op.min)
-        tt(A("FT"), A("FD", 240, 280), A("TH"), Op.mult)
-        ts(A("FA", 0, 40), A("FT"), col("LM", 1), Op.mult); ts(A("FT"), A("FT"), -65536.0, Op.mult, col("LM", 2), Op.add)
-        for k in range(4):
-            act(A("LK", SL * k, SL * k + SL), IND(A("IDW"), A("ML", 40 * k, 40 * k + 40)), scale=col("RM", k))
-        for ch in range(2):
-            o = 1280 * ch; y = A("YB", 320 * ch, 320 * ch + 320)
-            scan(A("MX", o, o + 1280), A("KX"), A("M", o, o + 1280), Op.min, Op.max)
-            scan(A("MN", o, o + 1280), A("KN"), A("M", o, o + 1280), Op.max, Op.min)
-            mm(PS(ch, 0, 320), idm(2), A("HF"), True, False)
-            for k in range(4):
-                mm(PS(ch, 0, 320), idm(1), A("M", o + k, o + 1280, 4), False, False)
-            mm(PS(ch, 0, 320), idm(2), A("MX", o + 3, o + 1280, 4), False, False)
-            mm(PS(ch, 0, 320), idm(2), A("MN", o + 3, o + 1280, 4), False, True)
-            ts(y, PS(ch, 0, 320), M23, Op.add, M23, Op.subtract)
-            for k in range(4):
-                c = SL * k + 320 * ch
-                mm(PS(2 + k % 2, 0, 320), idm(0), A("M", o + k, o + 1280, 4), True, False); mm(PS(2 + k % 2, 0, 320), idm(5), y, False, True)
-                act(A("R", c, c + 320), PS(2 + k % 2, 0, 320), Fn.Abs)
-                if ch and k % 2:
-                    wrap(PS(4 + k // 2, 0, 80), Z4, "R", SL * (k - 1), SL * (k + 1))
-        act(A("Y7"), A("YB"), bias=448.0, scale=7.0)
-        tt(A("KK", 0, 80), PS(4, 0, 80), A("KC", 0, 80), Op.add)
-        tt(A("K2", 0, 40), A("KK", 0, 40), A("KK", 40, 80), Op.max)
-        tt(A("K2", 120, 160), A("K2", 0, 40), A("FT"), Op.max)
-        tt(A("KK", 80, 160), PS(5, 0, 80), A("KC", 80, 160), Op.add)
-        tt(A("K2", 40, 80), A("KK", 80, 120), A("KK", 120, 160), Op.max)
-        tt(A("K2", 80, 120), A("K2", 120, 160), A("K2", 40, 80), Op.max)
-        tt(A("K2", 160, 200), A("K2", 0, 40), A("K2", 40, 80), Op.max)
-        for k in range(4):
-            tt(A("EQ", 40 * k, 40 * k + 40), A("KK", 40 * k, 40 * k + 40), A("K2", 80, 120), Op.is_equal)
-        tt(A("EQ"), A("EQ"), A("MF"), Op.mult)
-        tt(A("E2", 0, 80), A("EQ", 0, 80), A("EQ", 80, 160), Op.add)
-        tt(A("E2", 80, 120), A("E2", 0, 40), A("E2", 40, 80), Op.add)
-        ts(A("WL"), A("E2", 80, 120), float(W), Op.add)
-        tt(A("FA", 40, 80), A("K2", 160, 200), A("FA", 0, 40), Op.is_lt)
-        tt(A("FA", 80, 120), A("FA", 40, 80), A("DV"), Op.mult)
-        tt(A("FA", 120, 160), A("FA", 80, 120), A("SW", 40, 80), Op.add)
-        cp(A("SCL"), A("FA", 120, 160))
-        cp(A("GW", 0, 384), IND(A("HW"), A("WL", 0, 24))); act(A("GW", 384, SL), IND(A("HW"), A("WL", 24, 40)))
-        for c in range(5):
-            mm(PS(4, 16 * c, 16 * c + 16), A("GW", 128 * c, 128 * c + 128), A("SEL"), True, True)
-        cp(A("SC"), PS(4, 0, 80))
-        for gr in range(8):
-            for c in range(5):
-                j = 5 * gr + c
-                ts(A("BB", 112 * j, 112 * j + 112), A("JF", 0, 112), col("SC", 16 * c + gr), Op.is_equal)
-                act(A("AA", 66 * j, 66 * j + 65), A("JA", 0, 65), Fn.Sign, col("SC", 16 * c + 8 + gr))
-            for c in range(5):
-                j = 5 * gr + c
-                mm(PH(gr, 0, 65, top), A("BB", 112 * j, 112 * j + 112), A("AA", 66 * j, 66 * j + 65), c == 0, c == 4,
-                   [A("BB", 560 * gr, 560 * gr + 560), A("AA", 330 * gr, 330 * gr + 330)])
-        cp(OS(0, 4, 0, 64), PH(0, 0, 64, top, 4)); act(OS(4, 8, 0, 64), PH(4, 0, 64, top, 8))
+        ts(col("LM", 1), col("LI", 1), 4.0, Op.mult, 4.0 * 176 + 3.5, Op.add)
+        ts(A("KD", 0, 96, 4), A("ALL", 0, 24), col("LM", 1), Op.mult)
+        for e, a, b in (("v", 0, GHOST[rnd]), ("a", GHOST[rnd], 768)):
+            if a < b:
+                lin(e, A("X7", V + a, V + b), A("ST", 768 * rnd + a, 768 * rnd + b), 7.0, 448.0)
+        part(rnd, 0); part(rnd, 1)
+        lin("v", OS(0, 4, 0, 64), PH(0, 0, 64, top, 4)); act(OS(4, 8, 0, 64), PH(4, 0, 64, top, 8))
         for d in blocks("f") + [0]:
             tt(A("FL", 128 * d, 128 * d + 128, p=top), PH(0, 16 * d + 1, 16 * d + 17, top, 8), OS(0, 8, 16 * d, 16 * d + 16), Op.not_equal)
         send(rnd, "f", "FL", 128)
-        for ch in range(2):
-            for k in range(4):
-                mm(PS(ch, 0, 320), idm(0), A("LK", SL * k + 320 * ch, SL * k + 320 * ch + 320), k == 0, k == 3)
-            act(A("MV", 320 * ch, 320 * ch + 320), PS(ch, 0, 320))
-        scatter(A("X7"), A("SCL"), A("Y7"))
-        scatter(A("LW"), A("SCL"), A("MV"))
-        ident = A("ID", 0, 112, p=top)
+        ts(A("FA", 0, 40), A("KS", 3, 160, 4), col("LM", 1), Op.not_equal, 65536.0, Op.mult)
+        tt(A("VF"), A("VF"), A("NF"), Op.subtract)
+        tt(A("FA", 40, 80), A("FA", 0, 40), A("VF"), Op.max)
+        tt(A("FA", 80, 120), A("FA", 40, 80), A("SW"), Op.min)
+        cp(A("SCL"), A("FA", 80, 120))
+        scatter(A("XB"), A("SCL"), A("YB"))
+        for c0, c1 in PARTS[::-1]:
+            scatter(A("LW"), A("SCL", c0, c1), A("MV", 16 * c0, 16 * c1))
         if rnd == 0:
-            act(A("SG"), A("X7", 0, V), Fn.Sign, 1.0, -1.0)
-            for b in range(4):
-                n = min(512, V - 512 * b)
-                mm(PS(b, 0, n), A("IDF"), A("X7", 512 * b, 512 * b + n), True, False)
-            wrap(PS(4, 0, 112), Z0, "SG", 0, V, stop=False)
+            wrap(PS(4, 0, 112), Z0, "XB", 0, V, stop=False)
             shown_digits()
             wrap(PH(7, 0, 48), ZL, "SH", 0, 768)
             cp(A("XL"), PH(7, 0, 48))
         else:
-            act(A("XB"), A("X7", 0, V), bias=BACK, scale=UN7)
-            for b in range(4):
-                n = min(512, V - 512 * b)
-                for j in range(n // 128):
-                    mm(PS(5, 128 * j, 128 * j + 128, p=low) if b % 2 else PH(j, 0, 128, low), A("YS"),
-                       A("LW", 512 * b + 128 * j, 512 * b + 128 * j + 128), True, True)
-                act(A("YN", 512 * b, 512 * b + n, p=low), PS(5, 0, n, p=low) if b % 2 else PH(0, 0, 128, low, n // 128))
-            dma(hbm(T.yn[:]), A("YN", p=low), 229376, "a")
-        mm(PS(4, 0, 112), A("FL", 0, 128, p=top), ident, rnd == 1, False)
-        for d in range(3):
-            o = 384 * rnd + 128 * d
-            mm(PS(4, 0, 112), A("NL", o, o + 128, p=top), ident, False, d == 2)
-    ts(A("FN"), PS(4, 0, 112), 1.0, Op.is_lt, 1.0 / 64, Op.subtract); unwrap(False)
-    for b in range(4):
-        n = min(512, V - 512 * b)
-        tt(A("YX", 512 * b, 512 * b + n), A("XB", 512 * b, 512 * b + n), PS(b, 0, n), Op.min)
-        dma(hbm(T.yx[:, 512 * b:512 * b + n]), A("YX", 512 * b, 512 * b + n), 256 * n)
+            mms([(PS(5, 0, 448), A("YS", 3 - q, 131 - q), A("LW", 448 * q, 448 * q + 448), q == 0, q == 3) for q in range(4)])
+            act(A("YN"), PS(5, 0, 448))
+            dma(hbm(T.yn[:]), A("YN"), 229376, "a")
+        mm(PS(0, 0, 112), idm(0), A("C112"), True, False)
+        for bank, j in ((0, 6), (4, 4))[:2 - rnd]:
+            for d in range(4):
+                o = 384 * rnd + 128 * (d - 1)
+                mm(PS(bank, 0, 112), A("NL", o, o + 128, p=top) if d else A("FL", 0, 128, p=top), A("ID", 128 * j, 128 * j + 112, p=top), False, d == 3)
+    keep("YX", LAST, 1.0, 0.0)
 
-    cost = [o["cost"] for o in ops]
-    before = [[(d, ops[d]["lag"] + WAKE) for d in o["deps"]] + [(d, 0.0) for d in o["after"] - o["deps"]] for o in ops]
-    behind = [[] for _ in ops]
-    for i, b in enumerate(before):
-        for d, gap in b:
-            behind[d].append((i, gap))
-    every = range(len(ops))
-    cases = [[o["cost"] * (trip if o["e"] is None else 1.0 if o["sem"] else ga if o["cost"] % 1 == 0.5 else co) for o in ops]
-             for co, ga, trip in CASES]
-
-    def fit(turn, first, lead):
-        end, busy = [0.0] * len(ops), {e: [] for e in queue}
-        for i in turn:
-            at = max([lead[i]] + [end[d] + gap for d, gap in first[i]])
-            if ops[i]["e"] is not None:
-                line = busy[ops[i]["e"]]; k = len(line)
-                while k and line[k - 1][1] > at:
-                    k -= 1
-                while k < len(line) and at + cost[i] > line[k][0]:
-                    at = max(at, line[k][1]); k += 1
-                line.insert(k, (at, at + cost[i]))
-            end[i] = at + cost[i]
-        return end
-
-    def place(weight):
-        ahead = [0.0] * len(ops)
-        for i in reversed(every):
-            ahead[i] = weight[i] + max([0.0] + [ahead[j] + gap for j, gap in behind[i]])
-        end = fit(sorted(every, key=lambda i: (-ahead[i], i)), before, [0.0] * len(ops))
-        for _ in range(2):
-            back = fit(sorted(every, key=lambda i: (-end[i], -i)), behind, [o["lag"] for o in ops])
-            end = fit(sorted(every, key=lambda i: (-back[i], i)), before, [0.0] * len(ops))
-        turn = sorted(every, key=lambda i: (end[i] - cost[i], i)); total = 0.0
-        for c in cases:
-            done, free = [0.0] * len(ops), {e: 0.0 for e in queue}
-            for i in turn:
-                e = ops[i]["e"]
-                done[i] = max([free.get(e, 0.0)] + [done[d] + gap for d, gap in before[i]]) + c[i]
-                if e is not None:
-                    free[e] = done[i]
-            total += max(done[i] + ops[i]["lag"] for i in every)
-        return total, end
-
+    def ns(kind, x, cycle, gather, scat, trip, call):
+        if kind == "call":
+            return call + x * cycle if call > 0 else max(-call, x * cycle)
+        return {"gather": 50 + x * gather * cycle, "scatter": 50 + x * scat * cycle, "plain": x * cycle, "ns": x, "trip": trip}[kind]
     if not ORDER:
-        seed, found = 1, []
-        for _ in range(STARTS):
-            w = cost
-            span, end = place(w)
-            for n in range(TRIES):
-                w2, wide = [], 0.5 if n % 2 else 0.25
-                for c in w:
-                    seed = (seed * 1103515245 + 12345) % 2147483648
-                    w2.append(c * (1 + (seed / 2147483648 - 0.5) * wide))
-                span2, end2 = place(w2)
-                if span2 < span:
-                    span, end, w = span2, end2, w2
-            found.append((span, end))
-        end = min(found)[1]
-        ORDER.extend(sorted(every, key=lambda i: (end[i] - cost[i], i)))
+        swap = {"v": "a", "a": "v"}
+        ORDER.extend(arrange([o["e"] for o in ops], [swap[o["e"]] if o["both"] else None for o in ops],
+                             [[(d, ops[d]["lag"] + WAKE) for d in o["deps"]] + [(d, 0.0) for d in o["after"] - o["deps"]] for o in ops],
+                             [o["lag"] for o in ops], [[ns(*o["cost"], *c) for o in ops] for c in CASES],
+                             [[ns(*(o["both"][swap[o["e"]]][1] if o["both"] else o["cost"]), *c) for o in ops] for c in CASES]))
+    for o, e in zip(ops, ORDER[1]):
+        if o["both"]:
+            o["e"], o["fn"] = e, o["both"][e][0]
 
     known = {e: {} for e in queue}
-    for n, i in enumerate(ORDER):
+    for n, i in enumerate(ORDER[0]):
         o = ops[i]; o["waits"] = []
         o["key"], o["val"] = (o["e"], n + 1) if o["sem"] is None else (o["sem"], 1)
         kn = known[o["e"]] if o["e"] is not None else {}
@@ -595,11 +701,11 @@ def rank_program(g, core, T, topo):
                     kn[k] = max(kn.get(k, 0), v)
         o["place"] = n; o["clock"] = dict(kn); o["clock"][o["key"]] = o["val"]
     count = {e: 0 for e in queue}
-    for i in ORDER:
+    for i in ORDER[0]:
         o = ops[i]
         if o["sem"] is None and o["need"]:
             count[o["e"]] += 1; o["cnt"] = count[o["e"]]
-    for i in ORDER:
+    for i in ORDER[0]:
         o = ops[i]
         if o["e"] is None:
             continue

import math
from concourse.bass import DstId, RemoteDMATransfer
from concourse.mybir import AluOpType as Op, ActivationFunctionType as Fn, AxisListType

N, V, G, W, SL = 4, 1792, 256, 2560, 640
BF, F32, I32, U16 = "bfloat16", "float32", "int32", "uint16"
SB = {
    "X7": (W + SL, F32), "LW": (W + SL, BF), "XB": (W + SL, BF), "IDW": (W, BF), "HW": (W + 16, BF), "QB": (V + 16, BF), "X0": (V, BF),
    "NB": (640, I32), "NT": (640, I32), "DG": (1280, BF), "IG": (1280, BF), "IH": (640, F32), "SHF": (768, F32),
    "SN": (48, I32), "SK": (96, I32), "S1": (96, F32), "S2": (48, F32), "CL": (96, U16), "KL": (96, U16), "XL": (48, U16),
    "MK": (1536, BF), "SH": (768, BF), "XS": (768, BF), "ST": (1536, BF), "FL": (512, BF), "NL": (768, BF), "RB": (1280, BF),
    "CI": (8, I32), "CF": (16, F32), "JF": (160, BF), "J16": (128, BF), "REL": (144, BF), "JM": (112, F32),
    "DM": (112, F32), "DB": (112, F32), "RM": (4, F32), "Z": (9 * 144, BF), "ZF": (144, F32), "ZS": (144, BF), "C112": (112, BF),
    "ONB": (128, BF), "CA": (128, BF), "UP": (128, BF), "ID": (896, BF), "KEEP": (112, U16),
    "ALL": (144, BF), "HF": (384, BF), "MW": (16, BF), "SEL": (8, BF), "YS": (132, BF), "C16": (48, F32), "SF": (SL, F32),
    "SW": (40, F32), "DK": (48, F32), "JA": (260, BF), "SX": (520, BF), "KX": (1536, BF), "KN": (1536, BF),
    "F": (112, BF), "INC": (112, F32), "PW": (120, F32), "W2": (112, F32), "TB": (8, F32),
    "BS": (14 * 41, BF), "AB": (7 * 128, BF), "LO": (40, U16), "L16": (40, BF), "VL": (40, U16),
    "VF": (40, F32), "NF": (40, BF), "KC": (96, BF), "LM": (4, F32), "LI": (4, I32), "GW": (SL, BF), "GL": (SL, BF), "GH": (SL, BF),
    "Q7": (SL, F32), "QS": (SL, BF), "MG": (2 * SL, BF), "R": (2 * W, BF), "LK": (2 * W, BF), "JL": (640, U16), "JB": (800, F32),
    "SS": (800, I32), "MI": (160, I32), "ML": (160, U16), "MF": (160, F32), "FD": (120, F32),
    "M": (W, BF), "MX": (W, BF), "MN": (W, BF), "YB": (SL, BF), "MV": (SL, BF), "KD": (96, F32),
    "KS": (160, F32), "EQ": (160, F32), "E2": (160, F32), "K4": (96, F32), "FA": (120, F32), "WL": (40, U16), "SCL": (40, U16),
    "BB": (40 * 112, BF), "AA": (40 * 65, BF), "YN": (448, F32), "YX": (V, BF),
}
SCRATCH = {n: ("sbuf", [128, c], d) for n, (c, d) in SB.items()}
SCRATCH["OS"] = ("sbuf", [128, 8, 64], F32)
SCRATCH["RD"] = ("sbuf", [128, 40, 64], BF)
SCRATCH["PS"] = ("psum", [128, 3072], F32)
SCRATCH["PH"] = ("psum", [128, 8, 128], F32)
KINDS = [(0, "x"), (0, "s"), (0, "f"), (1, "s"), (1, "x"), (1, "f")]
SEMAPHORES = ["v", "a", "p", "q", "left"] + ["in%d%s" % k for k in KINDS] + ["d%d" % i for i in range(40)]
M7, M23, M27, M31, B18 = 49152.0, 12582912.0, 201326592.0, 3221225472.0, 262144.0
UN7, BACK = 9363.0 / 65536, -448 * 9363.0 / 65536
CASES = [(0.855, 1.52, 3.7, 6000.0, 50.0), (1.1, 2.0, 5.0, 5500.0, -65.0), (0.95, 1.15, 2.5, 7500.0, 55.0)]
WAKE, ORDER, HEAT, STEPS = 130.0, [], 200.0, 120000
PARTS = ((0, 24), (24, 40))
FOLLOW = (("vava" "aaaa" "aaaa", "vava" "aaaa" "aaaa"), ("vava" "aaaa" "aaaa", "vava" "aaaa" "aaaa"))
TEST = (("vvvv" "vvvv" "vvva" "vvva", "vvaa" "vvaa" "vvaa" "vvaa"), ("vvvv" "vvvv" "vvva" "vvva", "vvaa" "vvaa" "vvaa" "vvaa"))
KEEP, LAST, SHOW, GHOST = "vava", "vava", ("ava", "ava"), (384, 384)
MONU, HOME = (0, 8), (0, 8)


def route(T, topo, src, dst):
    if topo.may_write(src, dst):
        return None
    far = [c for c in T.cores if c != src and not topo.may_write(src, c)]
    can = [c for c in topo.cores_of(src) if T.rank_of(c) is None and topo.may_write(c, dst)]
    can.sort(key=lambda c: topo.die(c) != topo.die(src))
    return can[far.index(dst) % len(can)]


def legs(kind, rank):
    return [(d, (rank - d) % N if kind == "f" else (rank + d) % N) for d in range(1, N)]


def landing(rnd, kind, d):
    if kind == "s":
        return "HW", V + (d - 1) * G, G
    if kind == "x":
        return "ST", 768 * rnd + (d - 1) * G, G
    return "NL", 384 * rnd + (d - 1) * 128, 128


def slot(rnd, kind):
    return 640 * rnd + {"s": 0, "x": 256, "f": 512}[kind]


def bits(engines):
    return sum(1 << e for e in engines)


def hops(T, topo, core, kind):
    todo = [(d, r, route(T, topo, core, T.cores[r])) for d, r in legs(kind, T.rank_of(core))]
    far = [x for x in todo if x[2] is not None]
    first = []
    for i, (d, r, via) in enumerate(far):
        e = topo.engines(core, via); n = len(e) // len(far)
        first.append((d, r, via, e[i * n:(i + 1) * n]))
    return first, [(d, r, T.cores[r], topo.engines(core, T.cores[r])) for d, r, via in todo if via is None]


def relay_program(g, core, T, topo):
    jobs = [(s, T.cores[r]) for s in T.cores for r in range(N) if T.cores[r] != s and route(T, topo, s, T.cores[r]) == core]
    total = 0
    for src, dst in jobs:
        rid, pid = topo.addr(dst, core); e = topo.engines(core, dst)
        for rnd, kind in KINDS:
            d, n = [(h[0], len(h[3])) for h in hops(T, topo, src, kind)[0] if h[2] == core][0]
            name, a, w = landing(rnd, kind, d); o = slot(rnd, kind); sem = T.sem["in%d%s" % (rnd, kind)]
            g.wait_ge(sem, n)
            g.remote_dma_fused([RemoteDMATransfer(dst_ids=[DstId(rid=rid, pnc=pid)], dma_engine_mask=bits(e), remote_sem=sem,
                                                  src=T.RB[:, o:o + w], dst=T[name][:, a:a + w])], local_sem=T.sem.left)
            total += len(e)
    if total:
        g.wait_ge(T.sem.left, total)


def arrange(eng, other, before, lag, cases, spare):
    n = len(eng); every = range(n); above = [0] * n; first = []; then = [[] for _ in every]
    for i in every:
        first.append([(d, gap) for d, gap in before[i] if not any(above[x] >> d & 1 and (y > 0 or gap == 0) for x, y in before[i])])
        for d, gap in before[i]:
            if gap > 0 or lag[d] == 0:
                above[i] |= above[d] | 1 << d
        for d, gap in first[i]:
            then[d].append((i, gap))

    def fit(turn, links, lead, cost):
        end, busy = [0.0] * n, {e: [] for e in eng}
        for i in turn:
            at = max([lead[i]] + [end[d] + gap for d, gap in links[i]])
            if eng[i]:
                line = busy[eng[i]]; k = len(line)
                while k and line[k - 1][1] > at:
                    k -= 1
                while k < len(line) and at + cost[i] > line[k][0]:
                    at = max(at, line[k][1]); k += 1
                line.insert(k, (at, at + cost[i]))
            end[i] = at + cost[i]
        return end

    def sweep(turn, cost, links, lead, out, a, b, step):
        free = {None: 0.0}
        for k in range(a, b + step, step):
            i = turn[k]; e = eng[i]; at = free.get(e)
            if at is None:
                j = a - step
                while 0 <= j < n and eng[turn[j]] != e:
                    j -= step
                at = out[turn[j]] if 0 <= j < n else 0.0
            if lead[i] > at:
                at = lead[i]
            for d, gap in links[i]:
                x = out[d] + gap
                if x > at:
                    at = x
            out[i] = at = at + cost[i]
            if e:
                free[e] = at

    def flip(i):
        eng[i], other[i] = other[i], eng[i]
        for c, c2 in zip(cases, spare):
            c[i], c2[i] = c2[i], c[i]
    none = [0.0] * n; back = [0.0] * n
    for i in reversed(every):
        back[i] = cases[0][i] + max([lag[i]] + [back[j] + gap for j, gap in then[i]])
    for _ in range(3):
        end = fit(sorted(every, key=lambda i: (-back[i], i)), first, none, cases[0])
        back = fit(sorted(every, key=lambda i: (-end[i], -i)), then, lag, cases[0])
    turn = sorted(every, key=lambda i: (end[i] - cases[0][i], i))
    done, left = [none[:] for c in cases], [none[:] for c in cases]
    best, pos, seed, lo = (1e30,), [0] * n, 1, n
    for step in range(STEPS + 1):
        if step % 400 == 0 or step == STEPS:
            for c, d, l in zip(cases, done, left):
                sweep(turn, c, first, none, d, 0, n - 1, 1); sweep(turn, c, then, lag, l, n - 1, 0, -1)
            span = [max(l) for l in left]; now = sum(span); pairs = None
            best = min(best, (now, turn[:], eng[:]))
            lo = lo + 100 if lo + 240 < n else 0; hi = min(n, lo + 240) - 1
            for k, i in enumerate(turn):
                pos[i] = k
            over = [max([0.0] + [d[i] + lag[i] for i in turn[:lo]] + [l[i] for i in turn[hi + 1:]] +
                        [d[i] + gap + l[j] for i in turn[:lo] for j, gap in then[i] if pos[j] > hi]) for d, l in zip(done, left)]
        if pairs is None:
            pairs = []
            for d, l, s in zip(done, left, span):
                last = {}
                for i in turn[lo:hi + 1]:
                    e = eng[i]
                    if e in last and d[last[e]] + l[i] > s - 1.0:
                        pairs.append((last[e], i))
                    if e:
                        last[e] = i
        if not pairs:
            continue
        seed = (seed * 1103515245 + 12345) % 2147483648; v, u = pairs[(seed >> 6) % len(pairs)]
        seed = (seed * 1103515245 + 12345) % 2147483648; far, kind = seed >> 8 & 3, (seed >> 12) % 5
        swap = -1
        if kind == 4:
            swap = u if far & 1 else v
            if not other[swap]:
                continue
            new = turn; a = b = pos[swap]; flip(swap)
        else:
            way, who, p, links = (-1, u, pos[v], first) if kind & 1 else (1, v, pos[u], then)
            k = p + way
            while far and lo <= k <= hi:
                if eng[turn[k]] == eng[u]:
                    p = k; far -= 1
                k += way
            move, todo = {who}, [who]
            while todo and len(move) < 9:
                for d, gap in links[todo.pop()]:
                    if (pos[d] - p) * way <= 0 and d not in move:
                        move.add(d); todo.append(d)
            if todo or turn[p] in move:
                continue
            a, b = min(p, pos[who]), max(p, pos[who])
            new = turn[:a] + sorted(turn[a:b + 1], key=lambda i: (i in move) * way) + turn[b + 1:]
        seed = (seed * 1103515245 + 12345) % 2147483648
        bar = now - HEAT * (1 - step / STEPS) * math.log((seed + 1) / 2147483649)
        seg = new[a:b + 1]; low = 0.0; old = []
        for c, d, l in zip(cases, done, left):
            old.append([(i, d[i], l[i]) for i in seg])
            sweep(new, c, first, none, d, a, b, 1); sweep(new, c, then, lag, l, b, a, -1)
            low += max(d[i] + l[i] - c[i] for i in seg)
        if low <= bar:
            d2, l2, seg = [d[:] for d in done], [l[:] for l in left], new[lo:hi + 1]
            for c, d, l in zip(cases, d2, l2):
                sweep(new, c, first, none, d, b + 1, hi, 1); sweep(new, c, then, lag, l, a - 1, lo, -1)
            s2 = [max(x, max(d[i] + l[i] - c[i] for i in seg)) for c, d, l, x in zip(cases, d2, l2, over)]; low = sum(s2)
        if low <= bar:
            now, done, left, span, pairs = low, d2, l2, s2, None
            turn = new[:lo] + [i for x, k, i in sorted((done[0][i] - cases[0][i], k, i) for k, i in enumerate(seg))] + new[hi + 1:]
            for k in range(lo, hi + 1):
                pos[turn[k]] = k
        else:
            for was, d, l in zip(old, done, left):
                for i, x, y in was:
                    d[i], l[i] = x, y
            if swap >= 0:
                flip(swap)
    return best[1:]


def rank_program(g, core, T, topo):
    rank = T.rank_of(core)
    if rank is None:
        relay_program(g, core, T, topo)
        return
    ops, hist, free_sems = [], {}, ["d%d" % i for i in range(40)]
    queue = {"v": g.vector, "a": g.scalar, "p": g.tensor, "q": g, "s": g.sync}

    def A(name, a=0, b=None, st=None, p=slice(0, 128), lane=None):
        b = SB[name][0] if b is None else b
        return (T[name][p, a:b] if st is None else T[name][p, a:b:st], [(name, a, b, lane)], len(range(a, b, st or 1)),
                2 if SB[name][1] in (BF, U16) else 4, "")

    def PS(bank, a, b, st=None, p=slice(0, 128)):
        o = 512 * bank
        ap = T.PS[p, o + a:o + b] if st is None else T.PS[p, o + a:o + b:st]
        return (ap, [("PS", k, k + 1, None) for k in range((o + a) // 512, (o + b - 1) // 512 + 1)], len(range(a, b, st or 1)), 4, "ps")

    def PH(j, a, b, p=slice(0, 128), j2=None):
        if j2 is None:
            return (T.PH[p, j, a:b], [("PS", 6 + j // 4, 7 + j // 4, None)], b - a, 4, "ps")
        return (T.PH[p, j:j2, a:b], [("PS", k, k + 1, None) for k in range(6 + j // 4, 7 + (j2 - 1) // 4)], (b - a) * (j2 - j), 4, "ps")

    def OS(j, j2, a, b):
        return (T.OS[0:112, j:j2, a:b], [("OS", j // 4, (j2 - 1) // 4 + 1, None)], (j2 - j) * (b - a), 4, "")

    def RD(c, c2, a, b):
        return (T.RD[:, c:c2, a:b], [("RD", c, c2, None)], (c2 - c) * (b - a), 2, "")

    def IND(win, off):
        return (win[0].indirect(off[0]), win[1] + off[1], 16 * off[2], win[3], "ind")

    def add(e, fn, rd, wr, cost, sem=None, cnt=0, lag=0.0, both=None):
        me = len(ops); deps, after = set(), set()
        for regs, w in ((rd, False), (wr, True)):
            for (n, a, b, lane) in regs:
                for (a2, b2, lane2, o, w2) in hist.get(n, []):
                    if a2 >= b or a >= b2 or (lane is not None and lane2 is not None and lane != lane2):
                        continue
                    same = ops[o]["e"] == e and ops[o]["sem"] is None
                    if same and e == "p":
                        if w or w2:
                            after.add(o)
                    elif w or w2 or (n == "PS" and (not same or both or ops[o]["both"])):
                        deps.add(o)
        ops.append({"e": e, "fn": fn, "deps": deps, "after": after, "sem": sem, "cnt": cnt, "cost": cost, "lag": lag, "both": both, "need": False})
        for (n, a, b, lane) in wr:
            if lane is None:
                hist[n] = [h for h in hist.get(n, []) if not (a <= h[0] and h[1] <= b)]
        for regs, w in ((rd, False), (wr, True)):
            for (n, a, b, lane) in regs:
                hist.setdefault(n, []).append((a, b, lane, me, w))

    def val(x):
        return x[0] if isinstance(x, tuple) else x

    def reg(*xs):
        return [r for x in xs if isinstance(x, tuple) for r in x[1]]

    def span_of(o, i, rate=None, *more):
        if i[4] == "ind":
            return ("gather", o[2])
        if rate is None:
            rate = 0.5 if all(x[3] == 2 for x in (o, i) + more) else 1.0
        return ("call", o[2] * rate)

    def ts(o, i, s1, op0, s2=None, op1=None):
        if op1 is None:
            add("v", lambda q: q.tensor_scalar(o[0], i[0], val(s1), None, op0), reg(i, s1), o[1], span_of(o, i))
        else:
            add("v", lambda q: q.tensor_scalar(o[0], i[0], val(s1), val(s2), op0, op1), reg(i, s1, s2), o[1], span_of(o, i))

    def tt(o, x, y, op):
        add("v", lambda q: q.tensor_tensor(o[0], x[0], y[0], op), reg(x, y), o[1], span_of(o, x, 1.0 if "ps" in (x[4], y[4]) else 2.0))

    def cp(o, i):
        add("v", lambda q: q.tensor_copy(o[0], i[0]), i[1], o[1], span_of(o, i))

    def scatter(win, off, i):
        add("v", lambda q: q.tensor_copy(win[0].indirect(off[0]), i[0]), reg(off, i), win[1], ("scatter", i[2]))

    def ms(o, c):
        add("v", lambda q: q.memset(o[0], c), [], o[1], span_of(o, o))

    def scan(o, x, y, op0, op1, first=0.0):
        add("v", lambda q: q.tensor_tensor_scan(o[0], x[0], y[0], first, op0, op1), reg(x, y), o[1], span_of(o, x, None, y))

    def act(o, i, f=Fn.Identity, bias=0.0, scale=1.0):
        if f == Fn.Identity:
            return lin("a", o, i, scale, bias)
        add("a", lambda q: q.activation(o[0], i[0], f, bias=val(bias), scale=val(scale)), reg(i, bias, scale), o[1], span_of(o, i, 1.0))

    def lin(e, o, i, scale=1.0, bias=0.0):
        both = {"a": (lambda q: q.activation(o[0], i[0], Fn.Identity, bias=val(bias), scale=val(scale)), span_of(o, i, 1.0)),
                "v": (lambda q: q.tensor_scalar(o[0], i[0], val(scale), val(bias), Op.mult, Op.add), span_of(o, i))}
        add(e, both[e][0], reg(i, bias, scale), o[1], both[e][1], both=both)

    def mms(some):
        add("p", lambda q: [q.matmul(o[0], l[0], r[0], a, b) for o, l, r, a, b in some][-1], reg(*[x for m in some for x in m[1:3]]),
            reg(*[m[0] for m in some]), ("plain", sum(max(64, r[2]) * (2.0 if l[3] == 4 else 0.5) for o, l, r, a, b in some)))

    def mm(*one):
        mms([one])

    def iota(o, pat, base=0, cm=0):
        if SB[o[1][0][0]][1] == I32:
            add("q", lambda q: q.iota(o[0], pat, base, cm), [], o[1], ("plain", 150 + 2 * o[2]))
        else:
            add("q", lambda q: q.iota(o[0], pat, base, cm, allow_small_or_imprecise_dtypes=True), [], o[1], ("plain", 150 + 2 * o[2]))

    def pick(o, i, pat, base, cm):
        add("q", lambda q: q.affine_select(o[0], i[0], pat, Op.is_equal, 0.0, base, cm), i[1], o[1], ("plain", 200 + 2 * o[2]))

    def dma(o, i, nbytes, e="s"):
        add(e, lambda q: q.dma_start(o[0], i[0]), i[1], o[1], ("ns", 60.0), free_sems.pop(0), 16, 1800 + nbytes / 200)

    def behind():
        ops[-1]["after"].add(len(ops) - 2)

    def send(rnd, kind, src, w, after=()):
        off = w if kind == "f" else 0
        calls = []
        for pieces in hops(T, topo, core, kind):
            trs, n, rd = [], 0, []
            for d, r, to, e in pieces:
                rid, pid = topo.addr(to, core)
                name, a = landing(rnd, kind, d)[:2] if to == T.cores[r] else ("RB", slot(rnd, kind))
                piece = A(src, off + (d - 1) * w, off + d * w)
                trs.append(RemoteDMATransfer(dst_ids=[DstId(rid=rid, pnc=pid)], dma_engine_mask=bits(e),
                                             remote_sem=T.sem["in%d%s" % (rnd, kind)], src=piece[0], dst=T[name][:, a:a + w]))
                n += len(e); rd += piece[1]
            sem = free_sems.pop(0)
            add("q", lambda q, trs=trs, sem=sem: q.remote_dma_fused(trs, local_sem=T.sem[sem]), rd + reg(*after) + [("sent", 0, 1, None)],
                [("sent", 0, 1, None)], ("ns", 300.0), sem, n, 2500.0)
            ops[-1]["remote"] = True; calls.append(len(ops) - 1)
            turn = [o for o in ops[-1]["deps"] if "remote" in ops[o]]
            ops[-1]["deps"].difference_update(turn); ops[-1]["after"].update(turn)
        name, a, _ = landing(rnd, kind, 1)
        cnt = 0
        for s in T.cores:
            if s != core:
                cnt += len(topo.engines(route(T, topo, s, core) or s, core))
        add(None, None, [], A(name, a, a + 3 * w)[1], ("trip", 0), "in%d%s" % (rnd, kind), cnt)
        ops[-1]["after"].update(calls)

    def blocks(kind):
        return [h[0] for pieces in hops(T, topo, core, kind) for h in pieces]

    def Z(m, i):
        if m is None:
            return A("ZF", 15 - i, 143 - i)
        return A("Z", 144 * m + 15 - i, 144 * m + 143 - i)
    ZA, ZB, Z4, Z0, ZL, ZK = 0, 1, 2, 3, 4, 5

    def wrap(out, m, name, a, b, start=True, stop=True):
        mms([(out, Z(m, i), A(name, a + i, b, 16), start and i == 0, stop and i == 15) for i in range(16)])

    def col(name, j):
        return A(name, j, j + 1)

    def hbm(ap):
        return (ap, [])

    def zc(m):
        return A("Z", 144 * m, 144 * m + 144)

    def idm(j):
        return A("ID", 128 * j, 128 * j + 128)

    def J(a, b):
        return A("JF", 16 + a, 16 + b)
    XW, LWW = A("X7", 0, W), A("LW", 0, W)
    top, eight = slice(0, 112), slice(0, 8)

    dma(A("X0", p=eight), hbm(T.xv[0:128:16, :]), 28672); dma(A("SN"), hbm(T.snd[:]), 24576)
    dma(A("NB"), hbm(T.nb[:]), 327680, "a"); dma(A("XB", 0, V), hbm(T.xv[:]), 786432, "a"); behind()
    dma(A("QB", 0, V), hbm(T.cq[:]), 1245184, "a"); behind()
    iota(col("CI", 5), [[0, 1]], 0, 1); iota(A("JM"), [[0, 7], [1, 16]]); iota(A("JF"), [[1, 160]], -16); iota(A("J16"), [[16, 8], [0, 16]])
    iota(A("C16", 0, 41), [[32, 41]], -16); iota(A("SF"), [[1, SL]], -7)
    iota(A("DK"), [[4, 3], [0, 16]]); iota(A("SW"), [[16, 40]], W)
    ms(A("ALL"), 1.0); ms(A("PW", 112, 120), 4096.0); ms(A("HW", W, W + 16), 4096.0); ms(A("QB", V, V + 16), 1024.0)
    ms(A("JB", 0, 800, 5, lane=0), 0.0); ms(A("KD"), 1048576.0)
    pick(A("ZS", p=eight), A("ALL", p=eight), [[1, 144]], -15, -16)
    p = col("CI", 5)
    ts(col("CI", 0), p, 240, Op.bitwise_and); ts(col("CI", 1), p, 15, Op.bitwise_and); ts(col("CI", 2), p, 3, Op.bitwise_and)
    ts(col("CI", 3), p, 252, Op.bitwise_and); ts(col("CI", 4), p, 2, Op.logical_shift_right, 3, Op.bitwise_and)
    cp(A("CF", 0, 6), A("CI", 0, 6))
    g16, row, r4, pq, kr, pp = [col("CF", j) for j in range(6)]
    l2 = col("CF", 6)
    ts(A("DM"), A("JM"), row, Op.is_equal); ts(A("REL"), J(0, 144), g16, Op.subtract); ts(A("ONB"), A("J16"), g16, Op.is_equal)
    ts(l2, r4, 2.0, Op.is_lt); act(A("DB"), A("DM"), scale=4096.0)
    act(A("CA"), A("REL", 0, 128), bias=1.0); tt(A("CA"), A("CA"), A("ONB"), Op.mult); act(A("CA"), A("CA"), bias=-8.0)
    ts(A("RM"), J(0, 4), kr, Op.is_equal, l2, Op.mult); act(col("CF", 12), row, bias=-7.0)
    ts(A("UP"), A("CA"), col("CF", 12), Op.is_ge, -1.0, Op.mult); ts(zc(ZA), A("REL"), 15.0, Op.is_equal)
    ts(idm(0), J(0, 128), pp, Op.is_equal); ts(col("CF", 11), col("DM", 0), 1.0 / 64, Op.mult)
    act(A("ZF"), zc(ZA))
    for m, s in [(ZK + k, col("RM", k)) for k in range(4)] + [(ZB, 32768.0), (Z4, 4.0), (ZL, l2), (Z0, col("CF", 11))]:
        act(zc(m), zc(ZA), scale=s)
    for j, s in enumerate((0.5, -0.5, 7.0, -7.0, -1.0, 2048.0)):
        act(idm(j + 1), idm(0), scale=s)
    ts(A("SW"), A("SW"), row, Op.add)
    ts(col("CF", 7), r4, 0.0, Op.is_equal, 0.0625, Op.mult); ts(col("CF", 8), r4, 1.0, Op.is_equal, -1.0, Op.mult)
    ts(col("CF", 10), r4, 640.0, Op.mult)
    iota(A("JA"), [[0, 4], [1, 65]]); ts(A("YS", 0, 131), J(-3, 128), pq, Op.is_equal, l2, Op.mult)
    ts(col("CF", 9), col("DM", 2), 16.0, Op.mult, col("CF", 8), Op.add)
    ts(A("SEL"), A("J16", 0, 128, 16), g16, Op.is_equal, col("CF", 7), Op.mult)
    iota(A("SX"), [[16, 8], [0, 65]]); ts(A("SX"), A("SX"), g16, Op.is_equal, col("CF", 9), Op.mult)
    iota(A("C112"), [[16, 112]]); iota(A("KC"), [[0, 24], [-1, 4]], 3)
    iota(A("K4"), [[0, 24], [1, 4]]); ts(A("K4"), A("K4"), 1.0, Op.min); iota(A("FL"), [[0, 512]])
    for a in range(0, V, 448):
        iota(A("HW", a, a + 448), [[0, 448]])
    for a in range(0, 1536, 512):
        iota(A("KX", a, a + 512), [[0, 128], [256, 4]]); iota(A("KN", a, a + 512), [[0, 128], [-256, 4]], 256)
    ts(A("SK", 0, 48), A("SN"), 1.0 / 640, Op.mult, 0.5 / 640 - 0.5, Op.add)
    cp(A("KL", 0, 48), A("SK", 0, 48)); ts(A("S1", 0, 48), A("SK", 0, 48), -640.0, Op.mult)
    tt(A("S1", 0, 48), A("S1", 0, 48), A("SN"), Op.add); cp(A("CL", 0, 48), A("S1", 0, 48))
    act(A("MK", 0, 768), IND(A("DB", 0, 16), A("KL", 0, 48)))
    tt(A("SHF"), IND(A("NB"), A("CL", 0, 48)), A("MK", 0, 768), Op.min)
    act(A("X7", 0, V), A("XB", 0, V), bias=448.0, scale=7.0)
    mms([(PS(4, 0, 112), A("ZS", 15 - i, 143 - i, p=eight), A("X0", i, V, 16, p=eight), i == 0, i == 15) for i in range(16)])
    ts(A("IH"), A("NB"), -7.5, Op.add, M27, Op.add); act(A("DG", 0, 640), A("IH"), bias=-M27)
    ts(A("NT"), A("NB"), 15, Op.bitwise_and); cp(A("DG", 640, 1280), A("NT"))
    ms(A("LW", 0, 768), 0.0); act(A("XB", V, W), A("LW", 0, 768), bias=-64.0)
    for a in range(768, W, 448):
        iota(A("LW", a, a + 448), [[0, 448]])
    act(A("HF"), A("XB", V, V + 384), scale=0.0, bias=0.5)
    for j in range(2):
        dma(A("LW", 0, W, p=slice(j, 128, 4), lane=j), A("DG", 640 * (j % 2), 640 * (j % 2) + 640), 163840)
    iota(A("IG", 640, 1280), [[0, 40], [1, 16]]); iota(A("IH"), [[16, 40], [0, 16]])
    act(A("IG", 0, 640), A("IH"), bias=col("CF", 10))
    for j in range(4):
        dma(A("IDW", 0, W, p=slice(j, 128, 4), lane=j), A("IG", 640 * (j % 2), 640 * (j % 2) + 640), 163840)
    for j in range(2):
        dma(A("HW", 0, V, p=slice(j, 128, 16), lane=j), A("IDW", 0, V, p=slice(j, 128, 16)), 28672)
    ts(A("MW", 0, 4), A("RM"), 4096.0, Op.mult, col("DM", 2), Op.subtract)
    ts(A("MW", 4, 8), A("MW", 0, 4), col("DM", 2), Op.subtract); ts(A("MW", 8, 12), A("MW", 4, 8), col("DM", 2), Op.subtract)
    ts(A("SK", 48, 96), A("SK", 0, 48), 2, Op.logical_shift_right)
    ts(A("S1", 48, 96), A("SK", 48, 96), -float(W), Op.mult); tt(A("S2"), A("SK", 48, 96), A("DK"), Op.add)
    tt(A("S1", 48, 96), A("S1", 48, 96), A("SN"), Op.add); cp(A("KL", 48, 96), A("S2")); cp(A("CL", 48, 96), A("S1", 48, 96))
    act(A("MK", 768, 1536), IND(A("MW", 0, 12), A("KL", 48, 96)))

    def shown_digits():
        tt(A("SH"), IND(LWW, A("CL", 48, 96)), A("MK", 768, 1536), Op.min)

    def show(rnd):
        for d, e in zip(blocks("x"), SHOW[rnd]):
            o, l = A("XS", G * d - G, G * d), A("XL", 16 * d - 16, 16 * d)
            if rnd:
                lin(e, o, IND(XW, l), UN7, BACK)
            else:
                lin(e, o, IND(A("XB", 0, W), l))
        send(rnd, "x", "XS", G)

    def keep(out, who, scale, bias):
        ts(A("KEEP"), PS(0, 0, 112), row, Op.add, float(V), Op.min)
        n = V // len(who)
        for b, e in enumerate(who):
            lin(e, A(out, n * b, n * b + n), IND(A("XB", 0, W), A("KEEP", n // 16 * b, n // 16 * (b + 1))), scale, bias)
            if out == "YX":
                dma(hbm(T.yx[:, n * b:n * b + n]), A("YX", n * b, n * b + n), 256 * n)

    def runs(word, keep):
        out = []
        for k, c in enumerate(word):
            if c in keep:
                if out and out[-1][1] == k:
                    out[-1][1] = k + 1
                else:
                    out.append([k, k + 1])
        return out

    def part(rnd, s):
        c0, c1 = PARTS[s]; cn = c1 - c0; j0, j1, n = 16 * c0, 16 * c1, 16 * cn

        def jl(t, k, k2=None):
            return A("JL", 160 * t + 4 * c0 + cn * k, 160 * t + 4 * c0 + cn * (k2 or k + 1))

        def four(name, k=0, k2=4, a=0, b=None):
            return A(name, 4 * c0 + cn * k + a, 4 * c0 + cn * k2 if b is None else 4 * c0 + cn * k + b)
        mm(PS(4 + s, 0, cn), idm(0), A("L16", c0, c1), True, False)
        tt(A("GW", j0, j1), IND(A("PW"), A("LO", c0, c1)), A("SF", j0, j1), Op.is_lt)
        wrap(PS(4 + s, 0, cn), ZA, "GW", j0, j1, start=False)
        cp(A("VL", c0, c1), PS(4 + s, 0, cn))
        act(A("VF", c0, c1), PS(4 + s, 0, cn))
        h = (cn // 2 + 1) // 2 * 2
        lin("v", A("GL", j0, j0 + 16 * h), IND(LWW, A("VL", c0, c0 + h))); act(A("GL", j0 + 16 * h, j1), IND(LWW, A("VL", c0 + h, c1)))
        if TEST[rnd][s] == "v" * 16:
            act(A("Q7", j0, j1), IND(A("QB"), A("VL", c0, c1)), bias=448.0 - M7, scale=7.0)
        else:
            act(A("QS", j0, j1), IND(A("QB"), A("VL", c0, c1)))
            act(A("Q7", j0, j1), A("QS", j0, j1), bias=448.0 - M7, scale=7.0)
        for k in range(4):
            wrap(PS(s + k // 2 * 2, cn * k, cn * k + cn), ZK + k, "GL", j0, j1)
        for t in range(4):
            o = W * (t % 2) + 4 * j0
            for bank, k, k2 in ((s, 0, 4),) if t else ((s, 0, 2), (s + 2, 2, 4)):
                cp(jl(t, k, k2), PS(bank, cn * k, cn * k2))
                act(A("JB", 20 * c0 + 5 * cn * k + 4 - t, 20 * c0 + 5 * cn * k2, 5, lane=4 - t), PS(bank, cn * k, cn * k2), bias=B18 + 4096.0 * (4 - t))
            if rnd == t == 0:
                mm(PS(2 + s, 0, 20 * cn, 5), A("ONB"), A("ALL", 0, 4 * cn), True, True)
            if t < 3:
                for k in range(4):
                    lin(FOLLOW[rnd][s][4 * t + k], A("LK", o + n * k, o + n * k + n), IND(LWW, jl(t, k)), col("RM", k))
                wrap(PS(s, 0, 4 * cn), ZA, "LK", o, o + 4 * n)
        for t in range(4):
            o = W * (t % 2) + 4 * j0; way = TEST[rnd][s][4 * t:4 * t + 4]
            for k in range(4):
                r = A("R", o + n * k, o + n * k + n)
                if way[k] == "v":
                    tt(r, IND(XW, jl(t, k)), A("Q7", j0, j1), Op.subtract)
                    continue
                mg = A("MG", SL * (k % 2) + j0, SL * (k % 2) + j1)
                act(mg, IND(XW, jl(t, k)), bias=BACK, scale=UN7)
                mms([(PS(4 + s, 0, n), idm(4), A("QS", j0, j1), True, False), (PS(4 + s, 0, n), idm(3), mg, False, True)])
                if way[k] == "a":
                    act(r, PS(4 + s, 0, n), bias=M7)
                else:
                    ts(r, PS(4 + s, 0, n), M31, Op.add, M31, Op.is_equal)
            for k, k2 in runs(way, "va"):
                ts(A("R", o + n * k, o + n * k2), A("R", o + n * k, o + n * k2), M7, Op.is_equal)
            wrap(PS(2 + s, 4 - t, 20 * cn, 5), ZB, "R", o, o + 4 * n)
        scan(A("SS", 20 * c0, 20 * c1), PS(2 + s, 0, 20 * cn), A("JB", 20 * c0, 20 * c1), Op.max, Op.min)
        ts(four("MI"), A("SS", 20 * c0 + 4, 20 * c1, 5), 4095, Op.bitwise_and)
        cp(four("ML"), four("MI"))
        o = 4 * j0; x = MONU[s]
        for k in range(4):
            if x:
                lin("v", A("M", o + k, o + 64 * x, 4, lane=k), IND(XW, four("ML", k, b=x)), UN7, BACK)
            if x < cn:
                lin("a", A("M", o + 64 * x + k, o + 4 * n, 4, lane=k), IND(XW, four("ML", k, k + 1, x)), UN7, BACK)
        f = 3 * c0
        tt(A("FD", f, f + 2 * cn), A("SS", 20 * c0 + 4, 20 * c0 + 10 * cn, 5), A("SS", 20 * c0 + 10 * cn + 4, 20 * c1, 5), Op.min)
        tt(A("FD", f + 2 * cn, f + 3 * cn), A("FD", f, f + cn), A("FD", f + cn, f + 2 * cn), Op.min)
        ts(A("NF", c0, c1), A("FD", f + 2 * cn, f + 3 * cn), B18 + 4095.0, Op.is_le, -65536.0, Op.mult)
        for k in range(4):
            ts(A("MF", 4 * c0 + k, 4 * c1, 4, lane=k), four("MI", k, k + 1), -float(W), Op.add)
            act(A("LK", o + n * k, o + n * k + n), IND(A("IDW"), four("ML", k, k + 1)), scale=col("RM", k))
        y = A("YB", j0, j1)
        scan(A("MX", o, o + 4 * n), A("KX", 0, 4 * n), A("M", o, o + 4 * n), Op.min, Op.max)
        scan(A("MN", o, o + 4 * n), A("KN", 0, 4 * n), A("M", o, o + 4 * n), Op.max, Op.min)
        mm(PS(s, 0, n), idm(2), A("HF", 0, n), True, False)
        mms([(PS(s, 0, n), idm(1), A("M", o + k, o + 4 * n, 4), False, False) for k in range(4)])
        mm(PS(s, 0, n), idm(2), A("MX", o + 3, o + 4 * n, 4), False, False)
        mm(PS(s, 0, n), idm(2), A("MN", o + 3, o + 4 * n, 4), False, True)
        ts(y, PS(s, 0, n), M23, Op.add, M23, Op.subtract)
        for c in range(c0, c1, 8):
            bank = 2 + 2 * (c // 8 % 2) + s
            mm(PS(bank, 0, 512), idm(0), A("M", 64 * c, 64 * c + 512), True, False)
            mms([(PS(bank, k, 512, 4), idm(5), A("YB", 16 * c, 16 * c + 128), False, k == 3) for k in range(4)])
            act(RD(c, c + 8, 0, 64), PS(bank, 0, 512), Fn.Abs)
        mms([(PS(s, 0, 4 * cn), idm(0), A("KC", 0, 4 * cn), True, False)] +
            [(PS(s, k, 4 * cn, 4), idm(0), A("NF", c0, c1), False, False) for k in range(4)])
        mms([(PS(s, 0, 4 * cn), Z(Z4, i), RD(c0, c1, 4 * i, 4 * i + 4), False, i == 15) for i in range(16)])
        scan(four("KS"), A("KD", 0, 4 * cn), PS(s, 0, 4 * cn), Op.min, Op.max, 1048576.0)
        for k in range(4):
            tt(A("EQ", 4 * c0 + k, 4 * c1, 4, lane=k), PS(s, k, 4 * cn, 4), A("KS", 4 * c0 + 3, 4 * c1, 4), Op.is_equal)
        tt(four("EQ"), four("EQ"), four("MF"), Op.mult)
        scan(four("E2"), A("K4", 0, 4 * cn), four("EQ"), Op.mult, Op.add)
        ts(A("WL", c0, c1), A("E2", 4 * c0 + 3, 4 * c1, 4), float(W), Op.add)
        x = HOME[s]
        if x:
            lin("v", A("GH", j0, j0 + 16 * x), IND(A("HW"), A("WL", c0, c0 + x)))
        if x < cn:
            act(A("GH", j0 + 16 * x, j1), IND(A("HW"), A("WL", c0 + x, c1)))
        some = range(c0 // 8, c1 // 8)
        mms([(PS(s, 8 * c, 8 * c + 8), A("GH", 128 * c, 128 * c + 128), A("SEL"), True, True) for c in some])
        for hf in range(2):
            for c in some:
                d = PS(2 + 2 * ((c + hf * len(some)) % 2) + s, 0, 260)
                mm(d, A("ALL", 0, 128, p=slice(0, 1)), A("JA", p=slice(0, 1)), True, False)
                mm(d, A("GH", 128 * c, 128 * c + 128), A("SX", 260 * hf, 260 * hf + 260), False, True)
                act(A("AA", 520 * c + 260 * hf, 520 * c + 260 * hf + 260), d, Fn.Sign, -0.5)
        for gr in range(8):
            u = 8 * some[0] + len(some) * gr
            for j, c in enumerate(some, u):
                ts(A("BB", 112 * j, 112 * j + 112), J(0, 112), PS(s, 8 * c + gr, 8 * c + gr + 1), Op.is_equal)
            mms([(PH(gr, 0, 65, top), A("BB", 112 * j, 112 * j + 112), A("AA", 520 * c + 65 * gr, 520 * c + 65 * gr + 65),
                  c == 0 and gr % 4 == 0, c == 4 and gr % 4 == 3) for j, c in enumerate(some, u)])
        mms([(PS(4 + s, 0, n), idm(0), A("LK", o + n * k, o + n * k + n), k == 0, k == 3) for k in range(4)])
        act(A("MV", j0, j1), PS(4 + s, 0, n))

    for rnd in range(2):
        ts(A("F"), PS(4, 0, 112), 0.0, Op.is_lt)
        mm(PS(5, 0, 112), A("ONB"), A("F"), True, True); mm(PS(5, 112, 224), A("UP"), A("F"), True, False)
        mm(PS(5, 112, 224), A("ONB"), A("F"), False, True); mm(PS(5, 224, 336), A("ALL", 0, 128), A("F"), True, True)
        if rnd:
            keep("X7", KEEP, 7.0, 448.0)
            send(rnd, "s", "SH", G, [A("NL", 0, 384)])
        else:
            wrap(PH(7, 0, 48), None, "SHF", 0, 768)
            cp(A("XL"), PH(7, 0, 48))
        show(rnd)
        if rnd == 0:
            shown_digits(); send(rnd, "s", "SH", G)
        else:
            act(A("XB", 0, V), A("X7", 0, V), bias=BACK, scale=UN7)
        scan(A("INC"), A("ALL", 0, 112), PS(5, 0, 112), Op.mult, Op.add, -7.5)
        scan(A("W2"), A("DB"), A("INC"), Op.add, Op.min)
        ts(A("TB", 0, 7), A("W2", 15, 112, 16), M27, Op.add, M27, Op.subtract)
        tt(A("PW", 0, 112), A("INC"), PS(5, 112, 224), Op.subtract)
        add("v", lambda q: q.tensor_reduce(T.LM[:, 0:1], T.PS[:, 5 * 512 + 224:5 * 512 + 336], AxisListType.X, Op.add), PS(5, 0, 1)[1],
            col("LM", 0)[1], ("call", 112))
        for b in range(7):
            act(A("BS", 41 * b, 41 * b + 41), A("C16", 0, 41), Fn.Sign, col("W2", 16 * b + 15), -0.5)
            ts(A("AB", 128 * b, 128 * b + 128), A("CA"), col("TB", b), Op.add, col("W2", 16 * b + 15), Op.is_gt)
        for a, b in ((0, 4), (4, 7)):
            act(A("BS", 287 + 41 * a, 287 + 41 * b), A("BS", 41 * a, 41 * b), scale=-1.0)
        for b in range(7):
            mms([(PH(0, 0, 40), A("ONB"), A("BS", 41 * b, 41 * b + 40), b == 0, False),
                 (PH(0, 0, 40), A("AB", 128 * b, 128 * b + 128), A("BS", 41 * b + 1, 41 * b + 41), False, False)])
        for a, b in ((0, 4), (4, 7)):
            mms([(PH(0, 0, 40), A("AB", 128 * u, 128 * u + 128), A("BS", 287 + 41 * u, 287 + 41 * u + 40), False, u == 6) for u in range(a, b)])
        ts(A("LO"), PH(0, 0, 40), -0.5, Op.mult, 56.0, Op.add)
        act(A("L16"), PH(0, 0, 40), bias=896.0, scale=-8.0)
        cp(col("LI", 0), col("LM", 0))
        ts(col("LI", 1), col("LI", 0), 7, Op.bitwise_and)
        ts(col("LM", 1), col("LI", 1), 4.0, Op.mult, 4.0 * 176 + 3.5, Op.add)
        ts(A("KD", 0, 96, 4), A("ALL", 0, 24), col("LM", 1), Op.mult)
        for e, a, b in (("v", 0, GHOST[rnd]), ("a", GHOST[rnd], 768)):
            if a < b:
                lin(e, A("X7", V + a, V + b), A("ST", 768 * rnd + a, 768 * rnd + b), 7.0, 448.0)
        part(rnd, 0); part(rnd, 1)
        lin("v", OS(0, 4, 0, 64), PH(0, 0, 64, top, 4)); act(OS(4, 8, 0, 64), PH(4, 0, 64, top, 8))
        for d in blocks("f") + [0]:
            tt(A("FL", 128 * d, 128 * d + 128, p=top), PH(0, 16 * d + 1, 16 * d + 17, top, 8), OS(0, 8, 16 * d, 16 * d + 16), Op.not_equal)
        send(rnd, "f", "FL", 128)
        ts(A("FA", 0, 40), A("KS", 3, 160, 4), col("LM", 1), Op.not_equal, 65536.0, Op.mult)
        tt(A("VF"), A("VF"), A("NF"), Op.subtract)
        tt(A("FA", 40, 80), A("FA", 0, 40), A("VF"), Op.max)
        tt(A("FA", 80, 120), A("FA", 40, 80), A("SW"), Op.min)
        cp(A("SCL"), A("FA", 80, 120))
        scatter(A("XB"), A("SCL"), A("YB"))
        for c0, c1 in PARTS[::-1]:
            scatter(A("LW"), A("SCL", c0, c1), A("MV", 16 * c0, 16 * c1))
        if rnd == 0:
            wrap(PS(4, 0, 112), Z0, "XB", 0, V, stop=False)
            shown_digits()
            wrap(PH(7, 0, 48), ZL, "SH", 0, 768)
            cp(A("XL"), PH(7, 0, 48))
        else:
            mms([(PS(5, 0, 448), A("YS", 3 - q, 131 - q), A("LW", 448 * q, 448 * q + 448), q == 0, q == 3) for q in range(4)])
            act(A("YN"), PS(5, 0, 448))
            dma(hbm(T.yn[:]), A("YN"), 229376, "a")
        mm(PS(0, 0, 112), idm(0), A("C112"), True, False)
        for bank, j in ((0, 6), (4, 4))[:2 - rnd]:
            for d in range(4):
                o = 384 * rnd + 128 * (d - 1)
                mm(PS(bank, 0, 112), A("NL", o, o + 128, p=top) if d else A("FL", 0, 128, p=top), A("ID", 128 * j, 128 * j + 112, p=top), False, d == 3)
    keep("YX", LAST, 1.0, 0.0)

    def ns(kind, x, cycle, gather, scat, trip, call):
        if kind == "call":
            return call + x * cycle if call > 0 else max(-call, x * cycle)
        return {"gather": 50 + x * gather * cycle, "scatter": 50 + x * scat * cycle, "plain": x * cycle, "ns": x, "trip": trip}[kind]
    if not ORDER:
        swap = {"v": "a", "a": "v"}
        ORDER.extend(arrange([o["e"] for o in ops], [swap[o["e"]] if o["both"] else None for o in ops],
                             [[(d, ops[d]["lag"] + WAKE) for d in o["deps"]] + [(d, 0.0) for d in o["after"] - o["deps"]] for o in ops],
                             [o["lag"] for o in ops], [[ns(*o["cost"], *c) for o in ops] for c in CASES],
                             [[ns(*(o["both"][swap[o["e"]]][1] if o["both"] else o["cost"]), *c) for o in ops] for c in CASES]))
    for o, e in zip(ops, ORDER[1]):
        if o["both"]:
            o["e"], o["fn"] = e, o["both"][e][0]

    known = {e: {} for e in queue}
    for n, i in enumerate(ORDER[0]):
        o = ops[i]; o["waits"] = []
        o["key"], o["val"] = (o["e"], n + 1) if o["sem"] is None else (o["sem"], 1)
        kn = known[o["e"]] if o["e"] is not None else {}
        for d in sorted((ops[d] for d in o["deps"] if o["e"] is not None), key=lambda d: -d["place"]):
            if kn.get(d["key"], 0) < d["val"]:
                d["need"] = True; o["waits"].append(d)
                for k, v in d["clock"].items():
                    kn[k] = max(kn.get(k, 0), v)
        o["place"] = n; o["clock"] = dict(kn); o["clock"][o["key"]] = o["val"]
    count = {e: 0 for e in queue}
    for i in ORDER[0]:
        o = ops[i]
        if o["sem"] is None and o["need"]:
            count[o["e"]] += 1; o["cnt"] = count[o["e"]]
    for i in ORDER[0]:
        o = ops[i]
        if o["e"] is None:
            continue
        q = queue[o["e"]]
        for d in o["waits"]:
            q.wait_ge(T.sem[d["key"]], d["cnt"])
        ins = o["fn"](q)
        if o["sem"] is None:
            if o["need"]:
                ins.then_inc(T.sem[o["e"]], 1)
        elif "remote" not in o:
            ins.then_inc(T.sem[o["sem"]], 16)
    for o in ops:
        if o["sem"] is not None and not o["need"]:
            g.wait_ge(T.sem[o["sem"]], o["cnt"])
